import numpy as np
import ml_dtypes


def mxq(x, axis, fmt="e4m3"):
    dtype, down = {"e4m3": (ml_dtypes.float8_e4m3fn, 7), "e5m2": (ml_dtypes.float8_e5m2, 14)}[fmt]
    v = np.moveaxis(np.asarray(x, np.float32).astype(ml_dtypes.bfloat16).astype(np.float64), axis, -1)
    blocks = v.reshape(v.shape[:-1] + (-1, 32))
    amax = np.abs(blocks).max(-1, keepdims=True)
    byte = np.maximum(np.where(amax > 0, np.frexp(amax)[1] - 1 + 127, 0) - down, 1)
    scale = np.exp2(byte - 127.0)
    codes = (blocks / scale).astype(np.float32).astype(dtype).astype(np.float64)
    return np.moveaxis((codes * scale).reshape(v.shape), -1, axis)


WIDE = False


def mx_kscale(k):
    if not WIDE:
        return np.ones(k)
    levels = np.array([24, -24, 12, -12, 0])
    if k % 512:
        return np.exp2(np.random.permutation(np.resize(levels, k // 32))).repeat(32)
    a = np.empty((k // 512, 16))
    for p in range(k // 512):
        a[p, :8] = np.random.permutation(np.resize(levels, 8))
        for g in range(8):
            far = levels[np.abs(levels - a[p, g]) >= 10]
            a[p, g + 8] = far[np.random.randint(len(far))]
    return np.exp2(a.ravel()).repeat(32)


def f64(x):
    return np.asarray(x).astype(np.float64)


def striped(idx):
    return np.tile(idx.reshape(-1, 16).T, (8, 1)).astype(np.uint16)


def unstriped(offs):
    return offs[:16].T.reshape(-1).astype(np.int64)


E2M1 = np.array([0.0, 0.5, 1.0, 1.5, 2.0, 3.0, 4.0, 6.0, -0.0, -0.5, -1.0, -1.5, -2.0, -3.0, -4.0, -6.0])


def pack_weight(w, fmt):
    k, n = w.shape
    w = f64(np.asarray(w, np.float32).astype(ml_dtypes.bfloat16)).reshape(k // 32, 32, n)
    amax = np.abs(w).max(1)
    if fmt == "e4m3":
        byte = np.frexp(amax)[1] - 1 + 127 - 7
    else:
        mant, ex = np.frexp(amax / 6.0)
        byte = np.where(mant > 0.5, ex, ex - 1) + 127
    byte = np.clip(np.where(amax > 0, byte, 1), 1, 254)
    scaled = (w * np.exp2(127.0 - byte)[:, None, :]).reshape(k, n).astype(np.float32)
    by_word = np.ascontiguousarray(scaled.reshape(k // 512, 128, 4, n).transpose(0, 1, 3, 2))
    if fmt == "e4m3":
        words = by_word.astype(ml_dtypes.float8_e4m3fn).view(np.uint8)
    else:
        c = by_word.astype(ml_dtypes.float4_e2m1fn).view(np.uint8) & 0xF
        words = (c[..., 0::2] | (c[..., 1::2] << 4)).reshape(k // 512, 128, 2 * n)
    return np.ascontiguousarray(words), np.ascontiguousarray(byte.astype(np.uint8).reshape(k // 512, 16, n))


def unpack_weight(words, scales, fmt):
    g, _, n = scales.shape
    words = np.ascontiguousarray(words).reshape(g, 128, n, -1)
    if fmt == "e4m3":
        vals = words.view(ml_dtypes.float8_e4m3fn).astype(np.float64)
    else:
        nib = np.empty((g, 128, n, 4), np.uint8)
        nib[..., 0::2] = words & 0xF
        nib[..., 1::2] = words >> 4
        vals = E2M1[nib]
    vals = vals * np.repeat(np.exp2(scales.astype(np.float64) - 127.0), 8, axis=1)[..., None]
    return vals.transpose(0, 1, 3, 2).reshape(g * 512, n)


def gelu(f):
    return 0.5 * f * (1.0 + np.tanh(np.sqrt(2.0 / np.pi) * (f + 0.044715 * f**3)))


K, R, T, M, J = 512, 1024, 4096, 1024, 1024


def setup_inputs():
    n = np.random.standard_normal
    s = mx_kscale(K)[:, None]
    u = mx_kscale(R)[:, None]
    p_tab = pack_weight(n((K, T)) * s, "e4m3")
    p_wa = pack_weight(n((K, R)) / np.sqrt(K) / s, "e2m1")
    return {
        "tab_words": p_tab[0],
        "tab_scales": p_tab[1],
        "wa_words": p_wa[0],
        "wa_scales": p_wa[1],
        "wb": (n((K, R)) / np.sqrt(K) / s).astype(np.float32),
        "sa": (np.random.uniform(0.5, 2.0, R) * u[:, 0]).astype(np.float32),
        "sb": (np.random.uniform(0.5, 2.0, R) / u[:, 0]).astype(np.float32),
        "offs": striped(np.random.permutation(T)[:M]),
        "offs2": striped(np.random.permutation(T)[:J]),
    }


def reference(tab_words, tab_scales, wa_words, wa_scales, wb, sa, sb, offs, offs2):
    idx = unstriped(offs)
    idx2 = unstriped(offs2)
    tab_ = unpack_weight(tab_words, tab_scales, "e4m3")[:, idx]
    tabb_ = unpack_weight(tab_words, tab_scales, "e4m3")[:, idx2]
    wa_ = unpack_weight(wa_words, wa_scales, "e2m1")
    wb_ = mxq(f64(wb), 0, "e4m3")
    za = wa_.T @ tab_
    zb = wb_.T @ tabb_
    ha = f64(sa)[:, None] * gelu(za)
    hb = f64(sb)[:, None] * gelu(zb)
    ha_ = mxq(ha, 0, "e4m3")
    hb_ = mxq(hb, 0, "e4m3")
    y = ha_.T @ hb_
    return 8.0 * np.tanh(y * 0.00390625)

@@ -1,0 +1,234 @@
+from contextlib import ExitStack
+
+import concourse.mybir as mybir
+from concourse.masks import make_identity
+
+K, R, T, M, J = 512, 1024, 4096, 1024, 1024
+FLOPS = 2 * K * R * M + 2 * K * R * J + 2 * R * M * J
+
+F32 = mybir.dt.float32
+BF16 = mybir.dt.bfloat16
+I32 = mybir.dt.int32
+U32 = mybir.dt.uint32
+U16 = mybir.dt.uint16
+U8 = mybir.dt.uint8
+FP8X4 = mybir.dt.float8_e4m3fn_x4
+FP4X4 = mybir.dt.float4_e2m1fn_x4
+ACT = mybir.ActivationFunctionType
+ALU = mybir.AluOpType
+
+P = 128
+PASSES = 2
+HALF = 512
+X8_ON_VECTOR_FROM = 12
+
+
+def tile_list_biaff_gelu_cap_kernel(
+    tc, tab_words, tab_scales, wa_words, wa_scales, wb, sa, sb, offs, offs2, out
+):
+    nc = tc.nc
+    with ExitStack() as ctx:
+        keep = ctx.enter_context(tc.tile_pool(name="keep", bufs=1))
+        ring = ctx.enter_context(tc.tile_pool(name="ring", bufs=1))
+        psum = ctx.enter_context(tc.psum_pool(name="psum", bufs=1))
+
+        list_a = keep.tile([P, M // 16], U16, name="list_a")
+        list_b = keep.tile([P, J // 16], U16, name="list_b")
+        table = keep.tile([P, T], I32, name="table", align_bytes=64)
+        table_sc = keep.tile([P, T // 4], I32, name="table_sc", align_bytes=64)
+        wa_raw = keep.tile([P, R // 2], I32, name="wa_raw", align_bytes=64)
+        wa_sc_raw = keep.tile([P, R // 4], I32, name="wa_sc_raw", align_bytes=64)
+        wa_p = keep.tile([P, R // 2], I32, name="wa_p", align_bytes=64)
+        wa_sc = keep.tile([P, R // 4], I32, name="wa_sc", align_bytes=64)
+        wb_raw = [keep.tile([P, 4, HALF], F32, name=f"wb_raw{b}") for b in range(PASSES)]
+        wb_h = [keep.tile([P, 4 * HALF], BF16, name=f"wb_h{b}", align_bytes=64) for b in range(PASSES)]
+        wb_q = [keep.tile([P, HALF], U32, name=f"wb_q{b}", align_bytes=64) for b in range(PASSES)]
+        wb_sc = [keep.tile([P, HALF], U8, name=f"wb_sc{b}", align_bytes=64) for b in range(PASSES)]
+        rows = keep.tile([P, 2 * P], F32, name="rows")
+        ident = keep.tile([P, P], F32, name="ident")
+        warm_in = keep.tile([P, 1], F32, name="warm_in")
+        warm_out = keep.tile([P, 1], F32, name="warm_out")
+
+        nc.gpsimd.memset(table_sc[:, :512], 0)
+        nc.vector.memset(table_sc[:, 512:], 0)
+        nc.sync.dma_start(list_a[:], offs)
+        nc.sync.dma_start(list_b[:], offs2)
+        nc.scalar.dma_start(wa_raw[:], wa_words[0].bitcast(I32))
+        for q in range(4):
+            nc.scalar.dma_start(table_sc[32 * q : 32 * q + 4, :], tab_scales[0, 4 * q : 4 * q + 4, :].bitcast(I32))
+        for b in range(PASSES):
+            nc.sync.dma_start(wb_raw[b][:], wb[:, b * HALF : (b + 1) * HALF].rearrange("(p j) c -> p j c", j=4))
+        nc.sync.dma_start(table[:], tab_words[0].rearrange("p t i -> p (t i)").bitcast(I32))
+        nc.gpsimd.memset(wa_sc_raw[:], 0)
+        nc.gpsimd.memset(rows[:], 0.0)
+        for q in range(4):
+            nc.gpsimd.dma_start(wa_sc_raw[32 * q : 32 * q + 4, :], wa_scales[0, 4 * q : 4 * q + 4, :].bitcast(I32))
+        for side, s in enumerate((sa, sb)):
+            nc.gpsimd.dma_start(
+                rows[4 * side : 4 * side + 4, :].rearrange("t (c i) -> t c i", i=8),
+                s.rearrange("(c t i) -> t c i", t=4, i=8),
+            )
+        make_identity(nc, ident[:])
+        nc.vector.memset(warm_in[:], 0.0)
+        nc.scalar.activation(warm_out[:], warm_in[:], ACT.Gelu_apprx_tanh)
+
+        factors = psum.tile([P, PASSES, P], F32, name="factors", tag="factors", bufs=1)
+        for b in range(PASSES):
+            nc.tensor.transpose(factors[:, b, :], rows[:, b * P : (b + 1) * P], ident[:])
+
+        lists = (list_a, list_b)
+        v_words = {}
+        v_sc = {}
+
+        def gather_scales(side, h):
+            v_sc[side, h] = keep.tile([P, HALF], U8, name=f"v_sc{side}{h}", align_bytes=64)
+            nc.vector.tensor_copy(v_sc[side, h][:], table_sc[:].bitcast(U8).indirect(lists[side][:, 32 * h : 32 * h + 32]))
+
+        def gather_words(side, h):
+            v_words[side, h] = keep.tile([P, HALF], U32, name=f"v_words{side}{h}", align_bytes=64)
+            nc.vector.tensor_copy(v_words[side, h][:], table[:].bitcast(U32).indirect(lists[side][:, 32 * h : 32 * h + 32]))
+
+        def permute_wa():
+            for b in range(PASSES):
+                nc.vector.tensor_copy(
+                    wa_p[:, 256 * b : 256 * (b + 1)].rearrange("p (t q i) -> p t q i", t=4, i=4),
+                    wa_raw[:, 256 * b : 256 * (b + 1)].rearrange("p (q t i) -> p t q i", t=4, i=4),
+                )
+                nc.vector.tensor_copy(
+                    wa_sc[:, 128 * b : 128 * (b + 1)].rearrange("p (t q i) -> p t q i", t=4, i=2),
+                    wa_sc_raw[:, 128 * b : 128 * (b + 1)].rearrange("p (q t i) -> p t q i", t=4, i=2),
+                )
+
+        def round_wb(b):
+            src = wb_raw[b][:].rearrange("p j (q t i) -> p t q i j", t=4, i=8)
+            for t in range(4):
+                nc.scalar.activation(
+                    wb_h[b][:, HALF * t : HALF * (t + 1)].rearrange("p (q i j) -> p q i j", i=8, j=4),
+                    src[:, t],
+                    ACT.Copy,
+                )
+
+        def quantize_wb(b):
+            nc.vector.quantize_mx(wb_q[b][:].bitcast(FP8X4), wb_sc[b][:], wb_h[b][:])
+
+        def weights(side, b, t):
+            if side == 0:
+                c = 4 * b + t
+                return (
+                    wa_p[:].bitcast(U8)[:, 256 * c : 256 * (c + 1)].bitcast(FP4X4),
+                    wa_sc[:].bitcast(U8)[:, P * c : P * (c + 1)],
+                )
+            return wb_q[b][:, P * t : P * (t + 1)].bitcast(FP8X4), wb_sc[b][:, P * t : P * (t + 1)]
+
+        def hidden_bank(side, tile, b, dst):
+            h, c0 = divmod(tile * P, HALF)
+            bank = psum.tile([P, 4, P], F32, name="bank", tag="bank", bufs=7)
+            for t in range(4):
+                w, w_sc = weights(side, b, t)
+                nc.tensor.matmul_mx(
+                    bank[:, t, :],
+                    lhsT=w,
+                    lhsT_scale=w_sc,
+                    rhs=v_words[side, h][:, c0 : c0 + P].bitcast(FP8X4),
+                    rhs_scale=v_sc[side, h][:, c0 : c0 + P],
+                    start=True,
+                    stop=True,
+                )
+            nc.scalar.activation(dst, bank[:].rearrange("p t n -> p n t"), ACT.Gelu_apprx_tanh)
+
+        ha_q = [keep.tile([P, 2 * P], U32, name=f"ha_q{i}", align_bytes=64) for i in range(8)]
+        ha_sc = [keep.tile([P, 2 * P], U8, name=f"ha_sc{i}", align_bytes=64) for i in range(8)]
+        hb_q = [[keep.tile([P, HALF], U32, name=f"hb_q{h}{b}", align_bytes=64) for b in range(2)] for h in range(2)]
+        hb_sc = [[keep.tile([P, HALF], U8, name=f"hb_sc{h}{b}", align_bytes=64) for b in range(2)] for h in range(2)]
+
+        pending = []
+
+        def flush():
+            for codes, sc, src in pending:
+                nc.vector.quantize_mx(codes.bitcast(FP8X4), sc, src)
+            pending.clear()
+
+        def a_tile(i):
+            g = ring.tile([P, 2, P, 4], F32, name="g", tag="g", bufs=10)
+            for b in range(PASSES):
+                hidden_bank(0, i, b, g[:, b])
+            hh = ring.tile([P, 2 * P * 4], BF16, name="ha_h", tag="ha_h", bufs=3, align_bytes=64)
+            nc.vector.tensor_tensor(
+                hh[:].rearrange("p (b n t) -> p b n t", b=2, t=4),
+                g[:],
+                factors[:, :, 0:4].unsqueeze(2).to_broadcast([P, 2, P, 4]),
+                ALU.mult,
+            )
+            flush()
+            pending.append((ha_q[i][:], ha_sc[i][:], hh[:]))
+
+        def b_unit(h, b):
+            hh = ring.tile([P, HALF * 4], BF16, name="hb_h", tag="hb_h", bufs=2, align_bytes=64)
+            for u in range(2):
+                g = ring.tile([P, 2, P, 4], F32, name="g", tag="g", bufs=10)
+                for s in range(2):
+                    hidden_bank(1, 4 * h + 2 * u + s, b, g[:, s])
+                nc.vector.tensor_tensor(
+                    hh[:, 1024 * u : 1024 * (u + 1)].rearrange("p (n t) -> p n t", t=4),
+                    g[:].rearrange("p s n t -> p (s n) t"),
+                    factors[:, b, 4:8].unsqueeze(1).to_broadcast([P, 2 * P, 4]),
+                    ALU.mult,
+                )
+                if u == 0:
+                    flush()
+            pending.append((hb_q[h][b][:], hb_sc[h][b][:], hh[:]))
+
+        count = []
+
+        def scores(i, h):
+            bank = psum.tile([P, 4, P], F32, name="bank", tag="bank", bufs=7)
+            acc = bank[:].rearrange("p t n -> p (t n)")
+            for b in range(PASSES):
+                nc.tensor.matmul_mx(
+                    acc,
+                    lhsT=ha_q[i][:, P * b : P * (b + 1)].bitcast(FP8X4),
+                    lhsT_scale=ha_sc[i][:, P * b : P * (b + 1)],
+                    rhs=hb_q[h][b][:].bitcast(FP8X4),
+                    rhs_scale=hb_sc[h][b][:],
+                    start=(b == 0),
+                    stop=(b == PASSES - 1),
+                )
+            o = ring.tile([P, HALF], F32, name="o", tag="o", bufs=8)
+            nc.scalar.activation(o[:], acc, ACT.Tanh, scale=0.00390625)
+            if len(count) < X8_ON_VECTOR_FROM:
+                nc.gpsimd.tensor_scalar(o[:], o[:], 8.0, 0.0, ALU.mult, ALU.add)
+            else:
+                nc.vector.tensor_scalar_mul(o[:], o[:], 8.0)
+            count.append(0)
+            nc.sync.dma_start(out[P * i : P * (i + 1), HALF * h : HALF * (h + 1)], o[:])
+
+        round_wb(0)
+        round_wb(1)
+        gather_scales(0, 0)
+        gather_scales(1, 0)
+        gather_scales(1, 1)
+        gather_scales(0, 1)
+        quantize_wb(0)
+        permute_wa()
+        quantize_wb(1)
+        gather_words(0, 0)
+        gather_words(1, 0)
+        gather_words(1, 1)
+        gather_words(0, 1)
+        for i in range(4):
+            a_tile(i)
+        for h in range(2):
+            for b in range(PASSES):
+                b_unit(h, b)
+        a_tile(4)
+        for i in range(4):
+            scores(i, 0)
+        a_tile(5)
+        for i in range(4):
+            scores(i, 1)
+        a_tile(6)
+        a_tile(7)
+        flush()
+        for i in range(4, 8):
+            for h in range(2):
+                scores(i, h)

@@ -20,7 +20,6 @@ ALU = mybir.AluOpType
 P = 128
 PASSES = 2
 HALF = 512
-X8_ON_VECTOR_FROM = 12
 
 
 def tile_list_biaff_gelu_cap_kernel(
@@ -49,28 +48,36 @@ def tile_list_biaff_gelu_cap_kernel(
         warm_in = keep.tile([P, 1], F32, name="warm_in")
         warm_out = keep.tile([P, 1], F32, name="warm_out")
 
-        nc.gpsimd.memset(table_sc[:, :512], 0)
-        nc.vector.memset(table_sc[:, 512:], 0)
-        nc.sync.dma_start(list_a[:], offs)
-        nc.sync.dma_start(list_b[:], offs2)
-        nc.scalar.dma_start(wa_raw[:], wa_words[0].bitcast(I32))
-        for q in range(4):
-            nc.scalar.dma_start(table_sc[32 * q : 32 * q + 4, :], tab_scales[0, 4 * q : 4 * q + 4, :].bitcast(I32))
-        for b in range(PASSES):
+        def load_wb(b):
             nc.sync.dma_start(wb_raw[b][:], wb[:, b * HALF : (b + 1) * HALF].rearrange("(p j) c -> p j c", j=4))
-        nc.sync.dma_start(table[:], tab_words[0].rearrange("p t i -> p (t i)").bitcast(I32))
-        nc.gpsimd.memset(wa_sc_raw[:], 0)
+
+        def load_wa_scales(queue, q):
+            queue.dma_start(wa_sc_raw[32 * q : 32 * q + 4, :], wa_scales[0, 4 * q : 4 * q + 4, :].bitcast(I32))
+
+        nc.vector.memset(table_sc[:], 0)
         nc.gpsimd.memset(rows[:], 0.0)
+        nc.sync.dma_start(list_a[:], offs)
+        load_wa_scales(nc.scalar, 1)
+        nc.sync.dma_start(wa_raw[:], wa_words[0].bitcast(I32))
+        load_wa_scales(nc.sync, 0)
         for q in range(4):
-            nc.gpsimd.dma_start(wa_sc_raw[32 * q : 32 * q + 4, :], wa_scales[0, 4 * q : 4 * q + 4, :].bitcast(I32))
-        for side, s in enumerate((sa, sb)):
-            nc.gpsimd.dma_start(
+            queue = nc.sync if q < 2 else nc.scalar
+            queue.dma_start(table_sc[32 * q : 32 * q + 4, :], tab_scales[0, 4 * q : 4 * q + 4, :].bitcast(I32))
+        load_wa_scales(nc.sync, 2)
+        load_wa_scales(nc.sync, 3)
+        nc.sync.dma_start(list_b[:], offs2)
+        nc.sync.dma_start(table[:], tab_words[0].rearrange("p t i -> p (t i)").bitcast(I32))
+        for side, (s, queue) in enumerate(((sa, nc.sync), (sb, nc.gpsimd))):
+            queue.dma_start(
                 rows[4 * side : 4 * side + 4, :].rearrange("t (c i) -> t c i", i=8),
                 s.rearrange("(c t i) -> t c i", t=4, i=8),
             )
-        make_identity(nc, ident[:])
+        load_wb(0)
+        load_wb(1)
         nc.vector.memset(warm_in[:], 0.0)
         nc.scalar.activation(warm_out[:], warm_in[:], ACT.Gelu_apprx_tanh)
+        nc.vector.memset(wa_sc[:], 0)
+        make_identity(nc, ident[:])
 
         factors = psum.tile([P, PASSES, P], F32, name="factors", tag="factors", bufs=1)
         for b in range(PASSES):
@@ -94,19 +101,24 @@ def tile_list_biaff_gelu_cap_kernel(
                     wa_p[:, 256 * b : 256 * (b + 1)].rearrange("p (t q i) -> p t q i", t=4, i=4),
                     wa_raw[:, 256 * b : 256 * (b + 1)].rearrange("p (q t i) -> p t q i", t=4, i=4),
                 )
-                nc.vector.tensor_copy(
-                    wa_sc[:, 128 * b : 128 * (b + 1)].rearrange("p (t q i) -> p t q i", t=4, i=2),
-                    wa_sc_raw[:, 128 * b : 128 * (b + 1)].rearrange("p (q t i) -> p t q i", t=4, i=2),
-                )
+
+        def permute_wa_scales():
+            for q in range(4):
+                live = slice(32 * q, 32 * q + 4)
+                for b in range(PASSES):
+                    nc.vector.tensor_copy(
+                        wa_sc[live, 128 * b : 128 * (b + 1)].rearrange("p (t q i) -> p t q i", t=4, i=2),
+                        wa_sc_raw[live, 128 * b : 128 * (b + 1)].rearrange("p (q t i) -> p t q i", t=4, i=2),
+                    )
 
         def round_wb(b):
             src = wb_raw[b][:].rearrange("p j (q t i) -> p t q i j", t=4, i=8)
             for t in range(4):
-                nc.scalar.activation(
-                    wb_h[b][:, HALF * t : HALF * (t + 1)].rearrange("p (q i j) -> p q i j", i=8, j=4),
-                    src[:, t],
-                    ACT.Copy,
-                )
+                dst = wb_h[b][:, HALF * t : HALF * (t + 1)].rearrange("p (q i j) -> p q i j", i=8, j=4)
+                if b == 0:
+                    nc.vector.tensor_copy(dst, src[:, t])
+                else:
+                    nc.scalar.activation(dst, src[:, t], ACT.Copy)
 
         def quantize_wb(b):
             nc.vector.quantize_mx(wb_q[b][:].bitcast(FP8X4), wb_sc[b][:], wb_h[b][:])
@@ -136,12 +148,17 @@ def tile_list_biaff_gelu_cap_kernel(
                 )
             nc.scalar.activation(dst, bank[:].rearrange("p t n -> p n t"), ACT.Gelu_apprx_tanh)
 
-        ha_q = [keep.tile([P, 2 * P], U32, name=f"ha_q{i}", align_bytes=64) for i in range(8)]
-        ha_sc = [keep.tile([P, 2 * P], U8, name=f"ha_sc{i}", align_bytes=64) for i in range(8)]
-        hb_q = [[keep.tile([P, HALF], U32, name=f"hb_q{h}{b}", align_bytes=64) for b in range(2)] for h in range(2)]
-        hb_sc = [[keep.tile([P, HALF], U8, name=f"hb_sc{h}{b}", align_bytes=64) for b in range(2)] for h in range(2)]
+        ha_q = keep.tile([P, 8 * 2 * P], U32, name="ha_q", align_bytes=64)
+        ha_sc = keep.tile([P, 8 * 2 * P], U8, name="ha_sc", align_bytes=64)
+        ha_h = keep.tile([P, 8 * 1024], BF16, name="ha_h", align_bytes=64)
+        hb_q = keep.tile([P, 4 * HALF], U32, name="hb_q", align_bytes=64)
+        hb_sc = keep.tile([P, 4 * HALF], U8, name="hb_sc", align_bytes=64)
+        hb_h = keep.tile([P, 8 * 1024], BF16, name="hb_h", align_bytes=64)
 
         pending = []
+
+        def quantize_later(codes, sc, src, c0, c1):
+            pending.append((codes[:, c0:c1], sc[:, c0:c1], src[:, 4 * c0 : 4 * c1]))
 
         def flush():
             for codes, sc, src in pending:
@@ -149,86 +166,90 @@ def tile_list_biaff_gelu_cap_kernel(
             pending.clear()
 
         def a_tile(i):
-            g = ring.tile([P, 2, P, 4], F32, name="g", tag="g", bufs=10)
+            g = ring.tile([P, 2, P, 4], F32, name="g", tag="g", bufs=12)
             for b in range(PASSES):
                 hidden_bank(0, i, b, g[:, b])
-            hh = ring.tile([P, 2 * P * 4], BF16, name="ha_h", tag="ha_h", bufs=3, align_bytes=64)
             nc.vector.tensor_tensor(
-                hh[:].rearrange("p (b n t) -> p b n t", b=2, t=4),
+                ha_h[:, 1024 * i : 1024 * (i + 1)].rearrange("p (b n t) -> p b n t", b=2, t=4),
                 g[:],
                 factors[:, :, 0:4].unsqueeze(2).to_broadcast([P, 2, P, 4]),
                 ALU.mult,
             )
             flush()
-            pending.append((ha_q[i][:], ha_sc[i][:], hh[:]))
 
-        def b_unit(h, b):
-            hh = ring.tile([P, HALF * 4], BF16, name="hb_h", tag="hb_h", bufs=2, align_bytes=64)
-            for u in range(2):
-                g = ring.tile([P, 2, P, 4], F32, name="g", tag="g", bufs=10)
-                for s in range(2):
-                    hidden_bank(1, 4 * h + 2 * u + s, b, g[:, s])
-                nc.vector.tensor_tensor(
-                    hh[:, 1024 * u : 1024 * (u + 1)].rearrange("p (n t) -> p n t", t=4),
-                    g[:].rearrange("p s n t -> p (s n) t"),
-                    factors[:, b, 4:8].unsqueeze(1).to_broadcast([P, 2 * P, 4]),
-                    ALU.mult,
-                )
-                if u == 0:
-                    flush()
-            pending.append((hb_q[h][b][:], hb_sc[h][b][:], hh[:]))
+        def b_unit(h, b, u):
+            g = ring.tile([P, 2, P, 4], F32, name="g", tag="g", bufs=12)
+            for s in range(2):
+                hidden_bank(1, 4 * h + 2 * u + s, b, g[:, s])
+            c0 = 1024 * (4 * h + 2 * b + u)
+            nc.vector.tensor_tensor(
+                hb_h[:, c0 : c0 + 1024].rearrange("p (n t) -> p n t", t=4),
+                g[:].rearrange("p s n t -> p (s n) t"),
+                factors[:, b, 4:8].unsqueeze(1).to_broadcast([P, 2 * P, 4]),
+                ALU.mult,
+            )
+            flush()
 
-        count = []
-
-        def scores(i, h):
-            bank = psum.tile([P, 4, P], F32, name="bank", tag="bank", bufs=7)
-            acc = bank[:].rearrange("p t n -> p (t n)")
-            for b in range(PASSES):
-                nc.tensor.matmul_mx(
-                    acc,
-                    lhsT=ha_q[i][:, P * b : P * (b + 1)].bitcast(FP8X4),
-                    lhsT_scale=ha_sc[i][:, P * b : P * (b + 1)],
-                    rhs=hb_q[h][b][:].bitcast(FP8X4),
-                    rhs_scale=hb_sc[h][b][:],
-                    start=(b == 0),
-                    stop=(b == PASSES - 1),
-                )
-            o = ring.tile([P, HALF], F32, name="o", tag="o", bufs=8)
-            nc.scalar.activation(o[:], acc, ACT.Tanh, scale=0.00390625)
-            if len(count) < X8_ON_VECTOR_FROM:
-                nc.gpsimd.tensor_scalar(o[:], o[:], 8.0, 0.0, ALU.mult, ALU.add)
+        def scores(blocks, cap_engine):
+            o = ring.tile([P, len(blocks), HALF], F32, name="o", tag="o", bufs=10)
+            for n, (i, h) in enumerate(blocks):
+                bank = psum.tile([P, 4, P], F32, name="bank", tag="bank", bufs=7)
+                acc = bank[:].rearrange("p t n -> p (t n)")
+                for b in range(PASSES):
+                    ca = 2 * P * i + P * b
+                    cb = 2 * HALF * h + HALF * b
+                    nc.tensor.matmul_mx(
+                        acc,
+                        lhsT=ha_q[:, ca : ca + P].bitcast(FP8X4),
+                        lhsT_scale=ha_sc[:, ca : ca + P],
+                        rhs=hb_q[:, cb : cb + HALF].bitcast(FP8X4),
+                        rhs_scale=hb_sc[:, cb : cb + HALF],
+                        start=(b == 0),
+                        stop=(b == PASSES - 1),
+                    )
+                nc.scalar.activation(o[:, n], acc, ACT.Tanh, scale=0.00390625)
+            if cap_engine == "gpsimd":
+                for n in range(len(blocks)):
+                    nc.gpsimd.tensor_scalar(o[:, n], o[:, n], 8.0, 0.0, ALU.mult, ALU.add)
+            elif cap_engine == "scalar":
+                nc.scalar.activation(o[:], o[:], ACT.Copy, scale=8.0)
             else:
                 nc.vector.tensor_scalar_mul(o[:], o[:], 8.0)
-            count.append(0)
-            nc.sync.dma_start(out[P * i : P * (i + 1), HALF * h : HALF * (h + 1)], o[:])
+            for n, (i, h) in enumerate(blocks):
+                nc.sync.dma_start(out[P * i : P * (i + 1), HALF * h : HALF * (h + 1)], o[:, n])
 
-        round_wb(0)
-        round_wb(1)
+        permute_wa_scales()
         gather_scales(0, 0)
         gather_scales(1, 0)
         gather_scales(1, 1)
         gather_scales(0, 1)
-        quantize_wb(0)
         permute_wa()
-        quantize_wb(1)
         gather_words(0, 0)
         gather_words(1, 0)
+        round_wb(0)
         gather_words(1, 1)
+        quantize_wb(0)
         gather_words(0, 1)
         for i in range(4):
             a_tile(i)
+        quantize_later(ha_q, ha_sc, ha_h, 0, 1024)
+        round_wb(1)
+        quantize_wb(1)
         for h in range(2):
             for b in range(PASSES):
-                b_unit(h, b)
-        a_tile(4)
-        for i in range(4):
-            scores(i, 0)
-        a_tile(5)
-        for i in range(4):
-            scores(i, 1)
-        a_tile(6)
-        a_tile(7)
-        flush()
+                for u in range(2):
+                    b_unit(h, b, u)
+            quantize_later(hb_q, hb_sc, hb_h, 1024 * h, 1024 * (h + 1))
         for i in range(4, 8):
-            for h in range(2):
-                scores(i, h)
+            a_tile(i)
+            quantize_later(ha_q, ha_sc, ha_h, 256 * i, 256 * (i + 1))
+            if i == 5:
+                scores([(0, 0), (1, 0)], "gpsimd")
+                scores([(2, 0), (3, 0)], "gpsimd")
+        flush()
+        scores([(0, 1), (1, 1)], "scalar")
+        scores([(2, 1), (3, 1)], "scalar")
+        for i in range(4, 7):
+            scores([(i, 0), (i, 1)], "vector")
+        scores([(7, 0)], "vector")
+        scores([(7, 1)], "vector")

@@ -20,6 +20,8 @@ ALU = mybir.AluOpType
 P = 128
 PASSES = 2
 HALF = 512
+CAPS_AFTER = {6: ((0, 1), (1, 1)), 7: ((2, 1), (3, 1)), 8: tuple((i, h) for i in range(4, 8) for h in range(2))}
+EARLY = 4
 
 
 def tile_list_biaff_gelu_cap_kernel(
@@ -28,7 +30,7 @@ def tile_list_biaff_gelu_cap_kernel(
     nc = tc.nc
     with ExitStack() as ctx:
         keep = ctx.enter_context(tc.tile_pool(name="keep", bufs=1))
-        ring = ctx.enter_context(tc.tile_pool(name="ring", bufs=1))
+        late = ctx.enter_context(tc.tile_pool(name="late", bufs=1))
         psum = ctx.enter_context(tc.psum_pool(name="psum", bufs=1))
 
         list_a = keep.tile([P, M // 16], U16, name="list_a")
@@ -36,47 +38,37 @@ def tile_list_biaff_gelu_cap_kernel(
         table = keep.tile([P, T], I32, name="table", align_bytes=64)
         table_sc = keep.tile([P, T // 4], I32, name="table_sc", align_bytes=64)
         wa_raw = keep.tile([P, R // 2], I32, name="wa_raw", align_bytes=64)
-        wa_sc_raw = keep.tile([P, R // 4], I32, name="wa_sc_raw", align_bytes=64)
+        wa_sc_raw = late.tile([P, R // 4], I32, name="wa_sc_raw", align_bytes=64, offset=2048 - 512)
         wa_p = keep.tile([P, R // 2], I32, name="wa_p", align_bytes=64)
         wa_sc = keep.tile([P, R // 4], I32, name="wa_sc", align_bytes=64)
-        wb_raw = [keep.tile([P, 4, HALF], F32, name=f"wb_raw{b}") for b in range(PASSES)]
-        wb_h = [keep.tile([P, 4 * HALF], BF16, name=f"wb_h{b}", align_bytes=64) for b in range(PASSES)]
-        wb_q = [keep.tile([P, HALF], U32, name=f"wb_q{b}", align_bytes=64) for b in range(PASSES)]
-        wb_sc = [keep.tile([P, HALF], U8, name=f"wb_sc{b}", align_bytes=64) for b in range(PASSES)]
+        wb_raw = [late.tile([P, 4, HALF], F32, name=f"wb_raw{b}", align_bytes=64, offset=4096 + 8192 * b) for b in range(PASSES)]
+        wb_q = keep.tile([P, R], U32, name="wb_q", align_bytes=64)
+        wb_sc = keep.tile([P, R], U8, name="wb_sc", align_bytes=64)
         rows = keep.tile([P, 2 * P], F32, name="rows")
         ident = keep.tile([P, P], F32, name="ident")
         warm_in = keep.tile([P, 1], F32, name="warm_in")
         warm_out = keep.tile([P, 1], F32, name="warm_out")
 
-        def load_wb(b):
-            nc.sync.dma_start(wb_raw[b][:], wb[:, b * HALF : (b + 1) * HALF].rearrange("(p j) c -> p j c", j=4))
-
-        def load_wa_scales(queue, q):
-            queue.dma_start(wa_sc_raw[32 * q : 32 * q + 4, :], wa_scales[0, 4 * q : 4 * q + 4, :].bitcast(I32))
-
-        nc.vector.memset(table_sc[:], 0)
+        nc.gpsimd.memset(table_sc[:], 0)
+        nc.vector.memset(wa_sc_raw[:], 0)
         nc.gpsimd.memset(rows[:], 0.0)
         nc.sync.dma_start(list_a[:], offs)
-        load_wa_scales(nc.scalar, 1)
-        nc.sync.dma_start(wa_raw[:], wa_words[0].bitcast(I32))
-        load_wa_scales(nc.sync, 0)
-        for q in range(4):
-            queue = nc.sync if q < 2 else nc.scalar
-            queue.dma_start(table_sc[32 * q : 32 * q + 4, :], tab_scales[0, 4 * q : 4 * q + 4, :].bitcast(I32))
-        load_wa_scales(nc.sync, 2)
-        load_wa_scales(nc.sync, 3)
         nc.sync.dma_start(list_b[:], offs2)
+        nc.sync.dma_start(wa_raw[:], wa_words[0].bitcast(I32))
+        for q in range(4):
+            nc.sync.dma_start(table_sc[32 * q : 32 * q + 4, :], tab_scales[0, 4 * q : 4 * q + 4, :].bitcast(I32))
         nc.sync.dma_start(table[:], tab_words[0].rearrange("p t i -> p (t i)").bitcast(I32))
-        for side, (s, queue) in enumerate(((sa, nc.sync), (sb, nc.gpsimd))):
-            queue.dma_start(
+        for side, s in enumerate((sa, sb)):
+            nc.sync.dma_start(
                 rows[4 * side : 4 * side + 4, :].rearrange("t (c i) -> t c i", i=8),
                 s.rearrange("(c t i) -> t c i", t=4, i=8),
             )
-        load_wb(0)
-        load_wb(1)
+        for q in range(4):
+            nc.sync.dma_start(wa_sc_raw[32 * q : 32 * q + 4, :], wa_scales[0, 4 * q : 4 * q + 4, :].bitcast(I32))
+        for b in range(PASSES):
+            nc.sync.dma_start(wb_raw[b][:], wb[:, b * HALF : (b + 1) * HALF].rearrange("(p j) c -> p j c", j=4))
         nc.vector.memset(warm_in[:], 0.0)
         nc.scalar.activation(warm_out[:], warm_in[:], ACT.Gelu_apprx_tanh)
-        nc.vector.memset(wa_sc[:], 0)
         make_identity(nc, ident[:])
 
         factors = psum.tile([P, PASSES, P], F32, name="factors", tag="factors", bufs=1)
@@ -91,46 +83,43 @@ def tile_list_biaff_gelu_cap_kernel(
             v_sc[side, h] = keep.tile([P, HALF], U8, name=f"v_sc{side}{h}", align_bytes=64)
             nc.vector.tensor_copy(v_sc[side, h][:], table_sc[:].bitcast(U8).indirect(lists[side][:, 32 * h : 32 * h + 32]))
 
-        def gather_words(side, h):
-            v_words[side, h] = keep.tile([P, HALF], U32, name=f"v_words{side}{h}", align_bytes=64)
-            nc.vector.tensor_copy(v_words[side, h][:], table[:].bitcast(U32).indirect(lists[side][:, 32 * h : 32 * h + 32]))
+        def gather_words_a(h):
+            if h == 0:
+                v_words[0, h] = keep.tile([P, HALF], U32, name="v_words00", align_bytes=64)[:]
+            else:
+                v_words[0, h] = late.tile([P, HALF], U32, name="v_words01", align_bytes=64, offset=0)[:]
+            nc.vector.tensor_copy(v_words[0, h], table[:].bitcast(U32).indirect(list_a[:, 32 * h : 32 * h + 32]))
+
+        def gather_words_b(h):
+            v_words[1, h] = late.tile([P, HALF], U32, name=f"v_words1{h}", align_bytes=64, offset=2048 + 2048 * h)[:]
+            nc.vector.tensor_copy(v_words[1, h], table[:].bitcast(U32).indirect(list_b[:, 32 * h : 32 * h + 32]))
 
         def permute_wa():
-            for b in range(PASSES):
-                nc.vector.tensor_copy(
-                    wa_p[:, 256 * b : 256 * (b + 1)].rearrange("p (t q i) -> p t q i", t=4, i=4),
-                    wa_raw[:, 256 * b : 256 * (b + 1)].rearrange("p (q t i) -> p t q i", t=4, i=4),
-                )
+            nc.vector.tensor_copy(
+                wa_p[:].rearrange("p (b t q i) -> p b t q i", b=2, t=4, i=4),
+                wa_raw[:].rearrange("p (b q t i) -> p b t q i", b=2, t=4, i=4),
+            )
 
         def permute_wa_scales():
-            for q in range(4):
-                live = slice(32 * q, 32 * q + 4)
-                for b in range(PASSES):
-                    nc.vector.tensor_copy(
-                        wa_sc[live, 128 * b : 128 * (b + 1)].rearrange("p (t q i) -> p t q i", t=4, i=2),
-                        wa_sc_raw[live, 128 * b : 128 * (b + 1)].rearrange("p (q t i) -> p t q i", t=4, i=2),
-                    )
+            nc.vector.tensor_copy(
+                wa_sc[:].rearrange("p (b t q i) -> p b t q i", b=2, t=4, i=2),
+                wa_sc_raw[:].rearrange("p (b q t i) -> p b t q i", b=2, t=4, i=2),
+            )
 
-        def round_wb(b):
-            src = wb_raw[b][:].rearrange("p j (q t i) -> p t q i j", t=4, i=8)
-            for t in range(4):
-                dst = wb_h[b][:, HALF * t : HALF * (t + 1)].rearrange("p (q i j) -> p q i j", i=8, j=4)
-                if b == 0:
-                    nc.vector.tensor_copy(dst, src[:, t])
-                else:
-                    nc.scalar.activation(dst, src[:, t], ACT.Copy)
-
-        def quantize_wb(b):
-            nc.vector.quantize_mx(wb_q[b][:].bitcast(FP8X4), wb_sc[b][:], wb_h[b][:])
+        def round_wb(wb_h, b):
+            nc.vector.tensor_copy(
+                wb_h[:, 4 * HALF * b : 4 * HALF * (b + 1)].rearrange("p (t q i j) -> p t q i j", t=4, i=8, j=4),
+                wb_raw[b][:].rearrange("p j (q t i) -> p t q i j", t=4, i=8),
+            )
 
         def weights(side, b, t):
+            c = 4 * b + t
             if side == 0:
-                c = 4 * b + t
                 return (
                     wa_p[:].bitcast(U8)[:, 256 * c : 256 * (c + 1)].bitcast(FP4X4),
                     wa_sc[:].bitcast(U8)[:, P * c : P * (c + 1)],
                 )
-            return wb_q[b][:, P * t : P * (t + 1)].bitcast(FP8X4), wb_sc[b][:, P * t : P * (t + 1)]
+            return wb_q[:, P * c : P * (c + 1)].bitcast(FP8X4), wb_sc[:, P * c : P * (c + 1)]
 
         def hidden_bank(side, tile, b, dst):
             h, c0 = divmod(tile * P, HALF)
@@ -148,108 +137,120 @@ def tile_list_biaff_gelu_cap_kernel(
                 )
             nc.scalar.activation(dst, bank[:].rearrange("p t n -> p n t"), ACT.Gelu_apprx_tanh)
 
-        ha_q = keep.tile([P, 8 * 2 * P], U32, name="ha_q", align_bytes=64)
         ha_sc = keep.tile([P, 8 * 2 * P], U8, name="ha_sc", align_bytes=64)
-        ha_h = keep.tile([P, 8 * 1024], BF16, name="ha_h", align_bytes=64)
+        ha_q = keep.tile([P, 8 * 2 * P], U32, name="ha_q", align_bytes=64)
         hb_q = keep.tile([P, 4 * HALF], U32, name="hb_q", align_bytes=64)
         hb_sc = keep.tile([P, 4 * HALF], U8, name="hb_sc", align_bytes=64)
-        hb_h = keep.tile([P, 8 * 1024], BF16, name="hb_h", align_bytes=64)
 
-        pending = []
+        stage = keep.tile([P, 10 * 1024], BF16, name="stage", align_bytes=64)
+        gelus = keep.tile([P, 14, 1024], F32, name="gelus")
+        factors_sb = keep.tile([P, PASSES, 8], F32, name="factors_sb")
+        nc.scalar.copy(factors_sb[:], factors[:, :, 0:8])
 
-        def quantize_later(codes, sc, src, c0, c1):
-            pending.append((codes[:, c0:c1], sc[:, c0:c1], src[:, 4 * c0 : 4 * c1]))
+        def slots(first, count=1):
+            return stage[:, 1024 * first : 1024 * (first + count)]
 
-        def flush():
-            for codes, sc, src in pending:
-                nc.vector.quantize_mx(codes.bitcast(FP8X4), sc, src)
-            pending.clear()
+        def quantize(codes, sc, c0, c1, src):
+            nc.vector.quantize_mx(codes[:, c0:c1].bitcast(FP8X4), sc[:, c0:c1], src)
 
-        def a_tile(i):
-            g = ring.tile([P, 2, P, 4], F32, name="g", tag="g", bufs=12)
+        def gelu_a(i):
+            g = gelus[:, (0, 1, 2, 3, 4, 5, 0, 11)[i]].rearrange("p (s n t) -> p s n t", s=2, t=4)
             for b in range(PASSES):
                 hidden_bank(0, i, b, g[:, b])
-            nc.vector.tensor_tensor(
-                ha_h[:, 1024 * i : 1024 * (i + 1)].rearrange("p (b n t) -> p b n t", b=2, t=4),
-                g[:],
-                factors[:, :, 0:4].unsqueeze(2).to_broadcast([P, 2, P, 4]),
-                ALU.mult,
-            )
-            flush()
+            return g
 
-        def b_unit(h, b, u):
-            g = ring.tile([P, 2, P, 4], F32, name="g", tag="g", bufs=12)
+        def gelu_b(h, b, u):
+            g = gelus[:, 6 + 4 * h + 2 * b + u].rearrange("p (s n t) -> p s n t", s=2, t=4)
             for s in range(2):
                 hidden_bank(1, 4 * h + 2 * u + s, b, g[:, s])
-            c0 = 1024 * (4 * h + 2 * b + u)
-            nc.vector.tensor_tensor(
-                hb_h[:, c0 : c0 + 1024].rearrange("p (n t) -> p n t", t=4),
-                g[:].rearrange("p s n t -> p (s n) t"),
-                factors[:, b, 4:8].unsqueeze(1).to_broadcast([P, 2 * P, 4]),
+            return g
+
+        def scale_a(g, dst, on_gpsimd=False):
+            engine, f = (nc.gpsimd, factors_sb) if on_gpsimd else (nc.vector, factors)
+            engine.tensor_tensor(
+                dst.rearrange("p (b n t) -> p b n t", b=2, t=4),
+                g,
+                f[:, :, 0:4].unsqueeze(2).to_broadcast([P, 2, P, 4]),
                 ALU.mult,
             )
-            flush()
 
-        def scores(blocks, cap_engine):
-            o = ring.tile([P, len(blocks), HALF], F32, name="o", tag="o", bufs=10)
-            for n, (i, h) in enumerate(blocks):
-                bank = psum.tile([P, 4, P], F32, name="bank", tag="bank", bufs=7)
-                acc = bank[:].rearrange("p t n -> p (t n)")
-                for b in range(PASSES):
-                    ca = 2 * P * i + P * b
-                    cb = 2 * HALF * h + HALF * b
-                    nc.tensor.matmul_mx(
-                        acc,
-                        lhsT=ha_q[:, ca : ca + P].bitcast(FP8X4),
-                        lhsT_scale=ha_sc[:, ca : ca + P],
-                        rhs=hb_q[:, cb : cb + HALF].bitcast(FP8X4),
-                        rhs_scale=hb_sc[:, cb : cb + HALF],
-                        start=(b == 0),
-                        stop=(b == PASSES - 1),
-                    )
-                nc.scalar.activation(o[:, n], acc, ACT.Tanh, scale=0.00390625)
-            if cap_engine == "gpsimd":
-                for n in range(len(blocks)):
-                    nc.gpsimd.tensor_scalar(o[:, n], o[:, n], 8.0, 0.0, ALU.mult, ALU.add)
-            elif cap_engine == "scalar":
-                nc.scalar.activation(o[:], o[:], ACT.Copy, scale=8.0)
+        def scale_b(g, b, dst, on_gpsimd=False):
+            engine, f = (nc.gpsimd, factors_sb) if on_gpsimd else (nc.vector, factors)
+            engine.tensor_tensor(
+                dst.rearrange("p (n t) -> p n t", t=4),
+                g.rearrange("p s n t -> p (s n) t"),
+                f[:, b, 4:8].unsqueeze(1).to_broadcast([P, 2 * P, 4]),
+                ALU.mult,
+            )
+
+        outs = {}
+
+        def score(i, h):
+            o = keep.tile([P, HALF], F32, name=f"o{i}{h}")
+            outs[i, h] = o
+            bank = psum.tile([P, 4, P], F32, name="bank", tag="bank", bufs=7)
+            acc = bank[:].rearrange("p t n -> p (t n)")
+            for b in range(PASSES):
+                ca = 2 * P * i + P * b
+                cb = 2 * HALF * h + HALF * b
+                nc.tensor.matmul_mx(
+                    acc,
+                    lhsT=ha_q[:, ca : ca + P].bitcast(FP8X4),
+                    lhsT_scale=ha_sc[:, ca : ca + P],
+                    rhs=hb_q[:, cb : cb + HALF].bitcast(FP8X4),
+                    rhs_scale=hb_sc[:, cb : cb + HALF],
+                    start=(b == 0),
+                    stop=(b == PASSES - 1),
+                )
+            nc.scalar.activation(o[:], acc, ACT.Tanh, scale=0.00390625)
+
+        def cap(i, h, cap_engine, dst=None):
+            o = outs[i, h][:]
+            dst = o if dst is None else dst
+            if cap_engine == "scalar":
+                nc.scalar.activation(dst, o, ACT.Copy, scale=8.0)
             else:
-                nc.vector.tensor_scalar_mul(o[:], o[:], 8.0)
-            for n, (i, h) in enumerate(blocks):
-                nc.sync.dma_start(out[P * i : P * (i + 1), HALF * h : HALF * (h + 1)], o[:, n])
+                nc.vector.tensor_scalar_mul(dst, o, 8.0)
+            nc.sync.dma_start(out[P * i : P * (i + 1), HALF * h : HALF * (h + 1)], dst)
 
-        permute_wa_scales()
-        gather_scales(0, 0)
-        gather_scales(1, 0)
-        gather_scales(1, 1)
-        gather_scales(0, 1)
+        for side in range(2):
+            for h in range(2):
+                gather_scales(side, h)
         permute_wa()
-        gather_words(0, 0)
-        gather_words(1, 0)
-        round_wb(0)
-        gather_words(1, 1)
-        quantize_wb(0)
-        gather_words(0, 1)
-        for i in range(4):
-            a_tile(i)
-        quantize_later(ha_q, ha_sc, ha_h, 0, 1024)
-        round_wb(1)
-        quantize_wb(1)
+        gather_words_a(0)
+        permute_wa_scales()
+        gather_words_a(1)
+        gather_words_b(0)
+        ga = [gelu_a(i) for i in range(6)]
+        round_wb(stage, 0)
+        gather_words_b(1)
+        round_wb(stage, 1)
+        quantize(wb_q, wb_sc, 0, R, slots(0, 4))
+        gb = {(h, b, u): gelu_b(h, b, u) for h in range(2) for b in range(PASSES) for u in range(2)}
+        for i in range(EARLY):
+            scale_a(ga[i], slots(i), on_gpsimd=(i == 0))
+        quantize(ha_q, ha_sc, 0, 1024, slots(0, 4))
         for h in range(2):
             for b in range(PASSES):
                 for u in range(2):
-                    b_unit(h, b, u)
-            quantize_later(hb_q, hb_sc, hb_h, 1024 * h, 1024 * (h + 1))
-        for i in range(4, 8):
-            a_tile(i)
-            quantize_later(ha_q, ha_sc, ha_h, 256 * i, 256 * (i + 1))
-            if i == 5:
-                scores([(0, 0), (1, 0)], "gpsimd")
-                scores([(2, 0), (3, 0)], "gpsimd")
-        flush()
-        scores([(0, 1), (1, 1)], "scalar")
-        scores([(2, 1), (3, 1)], "scalar")
-        for i in range(4, 7):
-            scores([(i, 0), (i, 1)], "vector")
-        scores([(7, 0)], "vector")
-        scores([(7, 1)], "vector")
+                    scale_b(gb[h, b, u], b, slots(3 + 3 * h + 2 * b + u), on_gpsimd=(b == 0 and u == 0))
+            if h == 1:
+                ga.append(gelu_a(7))
+            quantize(hb_q, hb_sc, 1024 * h, 1024 * (h + 1), slots(3 + 3 * h, 4))
+            if h == 0:
+                ga.append(gelu_a(6))
+            for i in range(EARLY):
+                score(i, h)
+                if h == 0 and i < 3:
+                    cap(i, 0, "scalar")
+        cap(3, 0, "vector", gelus[:, 10, 0:HALF])
+        late_slot = (3, 4, 5, 0)
+        for i in range(EARLY, 9):
+            if i < 8:
+                scale_a(ga[i], slots(late_slot[i - EARLY]))
+            if i > EARLY:
+                quantize(ha_q, ha_sc, 256 * (i - 1), 256 * i, slots(late_slot[i - 1 - EARLY]))
+                for h in range(2):
+                    score(i - 1, h)
+            for key in CAPS_AFTER.get(i, ()):
+                cap(key[0], key[1], "vector")

@@ -20,7 +20,6 @@ ALU = mybir.AluOpType
 P = 128
 PASSES = 2
 HALF = 512
-CAPS_AFTER = {6: ((0, 1), (1, 1)), 7: ((2, 1), (3, 1)), 8: tuple((i, h) for i in range(4, 8) for h in range(2))}
 EARLY = 4
 
 
@@ -142,7 +141,7 @@ def tile_list_biaff_gelu_cap_kernel(
         hb_q = keep.tile([P, 4 * HALF], U32, name="hb_q", align_bytes=64)
         hb_sc = keep.tile([P, 4 * HALF], U8, name="hb_sc", align_bytes=64)
 
-        stage = keep.tile([P, 10 * 1024], BF16, name="stage", align_bytes=64)
+        stage = keep.tile([P, 6 * 1024], BF16, name="stage", align_bytes=64)
         gelus = keep.tile([P, 14, 1024], F32, name="gelus")
         factors_sb = keep.tile([P, PASSES, 8], F32, name="factors_sb")
         nc.scalar.copy(factors_sb[:], factors[:, :, 0:8])
@@ -207,7 +206,9 @@ def tile_list_biaff_gelu_cap_kernel(
         def cap(i, h, cap_engine, dst=None):
             o = outs[i, h][:]
             dst = o if dst is None else dst
-            if cap_engine == "scalar":
+            if cap_engine == "gpsimd":
+                nc.gpsimd.tensor_scalar(dst, o, 8.0, 0.0, ALU.mult, ALU.add)
+            elif cap_engine == "scalar":
                 nc.scalar.activation(dst, o, ACT.Copy, scale=8.0)
             else:
                 nc.vector.tensor_scalar_mul(dst, o, 8.0)
@@ -230,27 +231,45 @@ def tile_list_biaff_gelu_cap_kernel(
         for i in range(EARLY):
             scale_a(ga[i], slots(i), on_gpsimd=(i == 0))
         quantize(ha_q, ha_sc, 0, 1024, slots(0, 4))
-        for h in range(2):
+
+        def scale_half(h):
             for b in range(PASSES):
                 for u in range(2):
-                    scale_b(gb[h, b, u], b, slots(3 + 3 * h + 2 * b + u), on_gpsimd=(b == 0 and u == 0))
-            if h == 1:
-                ga.append(gelu_a(7))
-            quantize(hb_q, hb_sc, 1024 * h, 1024 * (h + 1), slots(3 + 3 * h, 4))
-            if h == 0:
-                ga.append(gelu_a(6))
-            for i in range(EARLY):
+                    scale_b(gb[h, b, u], b, slots(2 * b + u), on_gpsimd=(b == 0 and u == 0))
+
+        def quantize_a(i, slot):
+            quantize(ha_q, ha_sc, 256 * i, 256 * (i + 1), slots(slot))
+            for h in range(2):
                 score(i, h)
-                if h == 0 and i < 3:
-                    cap(i, 0, "scalar")
-        cap(3, 0, "vector", gelus[:, 10, 0:HALF])
-        late_slot = (3, 4, 5, 0)
-        for i in range(EARLY, 9):
-            if i < 8:
-                scale_a(ga[i], slots(late_slot[i - EARLY]))
-            if i > EARLY:
-                quantize(ha_q, ha_sc, 256 * (i - 1), 256 * i, slots(late_slot[i - 1 - EARLY]))
-                for h in range(2):
-                    score(i - 1, h)
-            for key in CAPS_AFTER.get(i, ()):
-                cap(key[0], key[1], "vector")
+
+        scale_half(0)
+        quantize(hb_q, hb_sc, 0, 1024, slots(0, 4))
+        ga.append(gelu_a(6))
+        for i in range(EARLY):
+            score(i, 0)
+            if i < 2:
+                cap(i, 0, "scalar")
+        scale_half(1)
+        ga.append(gelu_a(7))
+        cap(2, 0, "vector", gelus[:, 12, 0:HALF])
+        quantize(hb_q, hb_sc, 1024, 2048, slots(0, 4))
+        for i in range(EARLY):
+            score(i, 1)
+        cap(3, 0, "gpsimd", slots(2).bitcast(F32))
+        cap(0, 1, "gpsimd", slots(3).bitcast(F32))
+        scale_a(ga[4], slots(0))
+        scale_a(ga[5], slots(1))
+        quantize_a(4, 0)
+        quantize_a(5, 1)
+        cap(1, 1, "gpsimd", slots(1).bitcast(F32))
+        scale_a(ga[6], slots(4))
+        cap(2, 1, "vector")
+        quantize_a(6, 4)
+        cap(3, 1, "gpsimd", slots(4).bitcast(F32))
+        scale_a(ga[7], slots(5))
+        cap(4, 0, "vector")
+        cap(4, 1, "vector")
+        quantize_a(7, 5)
+        for i in range(5, 8):
+            for h in range(2):
+                cap(i, h, "vector")

@@ -20,6 +20,9 @@ ALU = mybir.AluOpType
 P = 128
 PASSES = 2
 HALF = 512
+UNIT_ORDER = (0, 2, 3, 1)
+GELU_ORDER = ((0, 1, 2, 3), UNIT_ORDER)
+ROW0 = 112
 EARLY = 4
 
 
@@ -35,12 +38,11 @@ def tile_list_biaff_gelu_cap_kernel(
         list_a = keep.tile([P, M // 16], U16, name="list_a")
         list_b = keep.tile([P, J // 16], U16, name="list_b")
         table = keep.tile([P, T], I32, name="table", align_bytes=64)
-        table_sc = keep.tile([P, T // 4], I32, name="table_sc", align_bytes=64)
-        wa_raw = keep.tile([P, R // 2], I32, name="wa_raw", align_bytes=64)
-        wa_sc_raw = late.tile([P, R // 4], I32, name="wa_sc_raw", align_bytes=64, offset=2048 - 512)
+        table_sc = late.tile([P, T // 4], I32, name="table_sc", align_bytes=64, offset=8192)
+        wa_raw = late.tile([P, R // 2], I32, name="wa_raw", align_bytes=64, offset=2048)
+        wa_sc_raw = keep.tile([P, R // 4], I32, name="wa_sc_raw", align_bytes=64)
         wa_p = keep.tile([P, R // 2], I32, name="wa_p", align_bytes=64)
-        wa_sc = keep.tile([P, R // 4], I32, name="wa_sc", align_bytes=64)
-        wb_raw = [late.tile([P, 4, HALF], F32, name=f"wb_raw{b}", align_bytes=64, offset=4096 + 8192 * b) for b in range(PASSES)]
+        wb_raw = [late.tile([P, 4, HALF], F32, name=f"wb_raw{b}", align_bytes=64, offset=8192 + 8192 * b) for b in range(PASSES)]
         wb_q = keep.tile([P, R], U32, name="wb_q", align_bytes=64)
         wb_sc = keep.tile([P, R], U8, name="wb_sc", align_bytes=64)
         rows = keep.tile([P, 2 * P], F32, name="rows")
@@ -48,24 +50,25 @@ def tile_list_biaff_gelu_cap_kernel(
         warm_in = keep.tile([P, 1], F32, name="warm_in")
         warm_out = keep.tile([P, 1], F32, name="warm_out")
 
-        nc.gpsimd.memset(table_sc[:], 0)
-        nc.vector.memset(wa_sc_raw[:], 0)
+        nc.vector.memset(table_sc[0:ROW0, :], 0)
+        nc.vector.memset(wa_sc_raw[96:ROW0, :], 0)
         nc.gpsimd.memset(rows[:], 0.0)
+        plane_a = keep.tile([P, (M + R) // 4], I32, name="plane_a", align_bytes=64)
+        plane_b = keep.tile([P, J // 4], I32, name="plane_b", align_bytes=64)
+        spread_a = keep.tile([P, (M + R) // 4], I32, name="spread_a", align_bytes=64)
+        nc.gpsimd.memset(plane_a[:], 0)
+        nc.gpsimd.memset(plane_b[:], 0)
+        nc.sync.dma_start(table_sc[ROW0:P, :], tab_scales[0].bitcast(I32))
         nc.sync.dma_start(list_a[:], offs)
+        nc.sync.dma_start(wa_sc_raw[ROW0:P, :], wa_scales[0].bitcast(I32))
         nc.sync.dma_start(list_b[:], offs2)
-        nc.sync.dma_start(wa_raw[:], wa_words[0].bitcast(I32))
-        for q in range(4):
-            nc.sync.dma_start(table_sc[32 * q : 32 * q + 4, :], tab_scales[0, 4 * q : 4 * q + 4, :].bitcast(I32))
         nc.sync.dma_start(table[:], tab_words[0].rearrange("p t i -> p (t i)").bitcast(I32))
+        nc.sync.dma_start(wa_raw[:], wa_words[0].bitcast(I32))
         for side, s in enumerate((sa, sb)):
             nc.sync.dma_start(
                 rows[4 * side : 4 * side + 4, :].rearrange("t (c i) -> t c i", i=8),
                 s.rearrange("(c t i) -> t c i", t=4, i=8),
             )
-        for q in range(4):
-            nc.sync.dma_start(wa_sc_raw[32 * q : 32 * q + 4, :], wa_scales[0, 4 * q : 4 * q + 4, :].bitcast(I32))
-        for b in range(PASSES):
-            nc.sync.dma_start(wb_raw[b][:], wb[:, b * HALF : (b + 1) * HALF].rearrange("(p j) c -> p j c", j=4))
         nc.vector.memset(warm_in[:], 0.0)
         nc.scalar.activation(warm_out[:], warm_in[:], ACT.Gelu_apprx_tanh)
         make_identity(nc, ident[:])
@@ -78,20 +81,37 @@ def tile_list_biaff_gelu_cap_kernel(
         v_words = {}
         v_sc = {}
 
-        def gather_scales(side, h):
-            v_sc[side, h] = keep.tile([P, HALF], U8, name=f"v_sc{side}{h}", align_bytes=64)
-            nc.vector.tensor_copy(v_sc[side, h][:], table_sc[:].bitcast(U8).indirect(lists[side][:, 32 * h : 32 * h + 32]))
+        def carry_rows(queue, plane, spread):
+            for q in range(4):
+                queue.dma_start(plane[32 * q : 32 * q + 4, :], spread[ROW0 + 4 * q : ROW0 + 4 * q + 4, :])
+
+        def gather_scales(side):
+            picked = late.tile([P, M], U8, name=f"picked{side}", align_bytes=64, offset=0)
+            nc.vector.tensor_copy(picked[:], table_sc[:].bitcast(U8).indirect(lists[side][:]))
+            if side == 0:
+                permute_wa_scales()
+                nc.vector.tensor_copy(spread_a[96:P, 0 : M // 4], picked[:].bitcast(I32)[96:P, :])
+                carry_rows(nc.scalar, plane_a[:], spread_a[:])
+            else:
+                for b in range(PASSES):
+                    nc.sync.dma_start(wb_raw[b][:], wb[:, b * HALF : (b + 1) * HALF].rearrange("(p j) c -> p j c", j=4))
+                carry_rows(nc.sync, plane_b[:], picked[:].bitcast(I32))
+            plane = (plane_a, plane_b)[side]
+            for h in range(2):
+                v_sc[side, h] = plane[:].bitcast(U8)[:, HALF * h : HALF * (h + 1)]
 
         def gather_words_a(h):
             if h == 0:
                 v_words[0, h] = keep.tile([P, HALF], U32, name="v_words00", align_bytes=64)[:]
             else:
-                v_words[0, h] = late.tile([P, HALF], U32, name="v_words01", align_bytes=64, offset=0)[:]
+                v_words[0, h] = late.tile([P, HALF], U32, name="v_words01", align_bytes=64, offset=1024)[:]
             nc.vector.tensor_copy(v_words[0, h], table[:].bitcast(U32).indirect(list_a[:, 32 * h : 32 * h + 32]))
 
-        def gather_words_b(h):
-            v_words[1, h] = late.tile([P, HALF], U32, name=f"v_words1{h}", align_bytes=64, offset=2048 + 2048 * h)[:]
-            nc.vector.tensor_copy(v_words[1, h], table[:].bitcast(U32).indirect(list_b[:, 32 * h : 32 * h + 32]))
+        def gather_words_b():
+            words = late.tile([P, J], U32, name="v_words1", align_bytes=64, offset=3072)
+            nc.vector.tensor_copy(words[:], table[:].bitcast(U32).indirect(list_b[:]))
+            for h in range(2):
+                v_words[1, h] = words[:, HALF * h : HALF * (h + 1)]
 
         def permute_wa():
             nc.vector.tensor_copy(
@@ -101,13 +121,13 @@ def tile_list_biaff_gelu_cap_kernel(
 
         def permute_wa_scales():
             nc.vector.tensor_copy(
-                wa_sc[:].rearrange("p (b t q i) -> p b t q i", b=2, t=4, i=2),
-                wa_sc_raw[:].rearrange("p (b q t i) -> p b t q i", b=2, t=4, i=2),
+                spread_a[96:P, M // 4 :].rearrange("p (b t q i) -> p b t q i", b=2, t=4, i=2),
+                wa_sc_raw[96:P, :].rearrange("p (b q t i) -> p b t q i", b=2, t=4, i=2),
             )
 
-        def round_wb(wb_h, b):
+        def round_wb(dst, b):
             nc.vector.tensor_copy(
-                wb_h[:, 4 * HALF * b : 4 * HALF * (b + 1)].rearrange("p (t q i j) -> p t q i j", t=4, i=8, j=4),
+                dst.rearrange("p (t q i j) -> p t q i j", t=4, i=8, j=4),
                 wb_raw[b][:].rearrange("p j (q t i) -> p t q i j", t=4, i=8),
             )
 
@@ -116,7 +136,7 @@ def tile_list_biaff_gelu_cap_kernel(
             if side == 0:
                 return (
                     wa_p[:].bitcast(U8)[:, 256 * c : 256 * (c + 1)].bitcast(FP4X4),
-                    wa_sc[:].bitcast(U8)[:, P * c : P * (c + 1)],
+                    plane_a[:].bitcast(U8)[:, M + P * c : M + P * (c + 1)],
                 )
             return wb_q[:, P * c : P * (c + 1)].bitcast(FP8X4), wb_sc[:, P * c : P * (c + 1)]
 
@@ -141,19 +161,28 @@ def tile_list_biaff_gelu_cap_kernel(
         hb_q = keep.tile([P, 4 * HALF], U32, name="hb_q", align_bytes=64)
         hb_sc = keep.tile([P, 4 * HALF], U8, name="hb_sc", align_bytes=64)
 
-        stage = keep.tile([P, 6 * 1024], BF16, name="stage", align_bytes=64)
+        pairs = [
+            keep.tile([P, 2048], BF16, name="pair0", align_bytes=64),
+            late.tile([P, 2048], BF16, name="pair1", align_bytes=64, offset=16384),
+            keep.tile([P, 2048], BF16, name="pair2", align_bytes=64),
+        ]
         gelus = keep.tile([P, 14, 1024], F32, name="gelus")
         factors_sb = keep.tile([P, PASSES, 8], F32, name="factors_sb")
         nc.scalar.copy(factors_sb[:], factors[:, :, 0:8])
 
         def slots(first, count=1):
-            return stage[:, 1024 * first : 1024 * (first + count)]
+            c0 = 1024 * (first % 2)
+            return pairs[first // 2][:, c0 : c0 + 1024 * count]
 
         def quantize(codes, sc, c0, c1, src):
             nc.vector.quantize_mx(codes[:, c0:c1].bitcast(FP8X4), sc[:, c0:c1], src)
 
+        def quantize_stage(codes, sc, c0):
+            for n in (1, 0):
+                quantize(codes, sc, c0 + HALF * n, c0 + HALF * (n + 1), slots(2 * n, 2))
+
         def gelu_a(i):
-            g = gelus[:, (0, 1, 2, 3, 4, 5, 0, 11)[i]].rearrange("p (s n t) -> p s n t", s=2, t=4)
+            g = gelus[:, (0, 1, 2, 3, 4, 5, 0, 12)[i]].rearrange("p (s n t) -> p s n t", s=2, t=4)
             for b in range(PASSES):
                 hidden_bank(0, i, b, g[:, b])
             return g
@@ -184,8 +213,10 @@ def tile_list_biaff_gelu_cap_kernel(
 
         outs = {}
 
+        result = [keep.tile([P, J], F32, name=f"result{i}") for i in range(8)]
+
         def score(i, h):
-            o = keep.tile([P, HALF], F32, name=f"o{i}{h}")
+            o = result[i][:, HALF * h : HALF * (h + 1)]
             outs[i, h] = o
             bank = psum.tile([P, 4, P], F32, name="bank", tag="bank", bufs=7)
             acc = bank[:].rearrange("p t n -> p (t n)")
@@ -201,10 +232,10 @@ def tile_list_biaff_gelu_cap_kernel(
                     start=(b == 0),
                     stop=(b == PASSES - 1),
                 )
-            nc.scalar.activation(o[:], acc, ACT.Tanh, scale=0.00390625)
+            nc.scalar.activation(o, acc, ACT.Tanh, scale=0.00390625)
 
         def cap(i, h, cap_engine, dst=None):
-            o = outs[i, h][:]
+            o = outs[i, h]
             dst = o if dst is None else dst
             if cap_engine == "gpsimd":
                 nc.gpsimd.tensor_scalar(dst, o, 8.0, 0.0, ALU.mult, ALU.add)
@@ -214,28 +245,29 @@ def tile_list_biaff_gelu_cap_kernel(
                 nc.vector.tensor_scalar_mul(dst, o, 8.0)
             nc.sync.dma_start(out[P * i : P * (i + 1), HALF * h : HALF * (h + 1)], dst)
 
-        for side in range(2):
-            for h in range(2):
-                gather_scales(side, h)
-        permute_wa()
+        gather_scales(0)
+        gather_scales(1)
         gather_words_a(0)
-        permute_wa_scales()
+        permute_wa()
         gather_words_a(1)
-        gather_words_b(0)
+        gather_words_b()
         ga = [gelu_a(i) for i in range(6)]
-        round_wb(stage, 0)
-        gather_words_b(1)
-        round_wb(stage, 1)
-        quantize(wb_q, wb_sc, 0, R, slots(0, 4))
-        gb = {(h, b, u): gelu_b(h, b, u) for h in range(2) for b in range(PASSES) for u in range(2)}
-        for i in range(EARLY):
+        for b, first in ((0, 4), (1, 0)):
+            round_wb(slots(first, 2), b)
+            quantize(wb_q, wb_sc, HALF * b, HALF * (b + 1), slots(first, 2))
+        gb = {(h, n // 2, n % 2): gelu_b(h, n // 2, n % 2) for h in range(2) for n in GELU_ORDER[h]}
+        for i in UNIT_ORDER:
             scale_a(ga[i], slots(i), on_gpsimd=(i == 0))
-        quantize(ha_q, ha_sc, 0, 1024, slots(0, 4))
+        quantize_stage(ha_q, ha_sc, 0)
+
+        def cap_rows(i):
+            nc.vector.tensor_scalar_mul(result[i][:], result[i][:], 8.0)
+            nc.sync.dma_start(out[P * i : P * (i + 1), :], result[i][:])
 
         def scale_half(h):
-            for b in range(PASSES):
-                for u in range(2):
-                    scale_b(gb[h, b, u], b, slots(2 * b + u), on_gpsimd=(b == 0 and u == 0))
+            for n in UNIT_ORDER:
+                b, u = divmod(n, 2)
+                scale_b(gb[h, b, u], b, slots(n), on_gpsimd=(n == 0))
 
         def quantize_a(i, slot):
             quantize(ha_q, ha_sc, 256 * i, 256 * (i + 1), slots(slot))
@@ -243,33 +275,33 @@ def tile_list_biaff_gelu_cap_kernel(
                 score(i, h)
 
         scale_half(0)
-        quantize(hb_q, hb_sc, 0, 1024, slots(0, 4))
+        quantize_stage(hb_q, hb_sc, 0)
         ga.append(gelu_a(6))
         for i in range(EARLY):
             score(i, 0)
-            if i < 2:
+            if i in (1, 2):
                 cap(i, 0, "scalar")
         scale_half(1)
+        cap(0, 0, "gpsimd")
         ga.append(gelu_a(7))
-        cap(2, 0, "vector", gelus[:, 12, 0:HALF])
-        quantize(hb_q, hb_sc, 1024, 2048, slots(0, 4))
+        quantize_stage(hb_q, hb_sc, 1024)
         for i in range(EARLY):
             score(i, 1)
-        cap(3, 0, "gpsimd", slots(2).bitcast(F32))
-        cap(0, 1, "gpsimd", slots(3).bitcast(F32))
-        scale_a(ga[4], slots(0))
-        scale_a(ga[5], slots(1))
-        quantize_a(4, 0)
-        quantize_a(5, 1)
-        cap(1, 1, "gpsimd", slots(1).bitcast(F32))
+        cap(3, 0, "gpsimd", slots(0).bitcast(F32))
+        cap(0, 1, "gpsimd", slots(1).bitcast(F32))
+        scale_a(ga[4], slots(2))
+        scale_a(ga[5], slots(3))
+        quantize_a(4, 2)
+        quantize_a(5, 3)
+        cap(1, 1, "gpsimd", slots(3).bitcast(F32))
         scale_a(ga[6], slots(4))
         cap(2, 1, "vector")
         quantize_a(6, 4)
         cap(3, 1, "gpsimd", slots(4).bitcast(F32))
         scale_a(ga[7], slots(5))
-        cap(4, 0, "vector")
-        cap(4, 1, "vector")
+        cap_rows(4)
         quantize_a(7, 5)
-        for i in range(5, 8):
-            for h in range(2):
-                cap(i, h, "vector")
+        cap_rows(5)
+        cap_rows(6)
+        for h in range(2):
+            cap(7, h, "vector")

@@ -38,12 +38,12 @@ def tile_list_biaff_gelu_cap_kernel(
         list_a = keep.tile([P, M // 16], U16, name="list_a")
         list_b = keep.tile([P, J // 16], U16, name="list_b")
         table = keep.tile([P, T], I32, name="table", align_bytes=64)
-        table_sc = late.tile([P, T // 4], I32, name="table_sc", align_bytes=64, offset=8192)
+        table_sc = keep.tile([P, T // 4], I32, name="table_sc", align_bytes=64)
         wa_raw = late.tile([P, R // 2], I32, name="wa_raw", align_bytes=64, offset=2048)
         wa_sc_raw = keep.tile([P, R // 4], I32, name="wa_sc_raw", align_bytes=64)
         wa_p = keep.tile([P, R // 2], I32, name="wa_p", align_bytes=64)
         wb_raw = [late.tile([P, 4, HALF], F32, name=f"wb_raw{b}", align_bytes=64, offset=8192 + 8192 * b) for b in range(PASSES)]
-        wb_q = keep.tile([P, R], U32, name="wb_q", align_bytes=64)
+        wb_q = late.tile([P, R], U32, name="wb_q", align_bytes=64, offset=16384 + 4096)
         wb_sc = keep.tile([P, R], U8, name="wb_sc", align_bytes=64)
         rows = keep.tile([P, 2 * P], F32, name="rows")
         ident = keep.tile([P, P], F32, name="ident")
@@ -193,21 +193,21 @@ def tile_list_biaff_gelu_cap_kernel(
                 hidden_bank(1, 4 * h + 2 * u + s, b, g[:, s])
             return g
 
-        def scale_a(g, dst, on_gpsimd=False):
+        def scale_a(g, dst, on_gpsimd=False, n0=0, n1=P):
             engine, f = (nc.gpsimd, factors_sb) if on_gpsimd else (nc.vector, factors)
             engine.tensor_tensor(
-                dst.rearrange("p (b n t) -> p b n t", b=2, t=4),
-                g,
-                f[:, :, 0:4].unsqueeze(2).to_broadcast([P, 2, P, 4]),
+                dst.rearrange("p (b n t) -> p b n t", b=2, t=4)[:, :, n0:n1],
+                g[:, :, n0:n1],
+                f[:, :, 0:4].unsqueeze(2).to_broadcast([P, 2, n1 - n0, 4]),
                 ALU.mult,
             )
 
-        def scale_b(g, b, dst, on_gpsimd=False):
+        def scale_b(g, b, dst, on_gpsimd=False, n0=0, n1=2 * P):
             engine, f = (nc.gpsimd, factors_sb) if on_gpsimd else (nc.vector, factors)
             engine.tensor_tensor(
-                dst.rearrange("p (n t) -> p n t", t=4),
-                g.rearrange("p s n t -> p (s n) t"),
-                f[:, b, 4:8].unsqueeze(1).to_broadcast([P, 2 * P, 4]),
+                dst.rearrange("p (n t) -> p n t", t=4)[:, n0:n1],
+                g.rearrange("p s n t -> p (s n) t")[:, n0:n1],
+                f[:, b, 4:8].unsqueeze(1).to_broadcast([P, n1 - n0, 4]),
                 ALU.mult,
             )
 
@@ -254,10 +254,14 @@ def tile_list_biaff_gelu_cap_kernel(
         ga = [gelu_a(i) for i in range(6)]
         for b, first in ((0, 4), (1, 0)):
             round_wb(slots(first, 2), b)
+        for b, first in ((0, 4), (1, 0)):
             quantize(wb_q, wb_sc, HALF * b, HALF * (b + 1), slots(first, 2))
         gb = {(h, n // 2, n % 2): gelu_b(h, n // 2, n % 2) for h in range(2) for n in GELU_ORDER[h]}
-        for i in UNIT_ORDER:
-            scale_a(ga[i], slots(i), on_gpsimd=(i == 0))
+        scale_a(ga[0], slots(0), on_gpsimd=True)
+        scale_a(ga[1], slots(1), on_gpsimd=True, n1=P // 4)
+        scale_a(ga[2], slots(2))
+        scale_a(ga[3], slots(3))
+        scale_a(ga[1], slots(1), n0=P // 4)
         quantize_stage(ha_q, ha_sc, 0)
 
         def cap_rows(i):
@@ -267,7 +271,10 @@ def tile_list_biaff_gelu_cap_kernel(
         def scale_half(h):
             for n in UNIT_ORDER:
                 b, u = divmod(n, 2)
-                scale_b(gb[h, b, u], b, slots(n), on_gpsimd=(n == 0))
+                shared = P // 2 if (h, n) == (0, 1) else 0
+                scale_b(gb[h, b, u], b, slots(n), on_gpsimd=(n == 0), n0=shared)
+                if shared:
+                    scale_b(gb[h, b, u], b, slots(n), on_gpsimd=True, n1=shared)
 
         def quantize_a(i, slot):
             quantize(ha_q, ha_sc, 256 * i, 256 * (i + 1), slots(slot))

@@ -20,10 +20,25 @@ ALU = mybir.AluOpType
 P = 128
 PASSES = 2
 HALF = 512
+UNIT = 1024
+UNIT_WORDS = UNIT // 4
+TILES = M // P
+ROW0 = P - 16
+QUAD3 = 96
 UNIT_ORDER = (0, 2, 3, 1)
-GELU_ORDER = ((0, 1, 2, 3), UNIT_ORDER)
-ROW0 = 112
 EARLY = 4
+AHEAD = 6
+GELU_B0 = AHEAD
+BANKS = 7
+
+AT_WA_SCALES = 0
+AT_WORDS_A1 = 1024
+AT_WA = 2048
+AT_WORDS_B = 3072
+AT_PICKED_A = 7168
+AT_WB = (8192, 16384)
+AT_PAIR1 = AT_WB[1]
+AT_WB_CODES = AT_WB[1] + 4096
 
 
 def tile_list_biaff_gelu_cap_kernel(
@@ -32,283 +47,259 @@ def tile_list_biaff_gelu_cap_kernel(
     nc = tc.nc
     with ExitStack() as ctx:
         keep = ctx.enter_context(tc.tile_pool(name="keep", bufs=1))
-        late = ctx.enter_context(tc.tile_pool(name="late", bufs=1))
+        reuse = ctx.enter_context(tc.tile_pool(name="reuse", bufs=1))
         psum = ctx.enter_context(tc.psum_pool(name="psum", bufs=1))
 
         list_a = keep.tile([P, M // 16], U16, name="list_a")
         list_b = keep.tile([P, J // 16], U16, name="list_b")
         table = keep.tile([P, T], I32, name="table", align_bytes=64)
         table_sc = keep.tile([P, T // 4], I32, name="table_sc", align_bytes=64)
-        wa_raw = late.tile([P, R // 2], I32, name="wa_raw", align_bytes=64, offset=2048)
-        wa_sc_raw = keep.tile([P, R // 4], I32, name="wa_sc_raw", align_bytes=64)
-        wa_p = keep.tile([P, R // 2], I32, name="wa_p", align_bytes=64)
-        wb_raw = [late.tile([P, 4, HALF], F32, name=f"wb_raw{b}", align_bytes=64, offset=8192 + 8192 * b) for b in range(PASSES)]
-        wb_q = late.tile([P, R], U32, name="wb_q", align_bytes=64, offset=16384 + 4096)
-        wb_sc = keep.tile([P, R], U8, name="wb_sc", align_bytes=64)
-        rows = keep.tile([P, 2 * P], F32, name="rows")
+        wa_raw = reuse.tile([P, R // 2], I32, name="wa_raw", align_bytes=64, offset=AT_WA)
+        wa_sc_raw = reuse.tile([P, R // 4], I32, name="wa_sc_raw", align_bytes=64, offset=AT_WA_SCALES)
+        wa_codes = keep.tile([P, R // 2], I32, name="wa_codes", align_bytes=64)
+        wb_raw = [reuse.tile([P, 4, HALF], F32, name=f"wb_raw{b}", align_bytes=64, offset=AT_WB[b]) for b in range(PASSES)]
+        wb_codes = reuse.tile([P, R], U32, name="wb_codes", align_bytes=64, offset=AT_WB_CODES)
+        wb_plane = keep.tile([P, R], U8, name="wb_plane", align_bytes=64)
+        factor_rows = keep.tile([P, R // 4], F32, name="factor_rows")
         ident = keep.tile([P, P], F32, name="ident")
-        warm_in = keep.tile([P, 1], F32, name="warm_in")
-        warm_out = keep.tile([P, 1], F32, name="warm_out")
-
-        nc.vector.memset(table_sc[0:ROW0, :], 0)
-        nc.vector.memset(wa_sc_raw[96:ROW0, :], 0)
-        nc.gpsimd.memset(rows[:], 0.0)
         plane_a = keep.tile([P, (M + R) // 4], I32, name="plane_a", align_bytes=64)
         plane_b = keep.tile([P, J // 4], I32, name="plane_b", align_bytes=64)
-        spread_a = keep.tile([P, (M + R) // 4], I32, name="spread_a", align_bytes=64)
+        rows_a = keep.tile([P, (M + R) // 4], I32, name="rows_a", align_bytes=64)
+
+        nc.vector.memset(table_sc[0:ROW0, :], 0)
+        nc.vector.memset(wa_sc_raw[QUAD3:ROW0, :], 0)
+        nc.gpsimd.memset(factor_rows[:], 0.0)
         nc.gpsimd.memset(plane_a[:], 0)
         nc.gpsimd.memset(plane_b[:], 0)
+
         nc.sync.dma_start(table_sc[ROW0:P, :], tab_scales[0].bitcast(I32))
         nc.sync.dma_start(list_a[:], offs)
         nc.sync.dma_start(wa_sc_raw[ROW0:P, :], wa_scales[0].bitcast(I32))
         nc.sync.dma_start(list_b[:], offs2)
         nc.sync.dma_start(table[:], tab_words[0].rearrange("p t i -> p (t i)").bitcast(I32))
         nc.sync.dma_start(wa_raw[:], wa_words[0].bitcast(I32))
-        for side, s in enumerate((sa, sb)):
+        for side, vector in enumerate((sa, sb)):
             nc.sync.dma_start(
-                rows[4 * side : 4 * side + 4, :].rearrange("t (c i) -> t c i", i=8),
-                s.rearrange("(c t i) -> t c i", t=4, i=8),
+                factor_rows[4 * side : 4 * side + 4, :].rearrange("t (c i) -> t c i", i=8),
+                vector.rearrange("(c t i) -> t c i", t=4, i=8),
             )
-        nc.vector.memset(warm_in[:], 0.0)
-        nc.scalar.activation(warm_out[:], warm_in[:], ACT.Gelu_apprx_tanh)
         make_identity(nc, ident[:])
 
         factors = psum.tile([P, PASSES, P], F32, name="factors", tag="factors", bufs=1)
         for b in range(PASSES):
-            nc.tensor.transpose(factors[:, b, :], rows[:, b * P : (b + 1) * P], ident[:])
+            nc.tensor.transpose(factors[:, b, :], factor_rows[:, b * P : (b + 1) * P], ident[:])
 
-        lists = (list_a, list_b)
-        v_words = {}
-        v_sc = {}
+        def carry_rows(queue, plane, rows):
+            for quad in range(4):
+                queue.dma_start(plane[32 * quad : 32 * quad + 4, :], rows[ROW0 + 4 * quad : ROW0 + 4 * quad + 4, :])
 
-        def carry_rows(queue, plane, spread):
-            for q in range(4):
-                queue.dma_start(plane[32 * q : 32 * q + 4, :], spread[ROW0 + 4 * q : ROW0 + 4 * q + 4, :])
+        def gather_scales(offsets, at, name):
+            picked = reuse.tile([P, M], U8, name=name, align_bytes=64, offset=at)
+            nc.vector.tensor_copy(picked[:], table_sc[:].bitcast(U8).indirect(offsets[:]))
+            return picked[:].bitcast(I32)
 
-        def gather_scales(side):
-            picked = late.tile([P, M], U8, name=f"picked{side}", align_bytes=64, offset=0)
-            nc.vector.tensor_copy(picked[:], table_sc[:].bitcast(U8).indirect(lists[side][:]))
-            if side == 0:
-                permute_wa_scales()
-                nc.vector.tensor_copy(spread_a[96:P, 0 : M // 4], picked[:].bitcast(I32)[96:P, :])
-                carry_rows(nc.scalar, plane_a[:], spread_a[:])
-            else:
-                for b in range(PASSES):
-                    nc.sync.dma_start(wb_raw[b][:], wb[:, b * HALF : (b + 1) * HALF].rearrange("(p j) c -> p j c", j=4))
-                carry_rows(nc.sync, plane_b[:], picked[:].bitcast(I32))
-            plane = (plane_a, plane_b)[side]
-            for h in range(2):
-                v_sc[side, h] = plane[:].bitcast(U8)[:, HALF * h : HALF * (h + 1)]
+        def gather_words(words, offsets):
+            nc.vector.tensor_copy(words[:], table[:].bitcast(U32).indirect(offsets))
 
-        def gather_words_a(h):
-            if h == 0:
-                v_words[0, h] = keep.tile([P, HALF], U32, name="v_words00", align_bytes=64)[:]
-            else:
-                v_words[0, h] = late.tile([P, HALF], U32, name="v_words01", align_bytes=64, offset=1024)[:]
-            nc.vector.tensor_copy(v_words[0, h], table[:].bitcast(U32).indirect(list_a[:, 32 * h : 32 * h + 32]))
+        picked_a = gather_scales(list_a, AT_PICKED_A, "picked_a")
+        nc.vector.tensor_copy(
+            rows_a[QUAD3:P, M // 4 :].rearrange("p (b t q i) -> p b t q i", b=PASSES, t=4, i=2),
+            wa_sc_raw[QUAD3:P, :].rearrange("p (b q t i) -> p b t q i", b=PASSES, t=4, i=2),
+        )
+        nc.vector.tensor_copy(rows_a[QUAD3:P, 0 : M // 4], picked_a[QUAD3:P, :])
+        carry_rows(nc.scalar, plane_a[:], rows_a[:])
+        picked_b = gather_scales(list_b, AT_WA_SCALES, "picked_b")
+        for b in range(PASSES):
+            nc.sync.dma_start(wb_raw[b][:], wb[:, b * HALF : (b + 1) * HALF].rearrange("(p j) c -> p j c", j=4))
+        carry_rows(nc.sync, plane_b[:], picked_b)
 
-        def gather_words_b():
-            words = late.tile([P, J], U32, name="v_words1", align_bytes=64, offset=3072)
-            nc.vector.tensor_copy(words[:], table[:].bitcast(U32).indirect(list_b[:]))
-            for h in range(2):
-                v_words[1, h] = words[:, HALF * h : HALF * (h + 1)]
+        ha_plane = keep.tile([P, TILES * UNIT_WORDS], U8, name="ha_plane", align_bytes=64)
+        ha_codes = keep.tile([P, TILES * UNIT_WORDS], U32, name="ha_codes", align_bytes=64)
+        hb_codes = keep.tile([P, TILES * UNIT_WORDS], U32, name="hb_codes", align_bytes=64)
+        hb_plane = keep.tile([P, TILES * UNIT_WORDS], U8, name="hb_plane", align_bytes=64)
+        pairs = [
+            keep.tile([P, 2 * UNIT], BF16, name="pair0", align_bytes=64),
+            reuse.tile([P, 2 * UNIT], BF16, name="pair1", align_bytes=64, offset=AT_PAIR1),
+            keep.tile([P, 2 * UNIT], BF16, name="pair2", align_bytes=64),
+        ]
+        gelus = keep.tile([P, AHEAD + 8, UNIT], F32, name="gelus")
+        factors_sb = keep.tile([P, PASSES, 8], F32, name="factors_sb")
+        nc.scalar.copy(factors_sb[:], factors[:, :, 0:8])
+        result = [keep.tile([P, J], F32, name=f"result{i}") for i in range(TILES)]
 
-        def permute_wa():
+        words_a = [
+            keep.tile([P, HALF], U32, name="words_a0", align_bytes=64),
+            reuse.tile([P, HALF], U32, name="words_a1", align_bytes=64, offset=AT_WORDS_A1),
+        ]
+        words_b = reuse.tile([P, J], U32, name="words_b", align_bytes=64, offset=AT_WORDS_B)
+        gather_words(words_a[0], list_a[:, 0:32])
+        for b in range(PASSES):
+            cols = slice(R // 4 * b, R // 4 * (b + 1))
             nc.vector.tensor_copy(
-                wa_p[:].rearrange("p (b t q i) -> p b t q i", b=2, t=4, i=4),
-                wa_raw[:].rearrange("p (b q t i) -> p b t q i", b=2, t=4, i=4),
+                wa_codes[:, cols].rearrange("p (t q i) -> p t q i", t=4, i=4),
+                wa_raw[:, cols].rearrange("p (q t i) -> p t q i", t=4, i=4),
             )
+        gather_words(words_a[1], list_a[:, 32:64])
+        gather_words(words_b, list_b[:])
 
-        def permute_wa_scales():
-            nc.vector.tensor_copy(
-                spread_a[96:P, M // 4 :].rearrange("p (b t q i) -> p b t q i", b=2, t=4, i=2),
-                wa_sc_raw[96:P, :].rearrange("p (b q t i) -> p b t q i", b=2, t=4, i=2),
-            )
+        def place(first, count=1):
+            c0 = UNIT * (first % 2)
+            return pairs[first // 2][:, c0 : c0 + UNIT * count]
 
-        def round_wb(dst, b):
-            nc.vector.tensor_copy(
-                dst.rearrange("p (t q i j) -> p t q i j", t=4, i=8, j=4),
-                wb_raw[b][:].rearrange("p j (q t i) -> p t q i j", t=4, i=8),
-            )
+        def quantize(codes, plane, word0, src):
+            cols = slice(word0, word0 + src.shape[1] // 4)
+            nc.vector.quantize_mx(codes[:, cols].bitcast(FP8X4), plane[:, cols], src)
 
-        def weights(side, b, t):
-            c = 4 * b + t
-            if side == 0:
-                return (
-                    wa_p[:].bitcast(U8)[:, 256 * c : 256 * (c + 1)].bitcast(FP4X4),
-                    plane_a[:].bitcast(U8)[:, M + P * c : M + P * (c + 1)],
-                )
-            return wb_q[:, P * c : P * (c + 1)].bitcast(FP8X4), wb_sc[:, P * c : P * (c + 1)]
+        def quantize_group(codes, plane, word0):
+            for pair in (1, 0):
+                quantize(codes, plane, word0 + 2 * UNIT_WORDS * pair, place(2 * pair, 2))
 
         def hidden_bank(side, tile, b, dst):
-            h, c0 = divmod(tile * P, HALF)
-            bank = psum.tile([P, 4, P], F32, name="bank", tag="bank", bufs=7)
+            entries = slice(P * tile, P * (tile + 1))
+            if side == 0:
+                half, c0 = divmod(P * tile, HALF)
+                moving, moving_plane = words_a[half][:, c0 : c0 + P], plane_a[:].bitcast(U8)[:, entries]
+            else:
+                moving, moving_plane = words_b[:, entries], plane_b[:].bitcast(U8)[:, entries]
+            bank = psum.tile([P, 4, P], F32, name="bank", tag="bank", bufs=BANKS)
             for t in range(4):
-                w, w_sc = weights(side, b, t)
+                c0 = P * (4 * b + t)
+                if side == 0:
+                    weight = wa_codes[:].bitcast(U8)[:, 2 * c0 : 2 * (c0 + P)].bitcast(FP4X4)
+                    weight_plane = plane_a[:].bitcast(U8)[:, M + c0 : M + c0 + P]
+                else:
+                    weight, weight_plane = wb_codes[:, c0 : c0 + P].bitcast(FP8X4), wb_plane[:, c0 : c0 + P]
                 nc.tensor.matmul_mx(
                     bank[:, t, :],
-                    lhsT=w,
-                    lhsT_scale=w_sc,
-                    rhs=v_words[side, h][:, c0 : c0 + P].bitcast(FP8X4),
-                    rhs_scale=v_sc[side, h][:, c0 : c0 + P],
+                    lhsT=weight,
+                    lhsT_scale=weight_plane,
+                    rhs=moving.bitcast(FP8X4),
+                    rhs_scale=moving_plane,
                     start=True,
                     stop=True,
                 )
             nc.scalar.activation(dst, bank[:].rearrange("p t n -> p n t"), ACT.Gelu_apprx_tanh)
 
-        ha_sc = keep.tile([P, 8 * 2 * P], U8, name="ha_sc", align_bytes=64)
-        ha_q = keep.tile([P, 8 * 2 * P], U32, name="ha_q", align_bytes=64)
-        hb_q = keep.tile([P, 4 * HALF], U32, name="hb_q", align_bytes=64)
-        hb_sc = keep.tile([P, 4 * HALF], U8, name="hb_sc", align_bytes=64)
-
-        pairs = [
-            keep.tile([P, 2048], BF16, name="pair0", align_bytes=64),
-            late.tile([P, 2048], BF16, name="pair1", align_bytes=64, offset=16384),
-            keep.tile([P, 2048], BF16, name="pair2", align_bytes=64),
-        ]
-        gelus = keep.tile([P, 14, 1024], F32, name="gelus")
-        factors_sb = keep.tile([P, PASSES, 8], F32, name="factors_sb")
-        nc.scalar.copy(factors_sb[:], factors[:, :, 0:8])
-
-        def slots(first, count=1):
-            c0 = 1024 * (first % 2)
-            return pairs[first // 2][:, c0 : c0 + 1024 * count]
-
-        def quantize(codes, sc, c0, c1, src):
-            nc.vector.quantize_mx(codes[:, c0:c1].bitcast(FP8X4), sc[:, c0:c1], src)
-
-        def quantize_stage(codes, sc, c0):
-            for n in (1, 0):
-                quantize(codes, sc, c0 + HALF * n, c0 + HALF * (n + 1), slots(2 * n, 2))
-
-        def gelu_a(i):
-            g = gelus[:, (0, 1, 2, 3, 4, 5, 0, 12)[i]].rearrange("p (s n t) -> p s n t", s=2, t=4)
+        def gelu_a(i, buffer):
+            g = gelus[:, buffer].rearrange("p (b n t) -> p b n t", b=PASSES, t=4)
             for b in range(PASSES):
                 hidden_bank(0, i, b, g[:, b])
             return g
 
-        def gelu_b(h, b, u):
-            g = gelus[:, 6 + 4 * h + 2 * b + u].rearrange("p (s n t) -> p s n t", s=2, t=4)
+        def gelu_b(h, n):
+            b, u = divmod(n, 2)
+            g = gelus[:, GELU_B0 + 4 * h + n].rearrange("p (s n t) -> p s n t", s=2, t=4)
             for s in range(2):
                 hidden_bank(1, 4 * h + 2 * u + s, b, g[:, s])
             return g
 
-        def scale_a(g, dst, on_gpsimd=False, n0=0, n1=P):
-            engine, f = (nc.gpsimd, factors_sb) if on_gpsimd else (nc.vector, factors)
+        def scaler(on_gpsimd):
+            return (nc.gpsimd, factors_sb) if on_gpsimd else (nc.vector, factors)
+
+        def scale_a(g, dst, on_gpsimd=False):
+            engine, f = scaler(on_gpsimd)
             engine.tensor_tensor(
-                dst.rearrange("p (b n t) -> p b n t", b=2, t=4)[:, :, n0:n1],
-                g[:, :, n0:n1],
-                f[:, :, 0:4].unsqueeze(2).to_broadcast([P, 2, n1 - n0, 4]),
+                dst.rearrange("p (b n t) -> p b n t", b=PASSES, t=4),
+                g,
+                f[:, :, 0:4].unsqueeze(2).to_broadcast([P, PASSES, P, 4]),
                 ALU.mult,
             )
 
-        def scale_b(g, b, dst, on_gpsimd=False, n0=0, n1=2 * P):
-            engine, f = (nc.gpsimd, factors_sb) if on_gpsimd else (nc.vector, factors)
-            engine.tensor_tensor(
-                dst.rearrange("p (n t) -> p n t", t=4)[:, n0:n1],
-                g.rearrange("p s n t -> p (s n) t")[:, n0:n1],
-                f[:, b, 4:8].unsqueeze(1).to_broadcast([P, n1 - n0, 4]),
-                ALU.mult,
-            )
-
-        outs = {}
-
-        result = [keep.tile([P, J], F32, name=f"result{i}") for i in range(8)]
+        def scale_half_b(h):
+            for n in UNIT_ORDER:
+                engine, f = scaler(n == 0)
+                engine.tensor_tensor(
+                    place(n).rearrange("p (n t) -> p n t", t=4),
+                    gb[h, n].rearrange("p s n t -> p (s n) t"),
+                    f[:, n // 2, 4:8].unsqueeze(1).to_broadcast([P, 2 * P, 4]),
+                    ALU.mult,
+                )
 
         def score(i, h):
-            o = result[i][:, HALF * h : HALF * (h + 1)]
-            outs[i, h] = o
-            bank = psum.tile([P, 4, P], F32, name="bank", tag="bank", bufs=7)
+            bank = psum.tile([P, 4, P], F32, name="bank", tag="bank", bufs=BANKS)
             acc = bank[:].rearrange("p t n -> p (t n)")
             for b in range(PASSES):
-                ca = 2 * P * i + P * b
-                cb = 2 * HALF * h + HALF * b
+                ca = UNIT_WORDS * i + P * b
+                cb = HALF * (PASSES * h + b)
                 nc.tensor.matmul_mx(
                     acc,
-                    lhsT=ha_q[:, ca : ca + P].bitcast(FP8X4),
-                    lhsT_scale=ha_sc[:, ca : ca + P],
-                    rhs=hb_q[:, cb : cb + HALF].bitcast(FP8X4),
-                    rhs_scale=hb_sc[:, cb : cb + HALF],
+                    lhsT=ha_codes[:, ca : ca + P].bitcast(FP8X4),
+                    lhsT_scale=ha_plane[:, ca : ca + P],
+                    rhs=hb_codes[:, cb : cb + HALF].bitcast(FP8X4),
+                    rhs_scale=hb_plane[:, cb : cb + HALF],
                     start=(b == 0),
                     stop=(b == PASSES - 1),
                 )
-            nc.scalar.activation(o, acc, ACT.Tanh, scale=0.00390625)
+            nc.scalar.activation(result[i][:, HALF * h : HALF * (h + 1)], acc, ACT.Tanh, scale=0.00390625)
 
-        def cap(i, h, cap_engine, dst=None):
-            o = outs[i, h]
-            dst = o if dst is None else dst
-            if cap_engine == "gpsimd":
-                nc.gpsimd.tensor_scalar(dst, o, 8.0, 0.0, ALU.mult, ALU.add)
-            elif cap_engine == "scalar":
-                nc.scalar.activation(dst, o, ACT.Copy, scale=8.0)
-            else:
-                nc.vector.tensor_scalar_mul(dst, o, 8.0)
-            nc.sync.dma_start(out[P * i : P * (i + 1), HALF * h : HALF * (h + 1)], dst)
+        def store(i, cols, src):
+            nc.sync.dma_start(out[P * i : P * (i + 1), cols], src)
 
-        gather_scales(0)
-        gather_scales(1)
-        gather_words_a(0)
-        permute_wa()
-        gather_words_a(1)
-        gather_words_b()
-        ga = [gelu_a(i) for i in range(6)]
-        for b, first in ((0, 4), (1, 0)):
-            round_wb(slots(first, 2), b)
-        for b, first in ((0, 4), (1, 0)):
-            quantize(wb_q, wb_sc, HALF * b, HALF * (b + 1), slots(first, 2))
-        gb = {(h, n // 2, n % 2): gelu_b(h, n // 2, n % 2) for h in range(2) for n in GELU_ORDER[h]}
-        scale_a(ga[0], slots(0), on_gpsimd=True)
-        scale_a(ga[1], slots(1), on_gpsimd=True, n1=P // 4)
-        scale_a(ga[2], slots(2))
-        scale_a(ga[3], slots(3))
-        scale_a(ga[1], slots(1), n0=P // 4)
-        quantize_stage(ha_q, ha_sc, 0)
+        def finish_vector(i, h, halves=1):
+            cols = slice(HALF * h, HALF * (h + halves))
+            nc.vector.tensor_scalar_mul(result[i][:, cols], result[i][:, cols], 8.0)
+            store(i, cols, result[i][:, cols])
 
-        def cap_rows(i):
-            nc.vector.tensor_scalar_mul(result[i][:], result[i][:], 8.0)
-            nc.sync.dma_start(out[P * i : P * (i + 1), :], result[i][:])
+        def finish_scalar(i, h):
+            cols = slice(HALF * h, HALF * (h + 1))
+            nc.scalar.activation(result[i][:, cols], result[i][:, cols], ACT.Copy, scale=8.0)
+            store(i, cols, result[i][:, cols])
 
-        def scale_half(h):
-            for n in UNIT_ORDER:
-                b, u = divmod(n, 2)
-                shared = P // 2 if (h, n) == (0, 1) else 0
-                scale_b(gb[h, b, u], b, slots(n), on_gpsimd=(n == 0), n0=shared)
-                if shared:
-                    scale_b(gb[h, b, u], b, slots(n), on_gpsimd=True, n1=shared)
+        def finish_gpsimd(i, h, dst):
+            cols = slice(HALF * h, HALF * (h + 1))
+            nc.gpsimd.tensor_scalar(dst, result[i][:, cols], 8.0, 0.0, ALU.mult, ALU.add)
+            store(i, cols, dst)
 
-        def quantize_a(i, slot):
-            quantize(ha_q, ha_sc, 256 * i, 256 * (i + 1), slots(slot))
+        def quantize_tile(i, at):
+            quantize(ha_codes, ha_plane, UNIT_WORDS * i, place(at))
             for h in range(2):
                 score(i, h)
 
-        scale_half(0)
-        quantize_stage(hb_q, hb_sc, 0)
-        ga.append(gelu_a(6))
+        ga = [gelu_a(i, i) for i in range(AHEAD)]
+        wb_places = (place(4, 2), place(0, 2))
+        for b in range(PASSES):
+            nc.vector.tensor_copy(
+                wb_places[b].rearrange("p (t q i j) -> p t q i j", t=4, i=8, j=4),
+                wb_raw[b][:].rearrange("p j (q t i) -> p t q i j", t=4, i=8),
+            )
+        for b in range(PASSES):
+            quantize(wb_codes, wb_plane, HALF * b, wb_places[b])
+        gb = {(h, n): gelu_b(h, n) for h in range(2) for n in UNIT_ORDER}
+
+        for i in UNIT_ORDER:
+            scale_a(ga[i], place(i), on_gpsimd=(i == 0))
+        quantize_group(ha_codes, ha_plane, 0)
+        scale_half_b(0)
+        quantize_group(hb_codes, hb_plane, 0)
+        ga.append(gelu_a(AHEAD, 0))
         for i in range(EARLY):
             score(i, 0)
-            if i in (1, 2):
-                cap(i, 0, "scalar")
-        scale_half(1)
-        cap(0, 0, "gpsimd")
-        ga.append(gelu_a(7))
-        quantize_stage(hb_q, hb_sc, 1024)
+            if 0 < i < EARLY - 1:
+                finish_scalar(i, 0)
+        scale_half_b(1)
+        finish_gpsimd(0, 0, result[0][:, 0:HALF])
+        ga.append(gelu_a(AHEAD + 1, GELU_B0 + 4 + 2))
+        quantize_group(hb_codes, hb_plane, 2 * HALF)
         for i in range(EARLY):
             score(i, 1)
-        cap(3, 0, "gpsimd", slots(0).bitcast(F32))
-        cap(0, 1, "gpsimd", slots(1).bitcast(F32))
-        scale_a(ga[4], slots(2))
-        scale_a(ga[5], slots(3))
-        quantize_a(4, 2)
-        quantize_a(5, 3)
-        cap(1, 1, "gpsimd", slots(3).bitcast(F32))
-        scale_a(ga[6], slots(4))
-        cap(2, 1, "vector")
-        quantize_a(6, 4)
-        cap(3, 1, "gpsimd", slots(4).bitcast(F32))
-        scale_a(ga[7], slots(5))
-        cap_rows(4)
-        quantize_a(7, 5)
-        cap_rows(5)
-        cap_rows(6)
-        for h in range(2):
-            cap(7, h, "vector")
+
+        finish_gpsimd(3, 0, place(0).bitcast(F32))
+        finish_gpsimd(0, 1, place(1).bitcast(F32))
+        scale_a(ga[4], place(2))
+        scale_a(ga[5], place(3))
+        quantize_tile(4, 2)
+        quantize_tile(5, 3)
+        finish_gpsimd(1, 1, place(3).bitcast(F32))
+        scale_a(ga[6], place(4))
+        finish_vector(2, 1)
+        finish_vector(3, 1)
+        quantize_tile(6, 4)
+        finish_gpsimd(4, 0, place(4).bitcast(F32))
+        scale_a(ga[7], place(5))
+        finish_vector(4, 1)
+        finish_vector(5, 0)
+        quantize_tile(7, 5)
+        finish_vector(5, 1)
+        finish_vector(6, 0, halves=2)
+        finish_vector(7, 0)
+        finish_vector(7, 1)

@@ -25,20 +25,22 @@ UNIT_WORDS = UNIT // 4
 TILES = M // P
 ROW0 = P - 16
 QUAD3 = 96
-UNIT_ORDER = (0, 2, 3, 1)
-EARLY = 4
-AHEAD = 6
-GELU_B0 = AHEAD
-BANKS = 7
+AHEAD = 5
+BANKS = 4
+BANK_BYTES = 2048
+KIB = 1024
 
 AT_WA_SCALES = 0
-AT_WORDS_A1 = 1024
-AT_WA = 2048
-AT_WORDS_B = 3072
-AT_PICKED_A = 7168
-AT_WB = (8192, 16384)
-AT_PAIR1 = AT_WB[1]
-AT_WB_CODES = AT_WB[1] + 4096
+AT_PICKED_A = KIB
+AT_WORDS_A1 = 3 * KIB // 2
+AT_WA = 3 * KIB
+AT_WORDS_B0 = 4 * KIB
+AT_WB = (8 * KIB, 16 * KIB)
+AT_PICKED_B1 = AT_WB[0]
+AT_WORDS_B1 = AT_WB[1]
+AT_STAGE = 24 * KIB
+AT_WB_ROUNDED = (AT_STAGE + 12 * KIB, AT_STAGE + 8 * KIB)
+AT_GELU_B = 48 * KIB
 
 
 def tile_list_biaff_gelu_cap_kernel(
@@ -50,27 +52,32 @@ def tile_list_biaff_gelu_cap_kernel(
         reuse = ctx.enter_context(tc.tile_pool(name="reuse", bufs=1))
         psum = ctx.enter_context(tc.psum_pool(name="psum", bufs=1))
 
+        def placed(shape, dtype, name, at):
+            return reuse.tile(shape, dtype, name=name, align_bytes=64, offset=at)
+
         list_a = keep.tile([P, M // 16], U16, name="list_a")
         list_b = keep.tile([P, J // 16], U16, name="list_b")
         table = keep.tile([P, T], I32, name="table", align_bytes=64)
         table_sc = keep.tile([P, T // 4], I32, name="table_sc", align_bytes=64)
-        wa_raw = reuse.tile([P, R // 2], I32, name="wa_raw", align_bytes=64, offset=AT_WA)
-        wa_sc_raw = reuse.tile([P, R // 4], I32, name="wa_sc_raw", align_bytes=64, offset=AT_WA_SCALES)
+        wa_raw = placed([P, R // 2], I32, "wa_raw", AT_WA)
+        wa_sc_raw = placed([P, R // 4], I32, "wa_sc_raw", AT_WA_SCALES)
         wa_codes = keep.tile([P, R // 2], I32, name="wa_codes", align_bytes=64)
-        wb_raw = [reuse.tile([P, 4, HALF], F32, name=f"wb_raw{b}", align_bytes=64, offset=AT_WB[b]) for b in range(PASSES)]
-        wb_codes = reuse.tile([P, R], U32, name="wb_codes", align_bytes=64, offset=AT_WB_CODES)
+        wb_raw = [placed([P, 4, HALF], F32, f"wb_raw{b}", AT_WB[b]) for b in range(PASSES)]
+        wb_rounded = [placed([P, 4 * HALF], BF16, f"wb_rounded{b}", AT_WB_ROUNDED[b]) for b in range(PASSES)]
+        wb_codes = keep.tile([P, R], U32, name="wb_codes", align_bytes=64)
         wb_plane = keep.tile([P, R], U8, name="wb_plane", align_bytes=64)
         factor_rows = keep.tile([P, R // 4], F32, name="factor_rows")
         ident = keep.tile([P, P], F32, name="ident")
         plane_a = keep.tile([P, (M + R) // 4], I32, name="plane_a", align_bytes=64)
-        plane_b = keep.tile([P, J // 4], I32, name="plane_b", align_bytes=64)
+        plane_b = [keep.tile([P, HALF // 4], I32, name=f"plane_b{h}", align_bytes=64) for h in range(2)]
         rows_a = keep.tile([P, (M + R) // 4], I32, name="rows_a", align_bytes=64)
 
         nc.vector.memset(table_sc[0:ROW0, :], 0)
         nc.vector.memset(wa_sc_raw[QUAD3:ROW0, :], 0)
         nc.gpsimd.memset(factor_rows[:], 0.0)
         nc.gpsimd.memset(plane_a[:], 0)
-        nc.gpsimd.memset(plane_b[:], 0)
+        for h in range(2):
+            nc.gpsimd.memset(plane_b[h][:], 0)
 
         nc.sync.dma_start(table_sc[ROW0:P, :], tab_scales[0].bitcast(I32))
         nc.sync.dma_start(list_a[:], offs)
@@ -83,55 +90,41 @@ def tile_list_biaff_gelu_cap_kernel(
                 factor_rows[4 * side : 4 * side + 4, :].rearrange("t (c i) -> t c i", i=8),
                 vector.rearrange("(c t i) -> t c i", t=4, i=8),
             )
-        make_identity(nc, ident[:])
-
-        factors = psum.tile([P, PASSES, P], F32, name="factors", tag="factors", bufs=1)
         for b in range(PASSES):
-            nc.tensor.transpose(factors[:, b, :], factor_rows[:, b * P : (b + 1) * P], ident[:])
+            nc.sync.dma_start(wb_raw[b][:], wb[:, b * HALF : (b + 1) * HALF].rearrange("(p j) c -> p j c", j=4))
+        make_identity(nc, ident[:])
 
         def carry_rows(queue, plane, rows):
             for quad in range(4):
                 queue.dma_start(plane[32 * quad : 32 * quad + 4, :], rows[ROW0 + 4 * quad : ROW0 + 4 * quad + 4, :])
 
-        def gather_scales(offsets, at, name):
-            picked = reuse.tile([P, M], U8, name=name, align_bytes=64, offset=at)
-            nc.vector.tensor_copy(picked[:], table_sc[:].bitcast(U8).indirect(offsets[:]))
+        def gather_scales(offsets, count, at, name):
+            picked = placed([P, count], U8, name, at)
+            nc.vector.tensor_copy(picked[:], table_sc[:].bitcast(U8).indirect(offsets))
             return picked[:].bitcast(I32)
 
         def gather_words(words, offsets):
             nc.vector.tensor_copy(words[:], table[:].bitcast(U32).indirect(offsets))
 
-        picked_a = gather_scales(list_a, AT_PICKED_A, "picked_a")
+        picked_a = gather_scales(list_a[:], M, AT_PICKED_A, "picked_a")
         nc.vector.tensor_copy(
             rows_a[QUAD3:P, M // 4 :].rearrange("p (b t q i) -> p b t q i", b=PASSES, t=4, i=2),
             wa_sc_raw[QUAD3:P, :].rearrange("p (b q t i) -> p b t q i", b=PASSES, t=4, i=2),
         )
         nc.vector.tensor_copy(rows_a[QUAD3:P, 0 : M // 4], picked_a[QUAD3:P, :])
         carry_rows(nc.scalar, plane_a[:], rows_a[:])
-        picked_b = gather_scales(list_b, AT_WA_SCALES, "picked_b")
-        for b in range(PASSES):
-            nc.sync.dma_start(wb_raw[b][:], wb[:, b * HALF : (b + 1) * HALF].rearrange("(p j) c -> p j c", j=4))
-        carry_rows(nc.sync, plane_b[:], picked_b)
+        carry_rows(nc.sync, plane_b[0][:], gather_scales(list_b[:, 0:32], HALF, AT_WA_SCALES, "picked_b0"))
 
-        ha_plane = keep.tile([P, TILES * UNIT_WORDS], U8, name="ha_plane", align_bytes=64)
         ha_codes = keep.tile([P, TILES * UNIT_WORDS], U32, name="ha_codes", align_bytes=64)
         hb_codes = keep.tile([P, TILES * UNIT_WORDS], U32, name="hb_codes", align_bytes=64)
-        hb_plane = keep.tile([P, TILES * UNIT_WORDS], U8, name="hb_plane", align_bytes=64)
-        pairs = [
-            keep.tile([P, 2 * UNIT], BF16, name="pair0", align_bytes=64),
-            reuse.tile([P, 2 * UNIT], BF16, name="pair1", align_bytes=64, offset=AT_PAIR1),
-            keep.tile([P, 2 * UNIT], BF16, name="pair2", align_bytes=64),
-        ]
-        gelus = keep.tile([P, AHEAD + 8, UNIT], F32, name="gelus")
         factors_sb = keep.tile([P, PASSES, 8], F32, name="factors_sb")
-        nc.scalar.copy(factors_sb[:], factors[:, :, 0:8])
         result = [keep.tile([P, J], F32, name=f"result{i}") for i in range(TILES)]
 
         words_a = [
             keep.tile([P, HALF], U32, name="words_a0", align_bytes=64),
-            reuse.tile([P, HALF], U32, name="words_a1", align_bytes=64, offset=AT_WORDS_A1),
+            placed([P, HALF], U32, "words_a1", AT_WORDS_A1),
         ]
-        words_b = reuse.tile([P, J], U32, name="words_b", align_bytes=64, offset=AT_WORDS_B)
+        words_b = [placed([P, HALF], U32, f"words_b{h}", at) for h, at in enumerate((AT_WORDS_B0, AT_WORDS_B1))]
         gather_words(words_a[0], list_a[:, 0:32])
         for b in range(PASSES):
             cols = slice(R // 4 * b, R // 4 * (b + 1))
@@ -140,28 +133,20 @@ def tile_list_biaff_gelu_cap_kernel(
                 wa_raw[:, cols].rearrange("p (q t i) -> p t q i", t=4, i=4),
             )
         gather_words(words_a[1], list_a[:, 32:64])
-        gather_words(words_b, list_b[:])
+        gather_words(words_b[0], list_b[:, 0:32])
 
-        def place(first, count=1):
-            c0 = UNIT * (first % 2)
-            return pairs[first // 2][:, c0 : c0 + UNIT * count]
+        def quantize(codes, plane, src):
+            nc.vector.quantize_mx(codes.bitcast(FP8X4), plane, src)
 
-        def quantize(codes, plane, word0, src):
-            cols = slice(word0, word0 + src.shape[1] // 4)
-            nc.vector.quantize_mx(codes[:, cols].bitcast(FP8X4), plane[:, cols], src)
+        def next_bank():
+            return psum.tile([P, 4, P], F32, name="bank", tag="bank", bufs=BANKS, offset=0)
 
-        def quantize_group(codes, plane, word0):
-            for pair in (1, 0):
-                quantize(codes, plane, word0 + 2 * UNIT_WORDS * pair, place(2 * pair, 2))
-
-        def hidden_bank(side, tile, b, dst):
-            entries = slice(P * tile, P * (tile + 1))
+        def hidden_bank(side, tile, b, dst, bank):
+            half, c0 = divmod(P * tile, HALF)
             if side == 0:
-                half, c0 = divmod(P * tile, HALF)
-                moving, moving_plane = words_a[half][:, c0 : c0 + P], plane_a[:].bitcast(U8)[:, entries]
+                moving, moving_plane = words_a[half][:, c0 : c0 + P], plane_a[:].bitcast(U8)[:, P * tile : P * (tile + 1)]
             else:
-                moving, moving_plane = words_b[:, entries], plane_b[:].bitcast(U8)[:, entries]
-            bank = psum.tile([P, 4, P], F32, name="bank", tag="bank", bufs=BANKS)
+                moving, moving_plane = words_b[half][:, c0 : c0 + P], plane_b[half][:].bitcast(U8)[:, c0 : c0 + P]
             for t in range(4):
                 c0 = P * (4 * b + t)
                 if side == 0:
@@ -180,53 +165,47 @@ def tile_list_biaff_gelu_cap_kernel(
                 )
             nc.scalar.activation(dst, bank[:].rearrange("p t n -> p n t"), ACT.Gelu_apprx_tanh)
 
-        def gelu_a(i, buffer):
-            g = gelus[:, buffer].rearrange("p (b n t) -> p b n t", b=PASSES, t=4)
-            for b in range(PASSES):
-                hidden_bank(0, i, b, g[:, b])
-            return g
+        def gelu_a(i, g, first_bank=None, passes=range(PASSES)):
+            for b in passes:
+                hidden_bank(0, i, b, g[:, b], first_bank if (first_bank is not None and b == 0) else next_bank())
+
+        def as_passes(ap):
+            return ap.rearrange("p (b n t) -> p b n t", b=PASSES, t=4)
+
+        def at_gelu_b(h, n):
+            return AT_GELU_B + 4 * KIB * (4 * h + n)
 
         def gelu_b(h, n):
             b, u = divmod(n, 2)
-            g = gelus[:, GELU_B0 + 4 * h + n].rearrange("p (s n t) -> p s n t", s=2, t=4)
+            g = placed([P, UNIT], F32, f"gelu_b{h}{n}", at_gelu_b(h, n))[:].rearrange("p (s n t) -> p s n t", s=2, t=4)
             for s in range(2):
-                hidden_bank(1, 4 * h + 2 * u + s, b, g[:, s])
+                hidden_bank(1, 4 * h + 2 * u + s, b, g[:, s], next_bank())
             return g
 
-        def scaler(on_gpsimd):
-            return (nc.gpsimd, factors_sb) if on_gpsimd else (nc.vector, factors)
-
-        def scale_a(g, dst, on_gpsimd=False):
-            engine, f = scaler(on_gpsimd)
+        def scale_a(on_gpsimd, g, dst):
+            engine, f = (nc.gpsimd, factors_sb) if on_gpsimd else (nc.vector, factors)
             engine.tensor_tensor(
-                dst.rearrange("p (b n t) -> p b n t", b=PASSES, t=4),
-                g,
-                f[:, :, 0:4].unsqueeze(2).to_broadcast([P, PASSES, P, 4]),
+                as_passes(dst), g, f[:, :, 0:4].unsqueeze(2).to_broadcast([P, PASSES, g.shape[2], 4]), ALU.mult
+            )
+
+        def scale_b(h, n, dst):
+            nc.vector.tensor_tensor(
+                dst.rearrange("p (n t) -> p n t", t=4),
+                gb[h, n].rearrange("p s n t -> p (s n) t"),
+                factors[:, n // 2, 4:8].unsqueeze(1).to_broadcast([P, 2 * P, 4]),
                 ALU.mult,
             )
 
-        def scale_half_b(h):
-            for n in UNIT_ORDER:
-                engine, f = scaler(n == 0)
-                engine.tensor_tensor(
-                    place(n).rearrange("p (n t) -> p n t", t=4),
-                    gb[h, n].rearrange("p s n t -> p (s n) t"),
-                    f[:, n // 2, 4:8].unsqueeze(1).to_broadcast([P, 2 * P, 4]),
-                    ALU.mult,
-                )
-
         def score(i, h):
-            bank = psum.tile([P, 4, P], F32, name="bank", tag="bank", bufs=BANKS)
-            acc = bank[:].rearrange("p t n -> p (t n)")
+            acc = next_bank()[:].rearrange("p t n -> p (t n)")
             for b in range(PASSES):
-                ca = UNIT_WORDS * i + P * b
                 cb = HALF * (PASSES * h + b)
                 nc.tensor.matmul_mx(
                     acc,
-                    lhsT=ha_codes[:, ca : ca + P].bitcast(FP8X4),
-                    lhsT_scale=ha_plane[:, ca : ca + P],
+                    lhsT=ha[i][0][:, b].bitcast(FP8X4),
+                    lhsT_scale=ha[i][1][:, b],
                     rhs=hb_codes[:, cb : cb + HALF].bitcast(FP8X4),
-                    rhs_scale=hb_plane[:, cb : cb + HALF],
+                    rhs_scale=hb_plane[h][:, HALF * b : HALF * (b + 1)],
                     start=(b == 0),
                     stop=(b == PASSES - 1),
                 )
@@ -235,8 +214,8 @@ def tile_list_biaff_gelu_cap_kernel(
         def store(i, cols, src):
             nc.sync.dma_start(out[P * i : P * (i + 1), cols], src)
 
-        def finish_vector(i, h, halves=1):
-            cols = slice(HALF * h, HALF * (h + halves))
+        def finish_vector(i, h):
+            cols = slice(HALF * h, HALF * (h + 1))
             nc.vector.tensor_scalar_mul(result[i][:, cols], result[i][:, cols], 8.0)
             store(i, cols, result[i][:, cols])
 
@@ -245,61 +224,117 @@ def tile_list_biaff_gelu_cap_kernel(
             nc.scalar.activation(result[i][:, cols], result[i][:, cols], ACT.Copy, scale=8.0)
             store(i, cols, result[i][:, cols])
 
-        def finish_gpsimd(i, h, dst):
+        def finish_gpsimd(i, h, at=None):
             cols = slice(HALF * h, HALF * (h + 1))
+            dst = result[i][:, cols] if at is None else placed([P, HALF], F32, f"times8_{i}{h}", at)[:]
             nc.gpsimd.tensor_scalar(dst, result[i][:, cols], 8.0, 0.0, ALU.mult, ALU.add)
             store(i, cols, dst)
 
-        def quantize_tile(i, at):
-            quantize(ha_codes, ha_plane, UNIT_WORDS * i, place(at))
+        def staged(name, kib, units=2):
+            return placed([P, units * UNIT], BF16, name, AT_STAGE + kib * KIB)
+
+        def unit(stage, n):
+            return stage[:, UNIT * n : UNIT * (n + 1)]
+
+        ha = {}
+        hb_plane = {}
+
+        def quantize_a(i, tiles, src, at):
+            plane = placed([P, tiles * UNIT_WORDS], U8, f"ha_plane{i}", at)
+            codes = ha_codes[:, UNIT_WORDS * i : UNIT_WORDS * (i + tiles)]
+            quantize(codes, plane[:], src)
+            for n in range(tiles):
+                ha[i + n] = [x.rearrange("p (b s c) -> p b s c", b=PASSES, s=tiles)[:, :, n, :] for x in (codes, plane[:])]
+
+        def quantize_b(h, stages, at):
+            hb_plane[h] = placed([P, PASSES * HALF], U8, f"hb_plane{h}", at)
+            for b in range(PASSES):
+                c0 = HALF * (PASSES * h + b)
+                quantize(hb_codes[:, c0 : c0 + HALF], hb_plane[h][:, HALF * b : HALF * (b + 1)], stages[b][:])
+
+        at_last_bank = BANKS * BANK_BYTES
+        pair01 = as_passes(keep.tile([P, 2 * UNIT], F32, name="gelu_a01")[:])
+        pair23 = as_passes(keep.tile([P, 2 * UNIT], F32, name="gelu_a23")[:])
+        ga = {0: pair01[:, :, 0:P], 1: pair01[:, :, P : 2 * P], 2: pair23[:, :, 0:P], 3: pair23[:, :, P : 2 * P]}
+        ga.update({i: as_passes(keep.tile([P, UNIT], F32, name=f"gelu_a{i}")[:]) for i in range(4, AHEAD)})
+        gelu_a(0, ga[0], psum.tile([P, 4, P], F32, name="first", offset=at_last_bank))
+        factors = psum.tile([P, PASSES, P], F32, name="factors", offset=at_last_bank)
+        gelu_a(1, ga[1])
+        for b in range(PASSES):
+            nc.tensor.transpose(factors[:, b, :], factor_rows[:, b * P : (b + 1) * P], ident[:])
+        gelu_a(2, ga[2])
+        nc.scalar.copy(factors_sb[:], factors[:, :, 0:8])
+        for i in range(3, AHEAD):
+            gelu_a(i, ga[i])
+
+        for b in range(PASSES):
+            nc.vector.tensor_copy(
+                wb_rounded[b][:].rearrange("p (t q i j) -> p t q i j", t=4, i=8, j=4),
+                wb_raw[b][:].rearrange("p j (q t i) -> p t q i j", t=4, i=8),
+            )
+            if b == 0:
+                carry_rows(nc.sync, plane_b[1][:], gather_scales(list_b[:, 32:64], HALF, AT_PICKED_B1, "picked_b1"))
+            else:
+                gather_words(words_b[1], list_b[:, 32:64])
+            cols = slice(HALF * b, HALF * (b + 1))
+            quantize(wb_codes[:, cols], wb_plane[:, cols], wb_rounded[b][:])
+        gb = {(h, n): gelu_b(h, n) for h in range(2) for n in range(4)}
+
+        stage_b = [staged("stage_b00", 0), staged("stage_b01", 4)]
+        stage_01 = staged("stage_a01", 8)
+        scale_a(True, pair01, stage_01[:])
+        for n in range(4):
+            scale_b(0, n, unit(stage_b[n // 2], n % 2))
+        quantize_b(0, stage_b, at_gelu_b(0, 2))
+        quantize_a(0, 2, stage_01[:], at_gelu_b(0, 2) + KIB)
+        for i in range(AHEAD, TILES):
+            ga[i] = as_passes(placed([P, UNIT], F32, f"gelu_a{i}", at_gelu_b(0, 3) + 4 * KIB * (i - AHEAD))[:])
+        score(0, 0)
+        score(1, 0)
+        finish_scalar(0, 0)
+        gelu_a(5, ga[5])
+        gelu_a(6, ga[6])
+        gelu_a(7, ga[7])
+
+        stage_b = [staged("stage_b10", 4), staged("stage_b11", 0)]
+        stage_23 = staged("stage_a23", 8)
+        scale_a(True, pair23, stage_23[:])
+        for n in range(4):
+            scale_b(1, n, unit(stage_b[n // 2], n % 2))
+        finish_vector(1, 0)
+        quantize_a(2, 2, stage_23[:], at_gelu_b(1, 2) + KIB)
+        for i in range(2, 4):
+            score(i, 0)
+        quantize_b(1, stage_b, at_gelu_b(1, 2))
+        for i in range(4):
+            score(i, 1)
+
+        def late_tile(i, src):
+            quantize_a(i, 1, src, at_gelu_b(0, 0) + UNIT_WORDS * i)
             for h in range(2):
                 score(i, h)
 
-        ga = [gelu_a(i, i) for i in range(AHEAD)]
-        wb_places = (place(4, 2), place(0, 2))
-        for b in range(PASSES):
-            nc.vector.tensor_copy(
-                wb_places[b].rearrange("p (t q i j) -> p t q i j", t=4, i=8, j=4),
-                wb_raw[b][:].rearrange("p j (q t i) -> p t q i j", t=4, i=8),
-            )
-        for b in range(PASSES):
-            quantize(wb_codes, wb_plane, HALF * b, wb_places[b])
-        gb = {(h, n): gelu_b(h, n) for h in range(2) for n in UNIT_ORDER}
-
-        for i in UNIT_ORDER:
-            scale_a(ga[i], place(i), on_gpsimd=(i == 0))
-        quantize_group(ha_codes, ha_plane, 0)
-        scale_half_b(0)
-        quantize_group(hb_codes, hb_plane, 0)
-        ga.append(gelu_a(AHEAD, 0))
-        for i in range(EARLY):
-            score(i, 0)
-            if 0 < i < EARLY - 1:
-                finish_scalar(i, 0)
-        scale_half_b(1)
-        finish_gpsimd(0, 0, result[0][:, 0:HALF])
-        ga.append(gelu_a(AHEAD + 1, GELU_B0 + 4 + 2))
-        quantize_group(hb_codes, hb_plane, 2 * HALF)
-        for i in range(EARLY):
-            score(i, 1)
-
-        finish_gpsimd(3, 0, place(0).bitcast(F32))
-        finish_gpsimd(0, 1, place(1).bitcast(F32))
-        scale_a(ga[4], place(2))
-        scale_a(ga[5], place(3))
-        quantize_tile(4, 2)
-        quantize_tile(5, 3)
-        finish_gpsimd(1, 1, place(3).bitcast(F32))
-        scale_a(ga[6], place(4))
-        finish_vector(2, 1)
+        stage_45 = staged("stage_a45", 4)
+        finish_gpsimd(2, 0, AT_STAGE)
+        finish_gpsimd(3, 0)
+        finish_gpsimd(0, 1)
+        for n in range(2):
+            scale_a(False, ga[4 + n], unit(stage_45, n))
+        for n in range(2):
+            late_tile(4 + n, unit(stage_45, n))
+        finish_vector(1, 1)
+        stage_6 = staged("stage_a6", 7, units=1)
+        finish_gpsimd(2, 1, AT_STAGE + 4 * KIB)
+        scale_a(False, ga[6], stage_6[:])
         finish_vector(3, 1)
-        quantize_tile(6, 4)
-        finish_gpsimd(4, 0, place(4).bitcast(F32))
-        scale_a(ga[7], place(5))
-        finish_vector(4, 1)
+        late_tile(6, stage_6[:])
+        finish_vector(4, 0)
+        stage_7 = staged("stage_a7", 6, units=1)
+        finish_gpsimd(4, 1, AT_STAGE + 8 * KIB)
+        scale_a(False, ga[7], stage_7[:])
         finish_vector(5, 0)
-        quantize_tile(7, 5)
+        late_tile(7, stage_7[:])
         finish_vector(5, 1)
-        finish_vector(6, 0, halves=2)
-        finish_vector(7, 0)
-        finish_vector(7, 1)
+        for i in range(6, 8):
+            for h in range(2):
+                finish_vector(i, h)

@@ -25,8 +25,9 @@ UNIT_WORDS = UNIT // 4
 TILES = M // P
 ROW0 = P - 16
 QUAD3 = 96
-AHEAD = 5
+AHEAD = 6
 BANKS = 4
+EXTRA = 128
 BANK_BYTES = 2048
 KIB = 1024
 
@@ -34,12 +35,13 @@ AT_WA_SCALES = 0
 AT_PICKED_A = KIB
 AT_WORDS_A1 = 3 * KIB // 2
 AT_WA = 3 * KIB
-AT_WORDS_B0 = 4 * KIB
+AT_PICKED_B1 = 7 * KIB // 2
+AT_WORDS_B = 4 * KIB
 AT_WB = (8 * KIB, 16 * KIB)
-AT_PICKED_B1 = AT_WB[0]
-AT_WORDS_B1 = AT_WB[1]
+AT_WB_CODES = AT_WB[1]
 AT_STAGE = 24 * KIB
 AT_WB_ROUNDED = (AT_STAGE + 12 * KIB, AT_STAGE + 8 * KIB)
+AT_GELU_A = 80 * KIB
 AT_GELU_B = 48 * KIB
 
 
@@ -64,18 +66,16 @@ def tile_list_biaff_gelu_cap_kernel(
         wa_codes = keep.tile([P, R // 2], I32, name="wa_codes", align_bytes=64)
         wb_raw = [placed([P, 4, HALF], F32, f"wb_raw{b}", AT_WB[b]) for b in range(PASSES)]
         wb_rounded = [placed([P, 4 * HALF], BF16, f"wb_rounded{b}", AT_WB_ROUNDED[b]) for b in range(PASSES)]
-        wb_codes = keep.tile([P, R], U32, name="wb_codes", align_bytes=64)
+        wb_codes = placed([P, R], U32, "wb_codes", AT_WB_CODES)
         wb_plane = keep.tile([P, R], U8, name="wb_plane", align_bytes=64)
         factor_rows = keep.tile([P, R // 4], F32, name="factor_rows")
         ident = keep.tile([P, P], F32, name="ident")
         plane_a = keep.tile([P, (M + R) // 4], I32, name="plane_a", align_bytes=64)
         plane_b = [keep.tile([P, HALF // 4], I32, name=f"plane_b{h}", align_bytes=64) for h in range(2)]
-        rows_a = keep.tile([P, (M + R) // 4], I32, name="rows_a", align_bytes=64)
 
         nc.vector.memset(table_sc[0:ROW0, :], 0)
-        nc.vector.memset(wa_sc_raw[QUAD3:ROW0, :], 0)
+        nc.vector.memset(wa_sc_raw[0:ROW0, :], 0)
         nc.gpsimd.memset(factor_rows[:], 0.0)
-        nc.gpsimd.memset(plane_a[:], 0)
         for h in range(2):
             nc.gpsimd.memset(plane_b[h][:], 0)
 
@@ -108,11 +108,11 @@ def tile_list_biaff_gelu_cap_kernel(
 
         picked_a = gather_scales(list_a[:], M, AT_PICKED_A, "picked_a")
         nc.vector.tensor_copy(
-            rows_a[QUAD3:P, M // 4 :].rearrange("p (b t q i) -> p b t q i", b=PASSES, t=4, i=2),
-            wa_sc_raw[QUAD3:P, :].rearrange("p (b q t i) -> p b t q i", b=PASSES, t=4, i=2),
+            plane_a[:, M // 4 :].rearrange("p (b t q i) -> p b t q i", b=PASSES, t=4, i=2),
+            wa_sc_raw[:].rearrange("p (b q t i) -> p b t q i", b=PASSES, t=4, i=2),
         )
-        nc.vector.tensor_copy(rows_a[QUAD3:P, 0 : M // 4], picked_a[QUAD3:P, :])
-        carry_rows(nc.scalar, plane_a[:], rows_a[:])
+        nc.vector.tensor_copy(plane_a[:, 0 : M // 4], picked_a)
+        carry_rows(nc.scalar, plane_a[:], plane_a[:])
         carry_rows(nc.sync, plane_b[0][:], gather_scales(list_b[:, 0:32], HALF, AT_WA_SCALES, "picked_b0"))
 
         ha_codes = keep.tile([P, TILES * UNIT_WORDS], U32, name="ha_codes", align_bytes=64)
@@ -124,7 +124,7 @@ def tile_list_biaff_gelu_cap_kernel(
             keep.tile([P, HALF], U32, name="words_a0", align_bytes=64),
             placed([P, HALF], U32, "words_a1", AT_WORDS_A1),
         ]
-        words_b = [placed([P, HALF], U32, f"words_b{h}", at) for h, at in enumerate((AT_WORDS_B0, AT_WORDS_B1))]
+        words_b = placed([P, J], U32, "words_b", AT_WORDS_B)
         gather_words(words_a[0], list_a[:, 0:32])
         for b in range(PASSES):
             cols = slice(R // 4 * b, R // 4 * (b + 1))
@@ -133,7 +133,8 @@ def tile_list_biaff_gelu_cap_kernel(
                 wa_raw[:, cols].rearrange("p (q t i) -> p t q i", t=4, i=4),
             )
         gather_words(words_a[1], list_a[:, 32:64])
-        gather_words(words_b[0], list_b[:, 0:32])
+        carry_rows(nc.sync, plane_b[1][:], gather_scales(list_b[:, 32:64], HALF, AT_PICKED_B1, "picked_b1"))
+        gather_words(words_b, list_b[:])
 
         def quantize(codes, plane, src):
             nc.vector.quantize_mx(codes.bitcast(FP8X4), plane, src)
@@ -146,7 +147,7 @@ def tile_list_biaff_gelu_cap_kernel(
             if side == 0:
                 moving, moving_plane = words_a[half][:, c0 : c0 + P], plane_a[:].bitcast(U8)[:, P * tile : P * (tile + 1)]
             else:
-                moving, moving_plane = words_b[half][:, c0 : c0 + P], plane_b[half][:].bitcast(U8)[:, c0 : c0 + P]
+                moving, moving_plane = words_b[:, P * tile : P * (tile + 1)], plane_b[half][:].bitcast(U8)[:, c0 : c0 + P]
             for t in range(4):
                 c0 = P * (4 * b + t)
                 if side == 0:
@@ -175,26 +176,32 @@ def tile_list_biaff_gelu_cap_kernel(
         def at_gelu_b(h, n):
             return AT_GELU_B + 4 * KIB * (4 * h + n)
 
-        def gelu_b(h, n):
-            b, u = divmod(n, 2)
-            g = placed([P, UNIT], F32, f"gelu_b{h}{n}", at_gelu_b(h, n))[:].rearrange("p (s n t) -> p s n t", s=2, t=4)
-            for s in range(2):
-                hidden_bank(1, 4 * h + 2 * u + s, b, g[:, s], next_bank())
-            return g
+        def gelu_b(h):
+            buffers = [
+                placed([P, UNIT * units], F32, f"gelu_b{h}{n}", at_gelu_b(h, n))[:].rearrange("p (n t) -> p n t", t=4)
+                for n, units in ((0, 2), (2, 1), (3, 1))
+            ]
+            for s in range(4):
+                hidden_bank(1, 4 * h + s, 0, buffers[0][:, P * s : P * (s + 1)], next_bank())
+            for s in range(4):
+                hidden_bank(1, 4 * h + s, 1, buffers[1 + s // 2][:, P * (s % 2) : P * (s % 2 + 1)], next_bank())
+            return buffers
 
         def scale_a(on_gpsimd, g, dst):
             engine, f = (nc.gpsimd, factors_sb) if on_gpsimd else (nc.vector, factors)
-            engine.tensor_tensor(
-                as_passes(dst), g, f[:, :, 0:4].unsqueeze(2).to_broadcast([P, PASSES, g.shape[2], 4]), ALU.mult
-            )
+            engine.tensor_tensor(dst, g, f[:, :, 0:4].unsqueeze(2).to_broadcast([P, PASSES, g.shape[2], 4]), ALU.mult)
 
-        def scale_b(h, n, dst):
-            nc.vector.tensor_tensor(
-                dst.rearrange("p (n t) -> p n t", t=4),
-                gb[h, n].rearrange("p s n t -> p (s n) t"),
-                factors[:, n // 2, 4:8].unsqueeze(1).to_broadcast([P, 2 * P, 4]),
-                ALU.mult,
-            )
+        def scale_b(on_gpsimd, b, g, dst):
+            engine, f = (nc.gpsimd, factors_sb) if on_gpsimd else (nc.vector, factors)
+            engine.tensor_tensor(dst, g, f[:, b, 4:8].unsqueeze(1).to_broadcast([P, g.shape[1], 4]), ALU.mult)
+
+        def scale_half_b(h, stages, extra):
+            cut = (UNIT + extra) // 4
+            dst = [s[:].rearrange("p (n t) -> p n t", t=4) for s in stages]
+            scale_b(True, 0, gb[h][0][:, 0:cut], dst[0][:, 0:cut])
+            scale_b(False, 1, gb[h][1], dst[1][:, 0 : 2 * P])
+            scale_b(False, 0, gb[h][0][:, cut:], dst[0][:, cut:])
+            scale_b(False, 1, gb[h][2], dst[1][:, 2 * P :])
 
         def score(i, h):
             acc = next_bank()[:].rearrange("p t n -> p (t n)")
@@ -254,9 +261,8 @@ def tile_list_biaff_gelu_cap_kernel(
 
         at_last_bank = BANKS * BANK_BYTES
         pair01 = as_passes(keep.tile([P, 2 * UNIT], F32, name="gelu_a01")[:])
-        pair23 = as_passes(keep.tile([P, 2 * UNIT], F32, name="gelu_a23")[:])
-        ga = {0: pair01[:, :, 0:P], 1: pair01[:, :, P : 2 * P], 2: pair23[:, :, 0:P], 3: pair23[:, :, P : 2 * P]}
-        ga.update({i: as_passes(keep.tile([P, UNIT], F32, name=f"gelu_a{i}")[:]) for i in range(4, AHEAD)})
+        ga = {0: pair01[:, :, 0:P], 1: pair01[:, :, P : 2 * P]}
+        ga.update({i: as_passes(placed([P, UNIT], F32, f"gelu_a{i}", AT_GELU_A + 4 * KIB * (i - 2))[:]) for i in range(2, AHEAD)})
         gelu_a(0, ga[0], psum.tile([P, 4, P], F32, name="first", offset=at_last_bank))
         factors = psum.tile([P, PASSES, P], F32, name="factors", offset=at_last_bank)
         gelu_a(1, ga[1])
@@ -272,39 +278,38 @@ def tile_list_biaff_gelu_cap_kernel(
                 wb_rounded[b][:].rearrange("p (t q i j) -> p t q i j", t=4, i=8, j=4),
                 wb_raw[b][:].rearrange("p j (q t i) -> p t q i j", t=4, i=8),
             )
-            if b == 0:
-                carry_rows(nc.sync, plane_b[1][:], gather_scales(list_b[:, 32:64], HALF, AT_PICKED_B1, "picked_b1"))
-            else:
-                gather_words(words_b[1], list_b[:, 32:64])
+        for b in range(PASSES):
             cols = slice(HALF * b, HALF * (b + 1))
             quantize(wb_codes[:, cols], wb_plane[:, cols], wb_rounded[b][:])
-        gb = {(h, n): gelu_b(h, n) for h in range(2) for n in range(4)}
+        gb = [gelu_b(h) for h in range(2)]
 
-        stage_b = [staged("stage_b00", 0), staged("stage_b01", 4)]
-        stage_01 = staged("stage_a01", 8)
-        scale_a(True, pair01, stage_01[:])
-        for n in range(4):
-            scale_b(0, n, unit(stage_b[n // 2], n % 2))
+        stage_01 = staged("stage_a01", 6)
+        stage_23 = staged("stage_a23", 12)
+        cut = P + EXTRA // 8
+        scale_a(True, pair01[:, :, 0:cut], as_passes(stage_01[:])[:, :, 0:cut])
+        scale_a(False, ga[2], as_passes(stage_23[:])[:, :, 0:P])
+        scale_a(False, pair01[:, :, cut:], as_passes(stage_01[:])[:, :, cut:])
+        scale_a(False, ga[3], as_passes(stage_23[:])[:, :, P:])
+        quantize_a(0, 2, stage_01[:], AT_GELU_A)
+        quantize_a(2, 2, stage_23[:], AT_GELU_A + KIB)
+
+        stage_b = [staged("stage_b00", 12), staged("stage_b01", 6)]
+        scale_half_b(0, stage_b, EXTRA)
         quantize_b(0, stage_b, at_gelu_b(0, 2))
-        quantize_a(0, 2, stage_01[:], at_gelu_b(0, 2) + KIB)
-        for i in range(AHEAD, TILES):
-            ga[i] = as_passes(placed([P, UNIT], F32, f"gelu_a{i}", at_gelu_b(0, 3) + 4 * KIB * (i - AHEAD))[:])
+        ga[6] = as_passes(placed([P, UNIT], F32, "gelu_a6", at_gelu_b(0, 3))[:])
+        ga[7] = as_passes(placed([P, UNIT], F32, "gelu_a7", at_gelu_b(1, 3))[:])
+        gelu_a(6, ga[6])
         score(0, 0)
         score(1, 0)
-        finish_scalar(0, 0)
-        gelu_a(5, ga[5])
-        gelu_a(6, ga[6])
-        gelu_a(7, ga[7])
+        score(2, 0)
+        finish_scalar(1, 0)
+        score(3, 0)
+        finish_scalar(2, 0)
 
-        stage_b = [staged("stage_b10", 4), staged("stage_b11", 0)]
-        stage_23 = staged("stage_a23", 8)
-        scale_a(True, pair23, stage_23[:])
-        for n in range(4):
-            scale_b(1, n, unit(stage_b[n // 2], n % 2))
-        finish_vector(1, 0)
-        quantize_a(2, 2, stage_23[:], at_gelu_b(1, 2) + KIB)
-        for i in range(2, 4):
-            score(i, 0)
+        stage_b = [staged("stage_b10", 6), staged("stage_b11", 12)]
+        scale_half_b(1, stage_b, 0)
+        finish_gpsimd(0, 0)
+        gelu_a(7, ga[7])
         quantize_b(1, stage_b, at_gelu_b(1, 2))
         for i in range(4):
             score(i, 1)
@@ -315,23 +320,22 @@ def tile_list_biaff_gelu_cap_kernel(
                 score(i, h)
 
         stage_45 = staged("stage_a45", 4)
-        finish_gpsimd(2, 0, AT_STAGE)
-        finish_gpsimd(3, 0)
-        finish_gpsimd(0, 1)
+        finish_gpsimd(3, 0, AT_STAGE + 12 * KIB)
+        finish_gpsimd(0, 1, AT_STAGE + 14 * KIB)
         for n in range(2):
-            scale_a(False, ga[4 + n], unit(stage_45, n))
+            scale_a(False, ga[4 + n], as_passes(unit(stage_45, n)))
         for n in range(2):
             late_tile(4 + n, unit(stage_45, n))
         finish_vector(1, 1)
         stage_6 = staged("stage_a6", 7, units=1)
         finish_gpsimd(2, 1, AT_STAGE + 4 * KIB)
-        scale_a(False, ga[6], stage_6[:])
+        scale_a(False, ga[6], as_passes(stage_6[:]))
         finish_vector(3, 1)
         late_tile(6, stage_6[:])
         finish_vector(4, 0)
         stage_7 = staged("stage_a7", 6, units=1)
         finish_gpsimd(4, 1, AT_STAGE + 8 * KIB)
-        scale_a(False, ga[7], stage_7[:])
+        scale_a(False, ga[7], as_passes(stage_7[:]))
         finish_vector(5, 0)
         late_tile(7, stage_7[:])
         finish_vector(5, 1)

@@ -25,7 +25,7 @@ UNIT_WORDS = UNIT // 4
 TILES = M // P
 ROW0 = P - 16
 QUAD3 = 96
-AHEAD = 6
+AHEAD = 7
 BANKS = 4
 EXTRA = 128
 BANK_BYTES = 2048
@@ -37,8 +37,6 @@ AT_WORDS_A1 = 3 * KIB // 2
 AT_WA = 3 * KIB
 AT_PICKED_B1 = 7 * KIB // 2
 AT_WORDS_B = 4 * KIB
-AT_WB = (8 * KIB, 16 * KIB)
-AT_WB_CODES = AT_WB[1]
 AT_STAGE = 24 * KIB
 AT_WB_ROUNDED = (AT_STAGE + 12 * KIB, AT_STAGE + 8 * KIB)
 AT_GELU_A = 80 * KIB
@@ -64,9 +62,9 @@ def tile_list_biaff_gelu_cap_kernel(
         wa_raw = placed([P, R // 2], I32, "wa_raw", AT_WA)
         wa_sc_raw = placed([P, R // 4], I32, "wa_sc_raw", AT_WA_SCALES)
         wa_codes = keep.tile([P, R // 2], I32, name="wa_codes", align_bytes=64)
-        wb_raw = [placed([P, 4, HALF], F32, f"wb_raw{b}", AT_WB[b]) for b in range(PASSES)]
+        wb_raw = keep.tile([P, 4, R], F32, name="wb_raw")
         wb_rounded = [placed([P, 4 * HALF], BF16, f"wb_rounded{b}", AT_WB_ROUNDED[b]) for b in range(PASSES)]
-        wb_codes = placed([P, R], U32, "wb_codes", AT_WB_CODES)
+        wb_codes = keep.tile([P, R], U32, name="wb_codes", align_bytes=64)
         wb_plane = keep.tile([P, R], U8, name="wb_plane", align_bytes=64)
         factor_rows = keep.tile([P, R // 4], F32, name="factor_rows")
         ident = keep.tile([P, P], F32, name="ident")
@@ -90,8 +88,7 @@ def tile_list_biaff_gelu_cap_kernel(
                 factor_rows[4 * side : 4 * side + 4, :].rearrange("t (c i) -> t c i", i=8),
                 vector.rearrange("(c t i) -> t c i", t=4, i=8),
             )
-        for b in range(PASSES):
-            nc.sync.dma_start(wb_raw[b][:], wb[:, b * HALF : (b + 1) * HALF].rearrange("(p j) c -> p j c", j=4))
+        nc.sync.dma_start(wb_raw[:], wb.rearrange("(p j) c -> p j c", j=4))
         make_identity(nc, ident[:])
 
         def carry_rows(queue, plane, rows):
@@ -221,8 +218,8 @@ def tile_list_biaff_gelu_cap_kernel(
         def store(i, cols, src):
             nc.sync.dma_start(out[P * i : P * (i + 1), cols], src)
 
-        def finish_vector(i, h):
-            cols = slice(HALF * h, HALF * (h + 1))
+        def finish_vector(i, h, halves=1):
+            cols = slice(HALF * h, HALF * (h + halves))
             nc.vector.tensor_scalar_mul(result[i][:, cols], result[i][:, cols], 8.0)
             store(i, cols, result[i][:, cols])
 
@@ -276,7 +273,7 @@ def tile_list_biaff_gelu_cap_kernel(
         for b in range(PASSES):
             nc.vector.tensor_copy(
                 wb_rounded[b][:].rearrange("p (t q i j) -> p t q i j", t=4, i=8, j=4),
-                wb_raw[b][:].rearrange("p j (q t i) -> p t q i j", t=4, i=8),
+                wb_raw[:, :, HALF * b : HALF * (b + 1)].rearrange("p j (q t i) -> p t q i j", t=4, i=8),
             )
         for b in range(PASSES):
             cols = slice(HALF * b, HALF * (b + 1))
@@ -296,9 +293,7 @@ def tile_list_biaff_gelu_cap_kernel(
         stage_b = [staged("stage_b00", 12), staged("stage_b01", 6)]
         scale_half_b(0, stage_b, EXTRA)
         quantize_b(0, stage_b, at_gelu_b(0, 2))
-        ga[6] = as_passes(placed([P, UNIT], F32, "gelu_a6", at_gelu_b(0, 3))[:])
         ga[7] = as_passes(placed([P, UNIT], F32, "gelu_a7", at_gelu_b(1, 3))[:])
-        gelu_a(6, ga[6])
         score(0, 0)
         score(1, 0)
         score(2, 0)
@@ -324,21 +319,21 @@ def tile_list_biaff_gelu_cap_kernel(
         finish_gpsimd(0, 1, AT_STAGE + 14 * KIB)
         for n in range(2):
             scale_a(False, ga[4 + n], as_passes(unit(stage_45, n)))
-        for n in range(2):
-            late_tile(4 + n, unit(stage_45, n))
+        late_tile(4, unit(stage_45, 0))
+        finish_scalar(4, 0)
+        late_tile(5, unit(stage_45, 1))
         finish_vector(1, 1)
         stage_6 = staged("stage_a6", 7, units=1)
         finish_gpsimd(2, 1, AT_STAGE + 4 * KIB)
         scale_a(False, ga[6], as_passes(stage_6[:]))
         finish_vector(3, 1)
         late_tile(6, stage_6[:])
-        finish_vector(4, 0)
         stage_7 = staged("stage_a7", 6, units=1)
         finish_gpsimd(4, 1, AT_STAGE + 8 * KIB)
         scale_a(False, ga[7], as_passes(stage_7[:]))
         finish_vector(5, 0)
         late_tile(7, stage_7[:])
         finish_vector(5, 1)
-        for i in range(6, 8):
-            for h in range(2):
-                finish_vector(i, h)
+        finish_vector(6, 0, halves=2)
+        finish_vector(7, 0)
+        finish_vector(7, 1)

@@ -218,8 +218,8 @@ def tile_list_biaff_gelu_cap_kernel(
         def store(i, cols, src):
             nc.sync.dma_start(out[P * i : P * (i + 1), cols], src)
 
-        def finish_vector(i, h, halves=1):
-            cols = slice(HALF * h, HALF * (h + halves))
+        def finish_vector(i, h):
+            cols = slice(HALF * h, HALF * (h + 1))
             nc.vector.tensor_scalar_mul(result[i][:, cols], result[i][:, cols], 8.0)
             store(i, cols, result[i][:, cols])
 
@@ -271,10 +271,10 @@ def tile_list_biaff_gelu_cap_kernel(
             gelu_a(i, ga[i])
 
         for b in range(PASSES):
-            nc.vector.tensor_copy(
-                wb_rounded[b][:].rearrange("p (t q i j) -> p t q i j", t=4, i=8, j=4),
-                wb_raw[:, :, HALF * b : HALF * (b + 1)].rearrange("p j (q t i) -> p t q i j", t=4, i=8),
-            )
+            dst = wb_rounded[b][:].rearrange("p (t q k e j) -> p t q k j e", t=4, k=4, e=2, j=4)
+            src = wb_raw[:, :, HALF * b : HALF * (b + 1)].rearrange("p j (q t k e) -> p t q k j e", t=4, k=4, e=2)
+            for t in range(4):
+                nc.vector.tensor_copy(dst[:, t], src[:, t])
         for b in range(PASSES):
             cols = slice(HALF * b, HALF * (b + 1))
             quantize(wb_codes[:, cols], wb_plane[:, cols], wb_rounded[b][:])
@@ -334,6 +334,6 @@ def tile_list_biaff_gelu_cap_kernel(
         finish_vector(5, 0)
         late_tile(7, stage_7[:])
         finish_vector(5, 1)
-        finish_vector(6, 0, halves=2)
-        finish_vector(7, 0)
-        finish_vector(7, 1)
+        for i in range(6, 8):
+            for h in range(2):
+                finish_vector(i, h)

@@ -27,7 +27,7 @@ ROW0 = P - 16
 QUAD3 = 96
 AHEAD = 7
 BANKS = 4
-EXTRA = 128
+EXTRA = 192
 BANK_BYTES = 2048
 KIB = 1024
 
@@ -35,7 +35,6 @@ AT_WA_SCALES = 0
 AT_PICKED_A = KIB
 AT_WORDS_A1 = 3 * KIB // 2
 AT_WA = 3 * KIB
-AT_PICKED_B1 = 7 * KIB // 2
 AT_WORDS_B = 4 * KIB
 AT_STAGE = 24 * KIB
 AT_WB_ROUNDED = (AT_STAGE + 12 * KIB, AT_STAGE + 8 * KIB)
@@ -69,13 +68,12 @@ def tile_list_biaff_gelu_cap_kernel(
         factor_rows = keep.tile([P, R // 4], F32, name="factor_rows")
         ident = keep.tile([P, P], F32, name="ident")
         plane_a = keep.tile([P, (M + R) // 4], I32, name="plane_a", align_bytes=64)
-        plane_b = [keep.tile([P, HALF // 4], I32, name=f"plane_b{h}", align_bytes=64) for h in range(2)]
+        plane_b = keep.tile([P, J // 4], I32, name="plane_b", align_bytes=64)
 
         nc.vector.memset(table_sc[0:ROW0, :], 0)
         nc.vector.memset(wa_sc_raw[0:ROW0, :], 0)
         nc.gpsimd.memset(factor_rows[:], 0.0)
-        for h in range(2):
-            nc.gpsimd.memset(plane_b[h][:], 0)
+        nc.gpsimd.memset(plane_b[:], 0)
 
         nc.sync.dma_start(table_sc[ROW0:P, :], tab_scales[0].bitcast(I32))
         nc.sync.dma_start(list_a[:], offs)
@@ -110,7 +108,7 @@ def tile_list_biaff_gelu_cap_kernel(
         )
         nc.vector.tensor_copy(plane_a[:, 0 : M // 4], picked_a)
         carry_rows(nc.scalar, plane_a[:], plane_a[:])
-        carry_rows(nc.sync, plane_b[0][:], gather_scales(list_b[:, 0:32], HALF, AT_WA_SCALES, "picked_b0"))
+        carry_rows(nc.sync, plane_b[:], gather_scales(list_b[:], J, AT_WA_SCALES, "picked_b"))
 
         ha_codes = keep.tile([P, TILES * UNIT_WORDS], U32, name="ha_codes", align_bytes=64)
         hb_codes = keep.tile([P, TILES * UNIT_WORDS], U32, name="hb_codes", align_bytes=64)
@@ -130,7 +128,6 @@ def tile_list_biaff_gelu_cap_kernel(
                 wa_raw[:, cols].rearrange("p (q t i) -> p t q i", t=4, i=4),
             )
         gather_words(words_a[1], list_a[:, 32:64])
-        carry_rows(nc.sync, plane_b[1][:], gather_scales(list_b[:, 32:64], HALF, AT_PICKED_B1, "picked_b1"))
         gather_words(words_b, list_b[:])
 
         def quantize(codes, plane, src):
@@ -144,7 +141,7 @@ def tile_list_biaff_gelu_cap_kernel(
             if side == 0:
                 moving, moving_plane = words_a[half][:, c0 : c0 + P], plane_a[:].bitcast(U8)[:, P * tile : P * (tile + 1)]
             else:
-                moving, moving_plane = words_b[:, P * tile : P * (tile + 1)], plane_b[half][:].bitcast(U8)[:, c0 : c0 + P]
+                moving, moving_plane = words_b[:, P * tile : P * (tile + 1)], plane_b[:].bitcast(U8)[:, P * tile : P * (tile + 1)]
             for t in range(4):
                 c0 = P * (4 * b + t)
                 if side == 0:
@@ -267,8 +264,9 @@ def tile_list_biaff_gelu_cap_kernel(
             nc.tensor.transpose(factors[:, b, :], factor_rows[:, b * P : (b + 1) * P], ident[:])
         gelu_a(2, ga[2])
         nc.scalar.copy(factors_sb[:], factors[:, :, 0:8])
-        for i in range(3, AHEAD):
+        for i in range(3, AHEAD - 1):
             gelu_a(i, ga[i])
+        gelu_a(6, ga[6], passes=[0])
 
         for b in range(PASSES):
             dst = wb_rounded[b][:].rearrange("p (t q k e j) -> p t q k j e", t=4, k=4, e=2, j=4)
@@ -294,18 +292,19 @@ def tile_list_biaff_gelu_cap_kernel(
         scale_half_b(0, stage_b, EXTRA)
         quantize_b(0, stage_b, at_gelu_b(0, 2))
         ga[7] = as_passes(placed([P, UNIT], F32, "gelu_a7", at_gelu_b(1, 3))[:])
+        gelu_a(6, ga[6], passes=[1])
         score(0, 0)
         score(1, 0)
         score(2, 0)
         finish_scalar(1, 0)
         score(3, 0)
-        finish_scalar(2, 0)
 
         stage_b = [staged("stage_b10", 6), staged("stage_b11", 12)]
-        scale_half_b(1, stage_b, 0)
+        scale_half_b(1, stage_b, -128)
         finish_gpsimd(0, 0)
         gelu_a(7, ga[7])
         quantize_b(1, stage_b, at_gelu_b(1, 2))
+        finish_vector(2, 0)
         for i in range(4):
             score(i, 1)
 

@@ -25,9 +25,12 @@ UNIT_WORDS = UNIT // 4
 TILES = M // P
 ROW0 = P - 16
 QUAD3 = 96
-AHEAD = 7
 BANKS = 4
-EXTRA = 192
+QUARTER = 256
+SHARE_A01 = 156
+SHARE_B0 = 312
+SHARE_C = 140
+SHARE_LATE = 40
 BANK_BYTES = 2048
 KIB = 1024
 
@@ -36,10 +39,9 @@ AT_PICKED_A = KIB
 AT_WORDS_A1 = 3 * KIB // 2
 AT_WA = 3 * KIB
 AT_WORDS_B = 4 * KIB
-AT_STAGE = 24 * KIB
-AT_WB_ROUNDED = (AT_STAGE + 12 * KIB, AT_STAGE + 8 * KIB)
-AT_GELU_A = 80 * KIB
-AT_GELU_B = 48 * KIB
+AT_LANE = (12 * KIB, 24 * KIB)
+AT_GELU = 32 * KIB
+AT_TANH = 88 * KIB
 
 
 def tile_list_biaff_gelu_cap_kernel(
@@ -62,10 +64,10 @@ def tile_list_biaff_gelu_cap_kernel(
         wa_sc_raw = placed([P, R // 4], I32, "wa_sc_raw", AT_WA_SCALES)
         wa_codes = keep.tile([P, R // 2], I32, name="wa_codes", align_bytes=64)
         wb_raw = keep.tile([P, 4, R], F32, name="wb_raw")
-        wb_rounded = [placed([P, 4 * HALF], BF16, f"wb_rounded{b}", AT_WB_ROUNDED[b]) for b in range(PASSES)]
+        wb_rounded = [placed([P, 4 * HALF], BF16, f"wb_rounded{b}", AT_LANE[b]) for b in range(PASSES)]
         wb_codes = keep.tile([P, R], U32, name="wb_codes", align_bytes=64)
         wb_plane = keep.tile([P, R], U8, name="wb_plane", align_bytes=64)
-        factor_rows = keep.tile([P, R // 4], F32, name="factor_rows")
+        factor_rows = keep.tile([P, P], F32, name="factor_rows")
         ident = keep.tile([P, P], F32, name="ident")
         plane_a = keep.tile([P, (M + R) // 4], I32, name="plane_a", align_bytes=64)
         plane_b = keep.tile([P, J // 4], I32, name="plane_b", align_bytes=64)
@@ -83,8 +85,8 @@ def tile_list_biaff_gelu_cap_kernel(
         nc.sync.dma_start(wa_raw[:], wa_words[0].bitcast(I32))
         for side, vector in enumerate((sa, sb)):
             nc.sync.dma_start(
-                factor_rows[4 * side : 4 * side + 4, :].rearrange("t (c i) -> t c i", i=8),
-                vector.rearrange("(c t i) -> t c i", t=4, i=8),
+                factor_rows[8 * side : 8 * side + 8, :].rearrange("c (q i) -> c q i", i=8),
+                vector.rearrange("(q c i) -> c q i", c=8, i=8),
             )
         nc.sync.dma_start(wb_raw[:], wb.rearrange("(p j) c -> p j c", j=4))
         make_identity(nc, ident[:])
@@ -103,8 +105,8 @@ def tile_list_biaff_gelu_cap_kernel(
 
         picked_a = gather_scales(list_a[:], M, AT_PICKED_A, "picked_a")
         nc.vector.tensor_copy(
-            plane_a[:, M // 4 :].rearrange("p (b t q i) -> p b t q i", b=PASSES, t=4, i=2),
-            wa_sc_raw[:].rearrange("p (b q t i) -> p b t q i", b=PASSES, t=4, i=2),
+            plane_a[:, M // 4 :].rearrange("p (c q i) -> p c q i", c=8, i=2),
+            wa_sc_raw[:].rearrange("p (q c i) -> p c q i", c=8, i=2),
         )
         nc.vector.tensor_copy(plane_a[:, 0 : M // 4], picked_a)
         carry_rows(nc.scalar, plane_a[:], plane_a[:])
@@ -112,8 +114,9 @@ def tile_list_biaff_gelu_cap_kernel(
 
         ha_codes = keep.tile([P, TILES * UNIT_WORDS], U32, name="ha_codes", align_bytes=64)
         hb_codes = keep.tile([P, TILES * UNIT_WORDS], U32, name="hb_codes", align_bytes=64)
-        factors_sb = keep.tile([P, PASSES, 8], F32, name="factors_sb")
-        result = [keep.tile([P, J], F32, name=f"result{i}") for i in range(TILES)]
+        factors_sb = keep.tile([P, 16], F32, name="factors_sb")
+        ha_plane = keep.tile([P, TILES * UNIT_WORDS], U8, name="ha_plane", align_bytes=64)
+        hb_plane = keep.tile([P, TILES * UNIT_WORDS], U8, name="hb_plane", align_bytes=64)
 
         words_a = [
             keep.tile([P, HALF], U32, name="words_a0", align_bytes=64),
@@ -122,10 +125,9 @@ def tile_list_biaff_gelu_cap_kernel(
         words_b = placed([P, J], U32, "words_b", AT_WORDS_B)
         gather_words(words_a[0], list_a[:, 0:32])
         for b in range(PASSES):
-            cols = slice(R // 4 * b, R // 4 * (b + 1))
             nc.vector.tensor_copy(
-                wa_codes[:, cols].rearrange("p (t q i) -> p t q i", t=4, i=4),
-                wa_raw[:, cols].rearrange("p (q t i) -> p t q i", t=4, i=4),
+                wa_codes[:].rearrange("p (b t q i) -> p b t q i", b=PASSES, t=4, i=4)[:, b],
+                wa_raw[:].rearrange("p (q b t i) -> p b t q i", b=PASSES, t=4, i=4)[:, b],
             )
         gather_words(words_a[1], list_a[:, 32:64])
         gather_words(words_b, list_b[:])
@@ -133,8 +135,12 @@ def tile_list_biaff_gelu_cap_kernel(
         def quantize(codes, plane, src):
             nc.vector.quantize_mx(codes.bitcast(FP8X4), plane, src)
 
+        turns = []
+
         def next_bank():
-            return psum.tile([P, 4, P], F32, name="bank", tag="bank", bufs=BANKS, offset=0)
+            turn = len(turns)
+            turns.append(psum.tile([P, 4, P], F32, name=f"bank{turn}", offset=BANK_BYTES * (turn % BANKS)))
+            return turns[turn]
 
         def hidden_bank(side, tile, b, dst, bank):
             half, c0 = divmod(P * tile, HALF)
@@ -167,172 +173,184 @@ def tile_list_biaff_gelu_cap_kernel(
         def as_passes(ap):
             return ap.rearrange("p (b n t) -> p b n t", b=PASSES, t=4)
 
-        def at_gelu_b(h, n):
-            return AT_GELU_B + 4 * KIB * (4 * h + n)
+        def entries(ap):
+            return ap.rearrange("p (n t) -> p n t", t=4)
 
-        def gelu_b(h):
-            buffers = [
-                placed([P, UNIT * units], F32, f"gelu_b{h}{n}", at_gelu_b(h, n))[:].rearrange("p (n t) -> p n t", t=4)
-                for n, units in ((0, 2), (2, 1), (3, 1))
-            ]
-            for s in range(4):
-                hidden_bank(1, 4 * h + s, 0, buffers[0][:, P * s : P * (s + 1)], next_bank())
-            for s in range(4):
-                hidden_bank(1, 4 * h + s, 1, buffers[1 + s // 2][:, P * (s % 2) : P * (s % 2 + 1)], next_bank())
-            return buffers
+        def at_gelu_a(i):
+            return AT_GELU + 4 * KIB * (i - 2)
+
+        def at_gelu_b(n):
+            return AT_GELU + 4 * KIB * (6 + n)
+
+        def gelu_b(tile0, tiles, b, dst):
+            for s in range(tiles):
+                hidden_bank(1, tile0 + s, b, dst[:, P * s : P * (s + 1)], next_bank())
 
         def scale_a(on_gpsimd, g, dst):
             engine, f = (nc.gpsimd, factors_sb) if on_gpsimd else (nc.vector, factors)
-            engine.tensor_tensor(dst, g, f[:, :, 0:4].unsqueeze(2).to_broadcast([P, PASSES, g.shape[2], 4]), ALU.mult)
+            engine.tensor_tensor(dst, g, f[:, 0:8].rearrange("p (b t) -> p b t", t=4).unsqueeze(2).to_broadcast([P, PASSES, g.shape[2], 4]), ALU.mult)
 
         def scale_b(on_gpsimd, b, g, dst):
             engine, f = (nc.gpsimd, factors_sb) if on_gpsimd else (nc.vector, factors)
-            engine.tensor_tensor(dst, g, f[:, b, 4:8].unsqueeze(1).to_broadcast([P, g.shape[1], 4]), ALU.mult)
-
-        def scale_half_b(h, stages, extra):
-            cut = (UNIT + extra) // 4
-            dst = [s[:].rearrange("p (n t) -> p n t", t=4) for s in stages]
-            scale_b(True, 0, gb[h][0][:, 0:cut], dst[0][:, 0:cut])
-            scale_b(False, 1, gb[h][1], dst[1][:, 0 : 2 * P])
-            scale_b(False, 0, gb[h][0][:, cut:], dst[0][:, cut:])
-            scale_b(False, 1, gb[h][2], dst[1][:, 2 * P :])
-
-        def score(i, h):
-            acc = next_bank()[:].rearrange("p t n -> p (t n)")
-            for b in range(PASSES):
-                cb = HALF * (PASSES * h + b)
-                nc.tensor.matmul_mx(
-                    acc,
-                    lhsT=ha[i][0][:, b].bitcast(FP8X4),
-                    lhsT_scale=ha[i][1][:, b],
-                    rhs=hb_codes[:, cb : cb + HALF].bitcast(FP8X4),
-                    rhs_scale=hb_plane[h][:, HALF * b : HALF * (b + 1)],
-                    start=(b == 0),
-                    stop=(b == PASSES - 1),
-                )
-            nc.scalar.activation(result[i][:, HALF * h : HALF * (h + 1)], acc, ACT.Tanh, scale=0.00390625)
-
-        def store(i, cols, src):
-            nc.sync.dma_start(out[P * i : P * (i + 1), cols], src)
-
-        def finish_vector(i, h):
-            cols = slice(HALF * h, HALF * (h + 1))
-            nc.vector.tensor_scalar_mul(result[i][:, cols], result[i][:, cols], 8.0)
-            store(i, cols, result[i][:, cols])
-
-        def finish_scalar(i, h):
-            cols = slice(HALF * h, HALF * (h + 1))
-            nc.scalar.activation(result[i][:, cols], result[i][:, cols], ACT.Copy, scale=8.0)
-            store(i, cols, result[i][:, cols])
-
-        def finish_gpsimd(i, h, at=None):
-            cols = slice(HALF * h, HALF * (h + 1))
-            dst = result[i][:, cols] if at is None else placed([P, HALF], F32, f"times8_{i}{h}", at)[:]
-            nc.gpsimd.tensor_scalar(dst, result[i][:, cols], 8.0, 0.0, ALU.mult, ALU.add)
-            store(i, cols, dst)
-
-        def staged(name, kib, units=2):
-            return placed([P, units * UNIT], BF16, name, AT_STAGE + kib * KIB)
-
-        def unit(stage, n):
-            return stage[:, UNIT * n : UNIT * (n + 1)]
+            engine.tensor_tensor(dst, g, f[:, 8 + 4 * b : 12 + 4 * b].unsqueeze(1).to_broadcast([P, g.shape[1], 4]), ALU.mult)
 
         ha = {}
-        hb_plane = {}
+        piece = {}
 
-        def quantize_a(i, tiles, src, at):
-            plane = placed([P, tiles * UNIT_WORDS], U8, f"ha_plane{i}", at)
-            codes = ha_codes[:, UNIT_WORDS * i : UNIT_WORDS * (i + tiles)]
-            quantize(codes, plane[:], src)
+        def score(name, tiles, col0, width, at=None):
+            acc = next_bank()[:].rearrange("p t n -> p (t n)")
+            h, c0 = divmod(col0, HALF)
+            for s, i in enumerate(tiles):
+                for b in range(PASSES):
+                    cb = HALF * (PASSES * h + b) + c0
+                    nc.tensor.matmul_mx(
+                        acc[:, width * s : width * (s + 1)],
+                        lhsT=ha[i][0][:, b].bitcast(FP8X4),
+                        lhsT_scale=ha[i][1][:, b],
+                        rhs=hb_codes[:, cb : cb + width].bitcast(FP8X4),
+                        rhs_scale=hb_plane[:, cb : cb + width],
+                        start=(b == 0),
+                        stop=(b == PASSES - 1),
+                    )
+            cols = width * len(tiles)
+            if at is None:
+                tanh = keep.tile([P, cols], F32, name=f"tanh_{name}")
+            else:
+                tanh = placed([P, cols], F32, f"tanh_{name}", at)
+            nc.scalar.activation(tanh[:], acc[:, 0:cols], ACT.Tanh, scale=0.00390625)
+            rows = out[P * tiles[0] : P * (tiles[-1] + 1), col0 : col0 + width]
+            piece[name] = (tanh, rows.rearrange("(s p) c -> p s c", p=P), len(tiles))
+
+        def store(name, src):
+            nc.sync.dma_start(piece[name][1], src.rearrange("p (s c) -> p s c", s=piece[name][2]))
+
+        def finish_vector(name, moved=False):
+            src = piece[name][0]
+            dst = keep.tile(list(src.shape), F32, name=f"times8_{name}") if moved else src
+            nc.vector.tensor_scalar_mul(dst[:], src[:], 8.0)
+            store(name, dst[:])
+
+        def finish_scalar(name):
+            src = piece[name][0]
+            nc.scalar.activation(src[:], src[:], ACT.Copy, scale=8.0)
+            store(name, src[:])
+
+        def finish_gpsimd(name, at):
+            dst = placed([P, HALF], F32, f"times8_{name}", at)
+            nc.gpsimd.tensor_scalar(dst[:], piece[name][0][:], 8.0, 0.0, ALU.mult, ALU.add)
+            store(name, dst[:])
+
+        def staged(name, at, units=1):
+            return placed([P, units * UNIT], BF16, name, at)
+
+        def quantize_a(i, tiles, src):
+            cols = slice(UNIT_WORDS * i, UNIT_WORDS * (i + tiles))
+            codes, plane = ha_codes[:, cols], ha_plane[:, cols]
+            quantize(codes, plane, src)
             for n in range(tiles):
-                ha[i + n] = [x.rearrange("p (b s c) -> p b s c", b=PASSES, s=tiles)[:, :, n, :] for x in (codes, plane[:])]
+                ha[i + n] = [x.rearrange("p (b s c) -> p b s c", b=PASSES, s=tiles)[:, :, n, :] for x in (codes, plane)]
 
-        def quantize_b(h, stages, at):
-            hb_plane[h] = placed([P, PASSES * HALF], U8, f"hb_plane{h}", at)
-            for b in range(PASSES):
-                c0 = HALF * (PASSES * h + b)
-                quantize(hb_codes[:, c0 : c0 + HALF], hb_plane[h][:, HALF * b : HALF * (b + 1)], stages[b][:])
+        def quantize_b(b, entry0, count, src):
+            h, c0 = divmod(entry0, HALF)
+            cols = slice(HALF * (PASSES * h + b) + c0, HALF * (PASSES * h + b) + c0 + count)
+            quantize(hb_codes[:, cols], hb_plane[:, cols], src)
 
         at_last_bank = BANKS * BANK_BYTES
         pair01 = as_passes(keep.tile([P, 2 * UNIT], F32, name="gelu_a01")[:])
         ga = {0: pair01[:, :, 0:P], 1: pair01[:, :, P : 2 * P]}
-        ga.update({i: as_passes(placed([P, UNIT], F32, f"gelu_a{i}", AT_GELU_A + 4 * KIB * (i - 2))[:]) for i in range(2, AHEAD)})
+        ga.update({i: as_passes(placed([P, UNIT], F32, f"gelu_a{i}", at_gelu_a(i))[:]) for i in range(2, TILES)})
         gelu_a(0, ga[0], psum.tile([P, 4, P], F32, name="first", offset=at_last_bank))
-        factors = psum.tile([P, PASSES, P], F32, name="factors", offset=at_last_bank)
+        factors = psum.tile([P, P], F32, name="factors", offset=at_last_bank)
         gelu_a(1, ga[1])
-        for b in range(PASSES):
-            nc.tensor.transpose(factors[:, b, :], factor_rows[:, b * P : (b + 1) * P], ident[:])
+        nc.tensor.transpose(factors[:], factor_rows[:], ident[:])
         gelu_a(2, ga[2])
-        nc.scalar.copy(factors_sb[:], factors[:, :, 0:8])
-        for i in range(3, AHEAD - 1):
+        nc.scalar.copy(factors_sb[:], factors[:, 0:16])
+        for i in range(3, 6):
             gelu_a(i, ga[i])
-        gelu_a(6, ga[6], passes=[0])
 
         for b in range(PASSES):
             dst = wb_rounded[b][:].rearrange("p (t q k e j) -> p t q k j e", t=4, k=4, e=2, j=4)
-            src = wb_raw[:, :, HALF * b : HALF * (b + 1)].rearrange("p j (q t k e) -> p t q k j e", t=4, k=4, e=2)
+            src = wb_raw[:].rearrange("p j (q b t k e) -> p b t q k j e", b=PASSES, t=4, k=4, e=2)[:, b]
             for t in range(4):
                 nc.vector.tensor_copy(dst[:, t], src[:, t])
         for b in range(PASSES):
             cols = slice(HALF * b, HALF * (b + 1))
             quantize(wb_codes[:, cols], wb_plane[:, cols], wb_rounded[b][:])
-        gb = [gelu_b(h) for h in range(2)]
 
-        stage_01 = staged("stage_a01", 6)
-        stage_23 = staged("stage_a23", 12)
-        cut = P + EXTRA // 8
-        scale_a(True, pair01[:, :, 0:cut], as_passes(stage_01[:])[:, :, 0:cut])
-        scale_a(False, ga[2], as_passes(stage_23[:])[:, :, 0:P])
-        scale_a(False, pair01[:, :, cut:], as_passes(stage_01[:])[:, :, cut:])
-        scale_a(False, ga[3], as_passes(stage_23[:])[:, :, P:])
-        quantize_a(0, 2, stage_01[:], AT_GELU_A)
-        quantize_a(2, 2, stage_23[:], AT_GELU_A + KIB)
+        gb_first = [entries(placed([P, UNIT * units], F32, f"gelu_b{n}", at_gelu_b(n))[:]) for n, units in ((0, 2), (2, 1), (3, 1))]
+        gelu_b(0, 4, 0, gb_first[0])
+        gelu_b(0, 2, 1, gb_first[1])
+        gelu_b(2, 2, 1, gb_first[2])
+        gb_late = [entries(placed([P, UNIT], F32, f"gelu_b{n}", at_gelu_b(n))[:]) for n in range(4, 8)]
+        for n in range(4):
+            gelu_b(4 + 2 * (n // 2), 2, n % 2, gb_late[n])
+        gelu_a(6, ga[6], passes=[0])
 
-        stage_b = [staged("stage_b00", 12), staged("stage_b01", 6)]
-        scale_half_b(0, stage_b, EXTRA)
-        quantize_b(0, stage_b, at_gelu_b(0, 2))
-        ga[7] = as_passes(placed([P, UNIT], F32, "gelu_a7", at_gelu_b(1, 3))[:])
-        gelu_a(6, ga[6], passes=[1])
-        score(0, 0)
-        score(1, 0)
-        score(2, 0)
-        finish_scalar(1, 0)
-        score(3, 0)
-
-        stage_b = [staged("stage_b10", 6), staged("stage_b11", 12)]
-        scale_half_b(1, stage_b, -128)
-        finish_gpsimd(0, 0)
-        gelu_a(7, ga[7])
-        quantize_b(1, stage_b, at_gelu_b(1, 2))
-        finish_vector(2, 0)
-        for i in range(4):
-            score(i, 1)
-
-        def late_tile(i, src):
-            quantize_a(i, 1, src, at_gelu_b(0, 0) + UNIT_WORDS * i)
-            for h in range(2):
-                score(i, h)
-
-        stage_45 = staged("stage_a45", 4)
-        finish_gpsimd(3, 0, AT_STAGE + 12 * KIB)
-        finish_gpsimd(0, 1, AT_STAGE + 14 * KIB)
+        stage = [staged(f"stage_a{n}", AT_LANE[n], 2) for n in range(2)]
+        scale_a(True, pair01[:, :, 0:SHARE_A01], as_passes(stage[0][:])[:, :, 0:SHARE_A01])
+        scale_a(False, pair01[:, :, SHARE_A01:], as_passes(stage[0][:])[:, :, SHARE_A01:])
+        scale_a(False, ga[2], as_passes(stage[1][:])[:, :, 0:P])
+        scale_a(False, ga[3], as_passes(stage[1][:])[:, :, P:])
         for n in range(2):
-            scale_a(False, ga[4 + n], as_passes(unit(stage_45, n)))
-        late_tile(4, unit(stage_45, 0))
-        finish_scalar(4, 0)
-        late_tile(5, unit(stage_45, 1))
-        finish_vector(1, 1)
-        stage_6 = staged("stage_a6", 7, units=1)
-        finish_gpsimd(2, 1, AT_STAGE + 4 * KIB)
-        scale_a(False, ga[6], as_passes(stage_6[:]))
-        finish_vector(3, 1)
-        late_tile(6, stage_6[:])
-        stage_7 = staged("stage_a7", 6, units=1)
-        finish_gpsimd(4, 1, AT_STAGE + 8 * KIB)
-        scale_a(False, ga[7], as_passes(stage_7[:]))
-        finish_vector(5, 0)
-        late_tile(7, stage_7[:])
-        finish_vector(5, 1)
-        for i in range(6, 8):
-            for h in range(2):
-                finish_vector(i, h)
+            quantize_a(2 * n, 2, stage[n][:])
+
+        stage = [staged(f"stage_b{n}", AT_LANE[n], 2) for n in range(2)]
+        scale_b(True, 0, gb_first[0][:, 0:SHARE_B0], entries(stage[0][:])[:, 0:SHARE_B0])
+        scale_b(False, 0, gb_first[0][:, SHARE_B0:], entries(stage[0][:])[:, SHARE_B0:])
+        scale_b(False, 1, gb_first[1], entries(stage[1][:])[:, 0:QUARTER])
+        scale_b(False, 1, gb_first[2], entries(stage[1][:])[:, QUARTER:])
+        for b in range(PASSES):
+            quantize_b(b, 0, HALF, stage[b][:])
+        for i in range(4):
+            score(f"{i}0", [i], 0, HALF)
+
+        stage = [staged(f"stage_c{n}", AT_LANE[n] + KIB) for n in range(2)]
+        scale_b(True, 0, gb_late[0][:, 0:SHARE_C], entries(stage[0][:])[:, 0:SHARE_C])
+        scale_b(False, 0, gb_late[0][:, SHARE_C:], entries(stage[0][:])[:, SHARE_C:])
+        scale_b(False, 1, gb_late[1], entries(stage[1][:]))
+        for b in range(PASSES):
+            quantize_b(b, HALF, QUARTER, stage[b][:])
+        score("0c", [0, 1], HALF, QUARTER)
+        finish_scalar("30")
+        score("2c", [2, 3], HALF, QUARTER, AT_TANH)
+        gelu_a(6, ga[6], passes=[1])
+        gelu_a(7, ga[7], passes=[0])
+
+        stage = [staged(f"stage_d{n}", AT_LANE[n] + 5 * KIB // 2) for n in range(2)]
+        finish_gpsimd("00", AT_LANE[0] - KIB // 2)
+        finish_gpsimd("10", AT_LANE[1] - KIB // 2)
+        for b in range(PASSES):
+            scale_b(False, b, gb_late[2 + b], entries(stage[b][:]))
+        finish_gpsimd("20", at_gelu_b(6))
+        for b in range(PASSES):
+            quantize_b(b, HALF + QUARTER, QUARTER, stage[b][:])
+        score("0d", [0, 1], HALF + QUARTER, QUARTER)
+        score("2d", [2, 3], HALF + QUARTER, QUARTER, AT_TANH + 2 * KIB)
+        gelu_a(7, ga[7], passes=[1])
+
+        def late_tile(i, at, plain, moved):
+            stage_i = staged(f"stage_late{i}", at)
+            scale_a(True, ga[i][:, :, 0:SHARE_LATE], as_passes(stage_i[:])[:, :, 0:SHARE_LATE])
+            scale_a(False, ga[i][:, :, SHARE_LATE:], as_passes(stage_i[:])[:, :, SHARE_LATE:])
+            for name in plain:
+                finish_vector(name)
+            for name in moved:
+                finish_vector(name, moved=True)
+            quantize_a(i, 1, stage_i[:])
+
+        late_tile(4, AT_LANE[0] + 5 * KIB // 2, ["0c"], ["2c"])
+        score("40", [4], 0, HALF)
+        score("41", [4], HALF, HALF, AT_TANH + 4 * KIB)
+        finish_scalar("40")
+        late_tile(5, AT_TANH, ["0d"], ["2d"])
+        score("50", [5], 0, HALF)
+        score("51", [5], HALF, HALF)
+        late_tile(6, AT_TANH + 2 * KIB, [], ["41"])
+        score("60", [6], 0, HALF)
+        score("61", [6], HALF, HALF)
+        late_tile(7, AT_TANH + 4 * KIB, ["50"], [])
+        score("70", [7], 0, HALF)
+        score("7c", [7], HALF, QUARTER)
+        score("7d", [7], HALF + QUARTER, QUARTER)
+        for name in ("51", "60", "61", "70", "7c", "7d"):
+            finish_vector(name)

@@ -27,21 +27,22 @@ ROW0 = P - 16
 QUAD3 = 96
 BANKS = 4
 QUARTER = 256
-SHARE_A01 = 156
-SHARE_B0 = 312
-SHARE_C = 140
-SHARE_LATE = 40
+SHARE_A01 = 152
+SHARE_B0 = 304
+SHARE_C = 128
+SHARE_D = 144
+SHARE_LATE = 32
 BANK_BYTES = 2048
 KIB = 1024
 
 AT_WA_SCALES = 0
-AT_PICKED_A = KIB
+AT_PICKED_A = 96 * KIB
 AT_WORDS_A1 = 3 * KIB // 2
 AT_WA = 3 * KIB
 AT_WORDS_B = 4 * KIB
 AT_LANE = (12 * KIB, 24 * KIB)
 AT_GELU = 32 * KIB
-AT_TANH = 88 * KIB
+AT_TANH = (99 * KIB, 105 * KIB, 111 * KIB)
 
 
 def tile_list_biaff_gelu_cap_kernel(
@@ -63,18 +64,14 @@ def tile_list_biaff_gelu_cap_kernel(
         wa_raw = placed([P, R // 2], I32, "wa_raw", AT_WA)
         wa_sc_raw = placed([P, R // 4], I32, "wa_sc_raw", AT_WA_SCALES)
         wa_codes = keep.tile([P, R // 2], I32, name="wa_codes", align_bytes=64)
-        wb_raw = keep.tile([P, 4, R], F32, name="wb_raw")
         wb_rounded = [placed([P, 4 * HALF], BF16, f"wb_rounded{b}", AT_LANE[b]) for b in range(PASSES)]
         wb_codes = keep.tile([P, R], U32, name="wb_codes", align_bytes=64)
-        wb_plane = keep.tile([P, R], U8, name="wb_plane", align_bytes=64)
-        factor_rows = keep.tile([P, P], F32, name="factor_rows")
         ident = keep.tile([P, P], F32, name="ident")
         plane_a = keep.tile([P, (M + R) // 4], I32, name="plane_a", align_bytes=64)
         plane_b = keep.tile([P, J // 4], I32, name="plane_b", align_bytes=64)
 
         nc.vector.memset(table_sc[0:ROW0, :], 0)
         nc.vector.memset(wa_sc_raw[0:ROW0, :], 0)
-        nc.gpsimd.memset(factor_rows[:], 0.0)
         nc.gpsimd.memset(plane_b[:], 0)
 
         nc.sync.dma_start(table_sc[ROW0:P, :], tab_scales[0].bitcast(I32))
@@ -83,12 +80,6 @@ def tile_list_biaff_gelu_cap_kernel(
         nc.sync.dma_start(list_b[:], offs2)
         nc.sync.dma_start(table[:], tab_words[0].rearrange("p t i -> p (t i)").bitcast(I32))
         nc.sync.dma_start(wa_raw[:], wa_words[0].bitcast(I32))
-        for side, vector in enumerate((sa, sb)):
-            nc.sync.dma_start(
-                factor_rows[8 * side : 8 * side + 8, :].rearrange("c (q i) -> c q i", i=8),
-                vector.rearrange("(q c i) -> c q i", c=8, i=8),
-            )
-        nc.sync.dma_start(wb_raw[:], wb.rearrange("(p j) c -> p j c", j=4))
         make_identity(nc, ident[:])
 
         def carry_rows(queue, plane, rows):
@@ -109,7 +100,16 @@ def tile_list_biaff_gelu_cap_kernel(
             wa_sc_raw[:].rearrange("p (q c i) -> p c q i", c=8, i=2),
         )
         nc.vector.tensor_copy(plane_a[:, 0 : M // 4], picked_a)
-        carry_rows(nc.scalar, plane_a[:], plane_a[:])
+        carry_rows(nc.sync, plane_a[:], plane_a[:])
+        wb_raw = placed([P, 4, R], F32, "wb_raw", AT_PICKED_A + KIB // 2)
+        nc.sync.dma_start(wb_raw[:], wb.rearrange("(p j) c -> p j c", j=4))
+        factor_rows = placed([P, P], F32, "factor_rows", AT_PICKED_A)
+        nc.gpsimd.memset(factor_rows[:], 0.0)
+        for side, vector in enumerate((sa, sb)):
+            nc.sync.dma_start(
+                factor_rows[8 * side : 8 * side + 8, :].rearrange("c (q i) -> c q i", i=8),
+                vector.rearrange("(q c i) -> c q i", c=8, i=8),
+            )
         carry_rows(nc.sync, plane_b[:], gather_scales(list_b[:], J, AT_WA_SCALES, "picked_b"))
 
         ha_codes = keep.tile([P, TILES * UNIT_WORDS], U32, name="ha_codes", align_bytes=64)
@@ -259,15 +259,19 @@ def tile_list_biaff_gelu_cap_kernel(
         pair01 = as_passes(keep.tile([P, 2 * UNIT], F32, name="gelu_a01")[:])
         ga = {0: pair01[:, :, 0:P], 1: pair01[:, :, P : 2 * P]}
         ga.update({i: as_passes(placed([P, UNIT], F32, f"gelu_a{i}", at_gelu_a(i))[:]) for i in range(2, TILES)})
-        gelu_a(0, ga[0], psum.tile([P, 4, P], F32, name="first", offset=at_last_bank))
+        for i in range(2):
+            gelu_a(i, ga[i])
+        gelu_a(2, ga[2], psum.tile([P, 4, P], F32, name="first", offset=at_last_bank))
         factors = psum.tile([P, P], F32, name="factors", offset=at_last_bank)
-        gelu_a(1, ga[1])
+        gelu_a(3, ga[3])
         nc.tensor.transpose(factors[:], factor_rows[:], ident[:])
-        gelu_a(2, ga[2])
-        nc.scalar.copy(factors_sb[:], factors[:, 0:16])
-        for i in range(3, 6):
+        passing = next_bank()
+        nc.tensor.transpose(passing[:, 0, :], factor_rows[:], ident[:])
+        nc.scalar.copy(factors_sb[:], passing[:, 0, 0:16])
+        for i in range(4, 7):
             gelu_a(i, ga[i])
 
+        wb_plane = placed([P, R], U8, "wb_plane", AT_PICKED_A - KIB // 2)
         for b in range(PASSES):
             dst = wb_rounded[b][:].rearrange("p (t q k e j) -> p t q k j e", t=4, k=4, e=2, j=4)
             src = wb_raw[:].rearrange("p j (q b t k e) -> p b t q k j e", b=PASSES, t=4, k=4, e=2)[:, b]
@@ -284,7 +288,6 @@ def tile_list_biaff_gelu_cap_kernel(
         gb_late = [entries(placed([P, UNIT], F32, f"gelu_b{n}", at_gelu_b(n))[:]) for n in range(4, 8)]
         for n in range(4):
             gelu_b(4 + 2 * (n // 2), 2, n % 2, gb_late[n])
-        gelu_a(6, ga[6], passes=[0])
 
         stage = [staged(f"stage_a{n}", AT_LANE[n], 2) for n in range(2)]
         scale_a(True, pair01[:, :, 0:SHARE_A01], as_passes(stage[0][:])[:, :, 0:SHARE_A01])
@@ -310,46 +313,45 @@ def tile_list_biaff_gelu_cap_kernel(
         scale_b(False, 1, gb_late[1], entries(stage[1][:]))
         for b in range(PASSES):
             quantize_b(b, HALF, QUARTER, stage[b][:])
-        score("0c", [0, 1], HALF, QUARTER)
-        finish_scalar("30")
-        score("2c", [2, 3], HALF, QUARTER, AT_TANH)
-        gelu_a(6, ga[6], passes=[1])
+        score("0c", [0, 1], HALF, QUARTER, AT_TANH[0])
+        score("2c", [2, 3], HALF, QUARTER)
         gelu_a(7, ga[7], passes=[0])
 
-        stage = [staged(f"stage_d{n}", AT_LANE[n] + 5 * KIB // 2) for n in range(2)]
-        finish_gpsimd("00", AT_LANE[0] - KIB // 2)
-        finish_gpsimd("10", AT_LANE[1] - KIB // 2)
-        for b in range(PASSES):
-            scale_b(False, b, gb_late[2 + b], entries(stage[b][:]))
-        finish_gpsimd("20", at_gelu_b(6))
+        stage = [staged(f"stage_d{n}", AT_LANE[n] + KIB) for n in range(2)]
+        scale_b(True, 0, gb_late[2][:, 0:SHARE_D], entries(stage[0][:])[:, 0:SHARE_D])
+        scale_b(False, 0, gb_late[2][:, SHARE_D:], entries(stage[0][:])[:, SHARE_D:])
+        scale_b(False, 1, gb_late[3], entries(stage[1][:]))
+        finish_vector("00")
+        finish_vector("10")
         for b in range(PASSES):
             quantize_b(b, HALF + QUARTER, QUARTER, stage[b][:])
-        score("0d", [0, 1], HALF + QUARTER, QUARTER)
-        score("2d", [2, 3], HALF + QUARTER, QUARTER, AT_TANH + 2 * KIB)
+        score("0d", [0, 1], HALF + QUARTER, QUARTER, AT_TANH[1])
+        score("2d", [2, 3], HALF + QUARTER, QUARTER)
         gelu_a(7, ga[7], passes=[1])
 
-        def late_tile(i, at, plain, moved):
-            stage_i = staged(f"stage_late{i}", at)
-            scale_a(True, ga[i][:, :, 0:SHARE_LATE], as_passes(stage_i[:])[:, :, 0:SHARE_LATE])
-            scale_a(False, ga[i][:, :, SHARE_LATE:], as_passes(stage_i[:])[:, :, SHARE_LATE:])
+        def late_tile(i, at, on_gpsimd, plain, moved, at_tanh=None):
+            stage_i = staged(f"stage_late{i}", at + 3 * KIB // 2)
+            share = 0
+            if on_gpsimd:
+                finish_gpsimd(on_gpsimd, at - 3 * KIB // 2)
+            else:
+                share = SHARE_LATE
+                scale_a(True, ga[i][:, :, 0:share], as_passes(stage_i[:])[:, :, 0:share])
+            scale_a(False, ga[i][:, :, share:], as_passes(stage_i[:])[:, :, share:])
             for name in plain:
                 finish_vector(name)
             for name in moved:
                 finish_vector(name, moved=True)
             quantize_a(i, 1, stage_i[:])
+            score(f"{i}0", [i], 0, HALF, at_tanh)
 
-        late_tile(4, AT_LANE[0] + 5 * KIB // 2, ["0c"], ["2c"])
-        score("40", [4], 0, HALF)
-        score("41", [4], HALF, HALF, AT_TANH + 4 * KIB)
-        finish_scalar("40")
-        late_tile(5, AT_TANH, ["0d"], ["2d"])
-        score("50", [5], 0, HALF)
+        late_tile(4, AT_LANE[0] + KIB, "20", ["30"], ["0c"], AT_TANH[2])
+        score("41", [4], HALF, HALF)
+        late_tile(5, AT_TANH[0], "2c", [], ["0d"])
         score("51", [5], HALF, HALF)
-        late_tile(6, AT_TANH + 2 * KIB, [], ["41"])
-        score("60", [6], 0, HALF)
+        late_tile(6, AT_TANH[1], "2d", [], ["40"])
         score("61", [6], HALF, HALF)
-        late_tile(7, AT_TANH + 4 * KIB, ["50"], [])
-        score("70", [7], 0, HALF)
+        late_tile(7, AT_TANH[2], "41", ["50"], [])
         score("7c", [7], HALF, QUARTER)
         score("7d", [7], HALF + QUARTER, QUARTER)
         for name in ("51", "60", "61", "70", "7c", "7d"):

@@ -345,14 +345,43 @@ def tile_list_biaff_gelu_cap_kernel(
             quantize_a(i, 1, stage_i[:])
             score(f"{i}0", [i], 0, HALF, at_tanh)
 
-        late_tile(4, AT_LANE[0] + KIB, "20", ["30"], ["0c"], AT_TANH[2])
-        score("41", [4], HALF, HALF)
+        late_tile(4, AT_LANE[0] + KIB, "20", ["30"], ["0c"])
+        score("41", [4], HALF, HALF, AT_TANH[2])
+        finish_scalar("40")
         late_tile(5, AT_TANH[0], "2c", [], ["0d"])
         score("51", [5], HALF, HALF)
-        late_tile(6, AT_TANH[1], "2d", [], ["40"])
+        late_tile(6, AT_TANH[1], "2d", [], ["41"])
         score("61", [6], HALF, HALF)
-        late_tile(7, AT_TANH[2], "41", ["50"], [])
-        score("7c", [7], HALF, QUARTER)
-        score("7d", [7], HALF + QUARTER, QUARTER)
-        for name in ("51", "60", "61", "70", "7c", "7d"):
-            finish_vector(name)
+
+        stage_7 = staged("stage_late7", AT_TANH[2] + 3 * KIB // 2)
+        finish_gpsimd("50", AT_TANH[2] - 3 * KIB // 2)
+        for b in range(PASSES):
+            cols = slice(HALF * b, HALF * (b + 1))
+            nc.vector.tensor_tensor(
+                entries(stage_7[:, cols]), ga[7][:, b], factors[:, 4 * b : 4 * b + 4].unsqueeze(1).to_broadcast([P, P, 4]), ALU.mult
+            )
+        banks = [psum.tile([P, HALF], F32, name=f"last{n}", offset=BANK_BYTES * (BANKS + 1 + n)) for n in range(3)]
+        banks.append(next_bank()[:].rearrange("p t n -> p (t n)"))
+        for b in range(PASSES):
+            cols = slice(7 * UNIT_WORDS + P * b, 7 * UNIT_WORDS + P * (b + 1))
+            if b == 1:
+                finish_vector("51")
+            quantize(ha_codes[:, cols], ha_plane[:, cols], stage_7[:, HALF * b : HALF * (b + 1)])
+            for n in range(4):
+                cb = HALF * (PASSES * (n // 2) + b) + QUARTER * (n % 2)
+                nc.tensor.matmul_mx(
+                    banks[n][:, 0:QUARTER],
+                    lhsT=ha_codes[:, cols].bitcast(FP8X4),
+                    lhsT_scale=ha_plane[:, cols],
+                    rhs=hb_codes[:, cb : cb + QUARTER].bitcast(FP8X4),
+                    rhs_scale=hb_plane[:, cb : cb + QUARTER],
+                    start=(b == 0),
+                    stop=(b == PASSES - 1),
+                )
+        finish_vector("60")
+        finish_vector("61")
+        for n in range(4):
+            tanh = keep.tile([P, QUARTER], F32, name=f"tanh_7{n}")
+            nc.scalar.activation(tanh[:], banks[n][:, 0:QUARTER], ACT.Tanh, scale=0.00390625)
+            piece[f"7{n}"] = (tanh, out[7 * P :, QUARTER * n : QUARTER * (n + 1)].rearrange("(s p) c -> p s c", p=P), 1)
+            finish_vector(f"7{n}")

@@ -27,9 +27,9 @@ ROW0 = P - 16
 QUAD3 = 96
 BANKS = 4
 QUARTER = 256
-SHARE_A01 = 152
-SHARE_B0 = 304
-SHARE_C = 128
+SHARE_A01 = 164
+SHARE_B0 = 328
+SHARE_C = 152
 SHARE_D = 144
 SHARE_LATE = 32
 BANK_BYTES = 2048
@@ -40,7 +40,7 @@ AT_PICKED_A = 96 * KIB
 AT_WORDS_A1 = 3 * KIB // 2
 AT_WA = 3 * KIB
 AT_WORDS_B = 4 * KIB
-AT_LANE = (12 * KIB, 24 * KIB)
+AT_LANE = (12 * KIB, 26 * KIB)
 AT_GELU = 32 * KIB
 AT_TANH = (99 * KIB, 105 * KIB, 111 * KIB)
 
@@ -268,7 +268,7 @@ def tile_list_biaff_gelu_cap_kernel(
         passing = next_bank()
         nc.tensor.transpose(passing[:, 0, :], factor_rows[:], ident[:])
         nc.scalar.copy(factors_sb[:], passing[:, 0, 0:16])
-        for i in range(4, 7):
+        for i in range(4, 6):
             gelu_a(i, ga[i])
 
         wb_plane = placed([P, R], U8, "wb_plane", AT_PICKED_A - KIB // 2)
@@ -288,52 +288,54 @@ def tile_list_biaff_gelu_cap_kernel(
         gb_late = [entries(placed([P, UNIT], F32, f"gelu_b{n}", at_gelu_b(n))[:]) for n in range(4, 8)]
         for n in range(4):
             gelu_b(4 + 2 * (n // 2), 2, n % 2, gb_late[n])
+        gelu_a(6, ga[6], passes=[0])
 
-        stage = [staged(f"stage_a{n}", AT_LANE[n], 2) for n in range(2)]
+        stage = [staged(f"stage_a{n}", AT_LANE[0] + (6 * n - 3) * KIB, 2) for n in range(2)]
         scale_a(True, pair01[:, :, 0:SHARE_A01], as_passes(stage[0][:])[:, :, 0:SHARE_A01])
-        scale_a(False, pair01[:, :, SHARE_A01:], as_passes(stage[0][:])[:, :, SHARE_A01:])
         scale_a(False, ga[2], as_passes(stage[1][:])[:, :, 0:P])
         scale_a(False, ga[3], as_passes(stage[1][:])[:, :, P:])
-        for n in range(2):
+        scale_a(False, pair01[:, :, SHARE_A01:], as_passes(stage[0][:])[:, :, SHARE_A01:])
+        for n in (1, 0):
             quantize_a(2 * n, 2, stage[n][:])
 
-        stage = [staged(f"stage_b{n}", AT_LANE[n], 2) for n in range(2)]
+        stage = [staged(f"stage_b{n}", AT_LANE[0] + (4 * n + 1) * KIB, 2) for n in range(2)]
         scale_b(True, 0, gb_first[0][:, 0:SHARE_B0], entries(stage[0][:])[:, 0:SHARE_B0])
-        scale_b(False, 0, gb_first[0][:, SHARE_B0:], entries(stage[0][:])[:, SHARE_B0:])
         scale_b(False, 1, gb_first[1], entries(stage[1][:])[:, 0:QUARTER])
         scale_b(False, 1, gb_first[2], entries(stage[1][:])[:, QUARTER:])
-        for b in range(PASSES):
+        scale_b(False, 0, gb_first[0][:, SHARE_B0:], entries(stage[0][:])[:, SHARE_B0:])
+        for b in (1, 0):
             quantize_b(b, 0, HALF, stage[b][:])
         for i in range(4):
             score(f"{i}0", [i], 0, HALF)
 
-        stage = [staged(f"stage_c{n}", AT_LANE[n] + KIB) for n in range(2)]
+        stage = [staged(f"stage_c{n}", AT_LANE[0] + (3 * n + 5) * KIB) for n in range(2)]
         scale_b(True, 0, gb_late[0][:, 0:SHARE_C], entries(stage[0][:])[:, 0:SHARE_C])
-        scale_b(False, 0, gb_late[0][:, SHARE_C:], entries(stage[0][:])[:, SHARE_C:])
         scale_b(False, 1, gb_late[1], entries(stage[1][:]))
-        for b in range(PASSES):
+        scale_b(False, 0, gb_late[0][:, SHARE_C:], entries(stage[0][:])[:, SHARE_C:])
+        for b in (1, 0):
             quantize_b(b, HALF, QUARTER, stage[b][:])
         score("0c", [0, 1], HALF, QUARTER, AT_TANH[0])
         score("2c", [2, 3], HALF, QUARTER)
+        gelu_a(6, ga[6], passes=[1])
         gelu_a(7, ga[7], passes=[0])
 
-        stage = [staged(f"stage_d{n}", AT_LANE[n] + KIB) for n in range(2)]
+        stage = [staged(f"stage_d{n}", AT_LANE[0] + (5 * n + 14) * KIB // 2) for n in range(2)]
         scale_b(True, 0, gb_late[2][:, 0:SHARE_D], entries(stage[0][:])[:, 0:SHARE_D])
-        scale_b(False, 0, gb_late[2][:, SHARE_D:], entries(stage[0][:])[:, SHARE_D:])
         scale_b(False, 1, gb_late[3], entries(stage[1][:]))
+        scale_b(False, 0, gb_late[2][:, SHARE_D:], entries(stage[0][:])[:, SHARE_D:])
         finish_vector("00")
         finish_vector("10")
-        for b in range(PASSES):
+        for b in (1, 0):
             quantize_b(b, HALF + QUARTER, QUARTER, stage[b][:])
         score("0d", [0, 1], HALF + QUARTER, QUARTER, AT_TANH[1])
         score("2d", [2, 3], HALF + QUARTER, QUARTER)
         gelu_a(7, ga[7], passes=[1])
 
         def late_tile(i, at, on_gpsimd, plain, moved, at_tanh=None):
-            stage_i = staged(f"stage_late{i}", at + 3 * KIB // 2)
+            stage_i = staged(f"stage_late{i}", at + KIB)
             share = 0
             if on_gpsimd:
-                finish_gpsimd(on_gpsimd, at - 3 * KIB // 2)
+                finish_gpsimd(on_gpsimd, at - KIB)
             else:
                 share = SHARE_LATE
                 scale_a(True, ga[i][:, :, 0:share], as_passes(stage_i[:])[:, :, 0:share])
@@ -345,12 +347,11 @@ def tile_list_biaff_gelu_cap_kernel(
             quantize_a(i, 1, stage_i[:])
             score(f"{i}0", [i], 0, HALF, at_tanh)
 
-        late_tile(4, AT_LANE[0] + KIB, "20", ["30"], ["0c"])
+        late_tile(4, AT_LANE[0] + 10 * KIB, "20", ["30"], ["0c"])
         score("41", [4], HALF, HALF, AT_TANH[2])
-        finish_scalar("40")
         late_tile(5, AT_TANH[0], "2c", [], ["0d"])
         score("51", [5], HALF, HALF)
-        late_tile(6, AT_TANH[1], "2d", [], ["41"])
+        late_tile(6, AT_TANH[1], "2d", ["40"], ["41"])
         score("61", [6], HALF, HALF)
 
         stage_7 = staged("stage_late7", AT_TANH[2] + 3 * KIB // 2)

@@ -20,29 +20,34 @@ ALU = mybir.AluOpType
 P = 128
 PASSES = 2
 HALF = 512
+QUARTER = 256
 UNIT = 1024
 UNIT_WORDS = UNIT // 4
 TILES = M // P
 ROW0 = P - 16
-QUAD3 = 96
 BANKS = 4
-QUARTER = 256
-SHARE_A01 = 164
-SHARE_B0 = 328
-SHARE_C = 152
-SHARE_D = 144
-SHARE_LATE = 32
+EARLY = 4
+AHEAD = 6
+LAST = TILES - 1
+SHARE_A = 156
+SHARE_HALF = 312
+SHARE_QUARTER = (144, 136)
 BANK_BYTES = 2048
 KIB = 1024
 
 AT_WA_SCALES = 0
-AT_PICKED_A = 96 * KIB
 AT_WORDS_A1 = 3 * KIB // 2
 AT_WA = 3 * KIB
 AT_WORDS_B = 4 * KIB
-AT_LANE = (12 * KIB, 26 * KIB)
+AT_WB_ROUNDED = (12 * KIB, 26 * KIB)
+AT_STAGES_A = (9 * KIB, 15 * KIB)
+AT_STAGES_HALF = (13 * KIB, 17 * KIB)
+AT_STAGES_QUARTER = ((17 * KIB, 20 * KIB), (19 * KIB, 43 * KIB // 2))
 AT_GELU = 32 * KIB
-AT_TANH = (99 * KIB, 105 * KIB, 111 * KIB)
+AT_PICKED_A = 96 * KIB
+AT_WB_RAW = AT_PICKED_A + KIB // 2
+AT_WB_PLANE = AT_PICKED_A - KIB // 2
+AT_RELEASE = {4: 22 * KIB, 5: 99 * KIB, 6: 105 * KIB, 7: 111 * KIB}
 
 
 def tile_list_biaff_gelu_cap_kernel(
@@ -64,7 +69,7 @@ def tile_list_biaff_gelu_cap_kernel(
         wa_raw = placed([P, R // 2], I32, "wa_raw", AT_WA)
         wa_sc_raw = placed([P, R // 4], I32, "wa_sc_raw", AT_WA_SCALES)
         wa_codes = keep.tile([P, R // 2], I32, name="wa_codes", align_bytes=64)
-        wb_rounded = [placed([P, 4 * HALF], BF16, f"wb_rounded{b}", AT_LANE[b]) for b in range(PASSES)]
+        wb_rounded = [placed([P, 4 * HALF], BF16, f"wb_rounded{b}", AT_WB_ROUNDED[b]) for b in range(PASSES)]
         wb_codes = keep.tile([P, R], U32, name="wb_codes", align_bytes=64)
         ident = keep.tile([P, P], F32, name="ident")
         plane_a = keep.tile([P, (M + R) // 4], I32, name="plane_a", align_bytes=64)
@@ -82,9 +87,9 @@ def tile_list_biaff_gelu_cap_kernel(
         nc.sync.dma_start(wa_raw[:], wa_words[0].bitcast(I32))
         make_identity(nc, ident[:])
 
-        def carry_rows(queue, plane, rows):
+        def carry_rows(plane, rows):
             for quad in range(4):
-                queue.dma_start(plane[32 * quad : 32 * quad + 4, :], rows[ROW0 + 4 * quad : ROW0 + 4 * quad + 4, :])
+                nc.sync.dma_start(plane[32 * quad : 32 * quad + 4, :], rows[ROW0 + 4 * quad : ROW0 + 4 * quad + 4, :])
 
         def gather_scales(offsets, count, at, name):
             picked = placed([P, count], U8, name, at)
@@ -100,8 +105,8 @@ def tile_list_biaff_gelu_cap_kernel(
             wa_sc_raw[:].rearrange("p (q c i) -> p c q i", c=8, i=2),
         )
         nc.vector.tensor_copy(plane_a[:, 0 : M // 4], picked_a)
-        carry_rows(nc.sync, plane_a[:], plane_a[:])
-        wb_raw = placed([P, 4, R], F32, "wb_raw", AT_PICKED_A + KIB // 2)
+        carry_rows(plane_a[:], plane_a[:])
+        wb_raw = placed([P, 4, R], F32, "wb_raw", AT_WB_RAW)
         nc.sync.dma_start(wb_raw[:], wb.rearrange("(p j) c -> p j c", j=4))
         factor_rows = placed([P, P], F32, "factor_rows", AT_PICKED_A)
         nc.gpsimd.memset(factor_rows[:], 0.0)
@@ -110,7 +115,7 @@ def tile_list_biaff_gelu_cap_kernel(
                 factor_rows[8 * side : 8 * side + 8, :].rearrange("c (q i) -> c q i", i=8),
                 vector.rearrange("(q c i) -> c q i", c=8, i=8),
             )
-        carry_rows(nc.sync, plane_b[:], gather_scales(list_b[:], J, AT_WA_SCALES, "picked_b"))
+        carry_rows(plane_b[:], gather_scales(list_b[:], J, AT_WA_SCALES, "picked_b"))
 
         ha_codes = keep.tile([P, TILES * UNIT_WORDS], U32, name="ha_codes", align_bytes=64)
         hb_codes = keep.tile([P, TILES * UNIT_WORDS], U32, name="hb_codes", align_bytes=64)
@@ -143,11 +148,12 @@ def tile_list_biaff_gelu_cap_kernel(
             return turns[turn]
 
         def hidden_bank(side, tile, b, dst, bank):
-            half, c0 = divmod(P * tile, HALF)
+            cols = slice(P * tile, P * (tile + 1))
             if side == 0:
-                moving, moving_plane = words_a[half][:, c0 : c0 + P], plane_a[:].bitcast(U8)[:, P * tile : P * (tile + 1)]
+                half, entry0 = divmod(P * tile, HALF)
+                moving, moving_plane = words_a[half][:, entry0 : entry0 + P], plane_a[:].bitcast(U8)[:, cols]
             else:
-                moving, moving_plane = words_b[:, P * tile : P * (tile + 1)], plane_b[:].bitcast(U8)[:, P * tile : P * (tile + 1)]
+                moving, moving_plane = words_b[:, cols], plane_b[:].bitcast(U8)[:, cols]
             for t in range(4):
                 c0 = P * (4 * b + t)
                 if side == 0:
@@ -166,82 +172,34 @@ def tile_list_biaff_gelu_cap_kernel(
                 )
             nc.scalar.activation(dst, bank[:].rearrange("p t n -> p n t"), ACT.Gelu_apprx_tanh)
 
-        def gelu_a(i, g, first_bank=None, passes=range(PASSES)):
-            for b in passes:
-                hidden_bank(0, i, b, g[:, b], first_bank if (first_bank is not None and b == 0) else next_bank())
-
         def as_passes(ap):
             return ap.rearrange("p (b n t) -> p b n t", b=PASSES, t=4)
 
-        def entries(ap):
+        def as_entries(ap):
             return ap.rearrange("p (n t) -> p n t", t=4)
 
-        def at_gelu_a(i):
-            return AT_GELU + 4 * KIB * (i - 2)
+        def gelu_a(i, b):
+            hidden_bank(0, i, b, ga[i][:, b], next_bank())
 
-        def at_gelu_b(n):
-            return AT_GELU + 4 * KIB * (6 + n)
-
-        def gelu_b(tile0, tiles, b, dst):
+        def gelu_b(unit0, tile0, tiles, b):
+            at = AT_GELU + 4 * KIB * (TILES - 2 + unit0)
+            dst = as_entries(placed([P, 4 * P * tiles], F32, f"gelu_b{unit0}", at)[:])
             for s in range(tiles):
                 hidden_bank(1, tile0 + s, b, dst[:, P * s : P * (s + 1)], next_bank())
+            return dst
 
-        def scale_a(on_gpsimd, g, dst):
-            engine, f = (nc.gpsimd, factors_sb) if on_gpsimd else (nc.vector, factors)
-            engine.tensor_tensor(dst, g, f[:, 0:8].rearrange("p (b t) -> p b t", t=4).unsqueeze(2).to_broadcast([P, PASSES, g.shape[2], 4]), ALU.mult)
+        def scale_a(engine, f, g, dst):
+            factor = f[:, 0:8].rearrange("p (b t) -> p b t", t=4).unsqueeze(2)
+            engine.tensor_tensor(dst, g, factor.to_broadcast([P, PASSES, g.shape[2], 4]), ALU.mult)
 
-        def scale_b(on_gpsimd, b, g, dst):
-            engine, f = (nc.gpsimd, factors_sb) if on_gpsimd else (nc.vector, factors)
-            engine.tensor_tensor(dst, g, f[:, 8 + 4 * b : 12 + 4 * b].unsqueeze(1).to_broadcast([P, g.shape[1], 4]), ALU.mult)
-
-        ha = {}
-        piece = {}
-
-        def score(name, tiles, col0, width, at=None):
-            acc = next_bank()[:].rearrange("p t n -> p (t n)")
-            h, c0 = divmod(col0, HALF)
-            for s, i in enumerate(tiles):
-                for b in range(PASSES):
-                    cb = HALF * (PASSES * h + b) + c0
-                    nc.tensor.matmul_mx(
-                        acc[:, width * s : width * (s + 1)],
-                        lhsT=ha[i][0][:, b].bitcast(FP8X4),
-                        lhsT_scale=ha[i][1][:, b],
-                        rhs=hb_codes[:, cb : cb + width].bitcast(FP8X4),
-                        rhs_scale=hb_plane[:, cb : cb + width],
-                        start=(b == 0),
-                        stop=(b == PASSES - 1),
-                    )
-            cols = width * len(tiles)
-            if at is None:
-                tanh = keep.tile([P, cols], F32, name=f"tanh_{name}")
-            else:
-                tanh = placed([P, cols], F32, f"tanh_{name}", at)
-            nc.scalar.activation(tanh[:], acc[:, 0:cols], ACT.Tanh, scale=0.00390625)
-            rows = out[P * tiles[0] : P * (tiles[-1] + 1), col0 : col0 + width]
-            piece[name] = (tanh, rows.rearrange("(s p) c -> p s c", p=P), len(tiles))
-
-        def store(name, src):
-            nc.sync.dma_start(piece[name][1], src.rearrange("p (s c) -> p s c", s=piece[name][2]))
-
-        def finish_vector(name, moved=False):
-            src = piece[name][0]
-            dst = keep.tile(list(src.shape), F32, name=f"times8_{name}") if moved else src
-            nc.vector.tensor_scalar_mul(dst[:], src[:], 8.0)
-            store(name, dst[:])
-
-        def finish_scalar(name):
-            src = piece[name][0]
-            nc.scalar.activation(src[:], src[:], ACT.Copy, scale=8.0)
-            store(name, src[:])
-
-        def finish_gpsimd(name, at):
-            dst = placed([P, HALF], F32, f"times8_{name}", at)
-            nc.gpsimd.tensor_scalar(dst[:], piece[name][0][:], 8.0, 0.0, ALU.mult, ALU.add)
-            store(name, dst[:])
+        def scale_pass(engine, f, side, b, g, dst):
+            c0 = 8 * side + 4 * b
+            engine.tensor_tensor(dst, g, f[:, c0 : c0 + 4].unsqueeze(1).to_broadcast([P, g.shape[1], 4]), ALU.mult)
 
         def staged(name, at, units=1):
             return placed([P, units * UNIT], BF16, name, at)
+
+        ha = {}
 
         def quantize_a(i, tiles, src):
             cols = slice(UNIT_WORDS * i, UNIT_WORDS * (i + tiles))
@@ -250,139 +208,178 @@ def tile_list_biaff_gelu_cap_kernel(
             for n in range(tiles):
                 ha[i + n] = [x.rearrange("p (b s c) -> p b s c", b=PASSES, s=tiles)[:, :, n, :] for x in (codes, plane)]
 
-        def quantize_b(b, entry0, count, src):
-            h, c0 = divmod(entry0, HALF)
-            cols = slice(HALF * (PASSES * h + b) + c0, HALF * (PASSES * h + b) + c0 + count)
-            quantize(hb_codes[:, cols], hb_plane[:, cols], src)
+        def hb_cols(b, col0, width):
+            half, entry0 = divmod(col0, HALF)
+            start = HALF * (PASSES * half + b) + entry0
+            return slice(start, start + width)
 
-        at_last_bank = BANKS * BANK_BYTES
-        pair01 = as_passes(keep.tile([P, 2 * UNIT], F32, name="gelu_a01")[:])
-        ga = {0: pair01[:, :, 0:P], 1: pair01[:, :, P : 2 * P]}
-        ga.update({i: as_passes(placed([P, UNIT], F32, f"gelu_a{i}", at_gelu_a(i))[:]) for i in range(2, TILES)})
+        def quantize_b(col0, width, stages):
+            for b in (1, 0):
+                cols = hb_cols(b, col0, width)
+                quantize(hb_codes[:, cols], hb_plane[:, cols], stages[b][:])
+
+        def score_pass(acc, codes, plane, b, col0, width):
+            cols = hb_cols(b, col0, width)
+            nc.tensor.matmul_mx(
+                acc,
+                lhsT=codes.bitcast(FP8X4),
+                lhsT_scale=plane,
+                rhs=hb_codes[:, cols].bitcast(FP8X4),
+                rhs_scale=hb_plane[:, cols],
+                start=(b == 0),
+                stop=(b == PASSES - 1),
+            )
+
+        pieces = {}
+
+        def tanh_piece(acc, i, tiles, col0, width, at=None):
+            shape, name = [P, tiles * width], f"tanh_{i}_{col0}"
+            values = keep.tile(shape, F32, name=name) if at is None else placed(shape, F32, name, at)
+            nc.scalar.activation(values[:], acc, ACT.Tanh, scale=0.00390625)
+            rows = out[P * i : P * (i + tiles), col0 : col0 + width].rearrange("(s p) c -> p s c", p=P)
+            pieces[i, col0] = (values, rows, tiles)
+
+        def score(i, col0, width, at=None):
+            tiles = HALF // width
+            acc = next_bank()[:].rearrange("p t n -> p (t n)")
+            for s in range(tiles):
+                for b in range(PASSES):
+                    codes, plane = ha[i + s]
+                    score_pass(acc[:, width * s : width * (s + 1)], codes[:, b], plane[:, b], b, col0, width)
+            tanh_piece(acc, i, tiles, col0, width, at)
+
+        def store(piece, src):
+            nc.sync.dma_start(pieces[piece][1], src.rearrange("p (s c) -> p s c", s=pieces[piece][2]))
+
+        def finish_vector(piece, moved=False):
+            src = pieces[piece][0]
+            dst = keep.tile([P, HALF], F32, name=f"times8_{piece[0]}_{piece[1]}") if moved else src
+            nc.vector.tensor_scalar_mul(dst[:], src[:], 8.0)
+            store(piece, dst[:])
+
+        def finish_scalar(piece):
+            src = pieces[piece][0]
+            nc.scalar.activation(src[:], src[:], ACT.Copy, scale=8.0)
+            store(piece, src[:])
+
+        def finish_gpsimd(piece, at):
+            dst = placed([P, HALF], F32, f"times8_{piece[0]}_{piece[1]}", at)
+            nc.gpsimd.tensor_scalar(dst[:], pieces[piece][0][:], 8.0, 0.0, ALU.mult, ALU.add)
+            store(piece, dst[:])
+
+        pair = as_passes(keep.tile([P, 2 * UNIT], F32, name="gelu_a01")[:])
+        ga = {0: pair[:, :, 0:P], 1: pair[:, :, P : 2 * P]}
+        for i in range(2, TILES):
+            ga[i] = as_passes(placed([P, UNIT], F32, f"gelu_a{i}", AT_GELU + 4 * KIB * (i - 2))[:])
         for i in range(2):
-            gelu_a(i, ga[i])
-        gelu_a(2, ga[2], psum.tile([P, 4, P], F32, name="first", offset=at_last_bank))
-        factors = psum.tile([P, P], F32, name="factors", offset=at_last_bank)
-        gelu_a(3, ga[3])
+            for b in range(PASSES):
+                gelu_a(i, b)
+        at_factors = BANKS * BANK_BYTES
+        hidden_bank(0, 2, 0, ga[2][:, 0], psum.tile([P, 4, P], F32, name="ahead_of_factors", offset=at_factors))
+        gelu_a(2, 1)
+        factors = psum.tile([P, P], F32, name="factors", offset=at_factors)
+        for b in range(PASSES):
+            gelu_a(3, b)
         nc.tensor.transpose(factors[:], factor_rows[:], ident[:])
         passing = next_bank()
         nc.tensor.transpose(passing[:, 0, :], factor_rows[:], ident[:])
         nc.scalar.copy(factors_sb[:], passing[:, 0, 0:16])
-        for i in range(4, 6):
-            gelu_a(i, ga[i])
+        for i in range(EARLY, AHEAD):
+            for b in range(PASSES):
+                gelu_a(i, b)
 
-        wb_plane = placed([P, R], U8, "wb_plane", AT_PICKED_A - KIB // 2)
+        wb_plane = placed([P, R], U8, "wb_plane", AT_WB_PLANE)
         for b in range(PASSES):
-            dst = wb_rounded[b][:].rearrange("p (t q k e j) -> p t q k j e", t=4, k=4, e=2, j=4)
-            src = wb_raw[:].rearrange("p j (q b t k e) -> p b t q k j e", b=PASSES, t=4, k=4, e=2)[:, b]
+            dst = wb_rounded[b][:].rearrange("p (t q u e j) -> p t q u j e", t=4, u=4, e=2, j=4)
+            src = wb_raw[:].rearrange("p j (q b t u e) -> p b t q u j e", b=PASSES, t=4, u=4, e=2)[:, b]
             for t in range(4):
                 nc.vector.tensor_copy(dst[:, t], src[:, t])
         for b in range(PASSES):
             cols = slice(HALF * b, HALF * (b + 1))
             quantize(wb_codes[:, cols], wb_plane[:, cols], wb_rounded[b][:])
 
-        gb_first = [entries(placed([P, UNIT * units], F32, f"gelu_b{n}", at_gelu_b(n))[:]) for n, units in ((0, 2), (2, 1), (3, 1))]
-        gelu_b(0, 4, 0, gb_first[0])
-        gelu_b(0, 2, 1, gb_first[1])
-        gelu_b(2, 2, 1, gb_first[2])
-        gb_late = [entries(placed([P, UNIT], F32, f"gelu_b{n}", at_gelu_b(n))[:]) for n in range(4, 8)]
-        for n in range(4):
-            gelu_b(4 + 2 * (n // 2), 2, n % 2, gb_late[n])
-        gelu_a(6, ga[6], passes=[0])
+        gb_half = [gelu_b(0, 0, 4, 0), gelu_b(2, 0, 2, 1), gelu_b(3, 2, 2, 1)]
+        gb_quarter = [[gelu_b(4 + 2 * n + b, 4 + 2 * n, 2, b) for b in range(PASSES)] for n in range(2)]
+        gelu_a(6, 0)
 
-        stage = [staged(f"stage_a{n}", AT_LANE[0] + (6 * n - 3) * KIB, 2) for n in range(2)]
-        scale_a(True, pair01[:, :, 0:SHARE_A01], as_passes(stage[0][:])[:, :, 0:SHARE_A01])
-        scale_a(False, ga[2], as_passes(stage[1][:])[:, :, 0:P])
-        scale_a(False, ga[3], as_passes(stage[1][:])[:, :, P:])
-        scale_a(False, pair01[:, :, SHARE_A01:], as_passes(stage[0][:])[:, :, SHARE_A01:])
+        stages = [staged(f"stage_a{n}", AT_STAGES_A[n], 2) for n in range(2)]
+        shared, own = as_passes(stages[0][:]), as_passes(stages[1][:])
+        scale_a(nc.gpsimd, factors_sb, pair[:, :, 0:SHARE_A], shared[:, :, 0:SHARE_A])
+        scale_a(nc.vector, factors, ga[2], own[:, :, 0:P])
+        scale_a(nc.vector, factors, ga[3], own[:, :, P:])
+        scale_a(nc.vector, factors, pair[:, :, SHARE_A:], shared[:, :, SHARE_A:])
         for n in (1, 0):
-            quantize_a(2 * n, 2, stage[n][:])
+            quantize_a(2 * n, 2, stages[n][:])
 
-        stage = [staged(f"stage_b{n}", AT_LANE[0] + (4 * n + 1) * KIB, 2) for n in range(2)]
-        scale_b(True, 0, gb_first[0][:, 0:SHARE_B0], entries(stage[0][:])[:, 0:SHARE_B0])
-        scale_b(False, 1, gb_first[1], entries(stage[1][:])[:, 0:QUARTER])
-        scale_b(False, 1, gb_first[2], entries(stage[1][:])[:, QUARTER:])
-        scale_b(False, 0, gb_first[0][:, SHARE_B0:], entries(stage[0][:])[:, SHARE_B0:])
-        for b in (1, 0):
-            quantize_b(b, 0, HALF, stage[b][:])
-        for i in range(4):
-            score(f"{i}0", [i], 0, HALF)
+        stages = [staged(f"stage_half{b}", AT_STAGES_HALF[b], 2) for b in range(PASSES)]
+        shared, own = as_entries(stages[0][:]), as_entries(stages[1][:])
+        scale_pass(nc.gpsimd, factors_sb, 1, 0, gb_half[0][:, 0:SHARE_HALF], shared[:, 0:SHARE_HALF])
+        scale_pass(nc.vector, factors, 1, 1, gb_half[1], own[:, 0:QUARTER])
+        scale_pass(nc.vector, factors, 1, 1, gb_half[2], own[:, QUARTER:])
+        scale_pass(nc.vector, factors, 1, 0, gb_half[0][:, SHARE_HALF:], shared[:, SHARE_HALF:])
+        quantize_b(0, HALF, stages)
+        for i in range(EARLY):
+            score(i, 0, HALF)
 
-        stage = [staged(f"stage_c{n}", AT_LANE[0] + (3 * n + 5) * KIB) for n in range(2)]
-        scale_b(True, 0, gb_late[0][:, 0:SHARE_C], entries(stage[0][:])[:, 0:SHARE_C])
-        scale_b(False, 1, gb_late[1], entries(stage[1][:]))
-        scale_b(False, 0, gb_late[0][:, SHARE_C:], entries(stage[0][:])[:, SHARE_C:])
-        for b in (1, 0):
-            quantize_b(b, HALF, QUARTER, stage[b][:])
-        score("0c", [0, 1], HALF, QUARTER, AT_TANH[0])
-        score("2c", [2, 3], HALF, QUARTER)
-        gelu_a(6, ga[6], passes=[1])
-        gelu_a(7, ga[7], passes=[0])
+        def scale_quarter(n):
+            share = SHARE_QUARTER[n]
+            quarter_stages = [staged(f"stage_quarter{n}{b}", AT_STAGES_QUARTER[n][b]) for b in range(PASSES)]
+            dst = [as_entries(stage[:]) for stage in quarter_stages]
+            scale_pass(nc.gpsimd, factors_sb, 1, 0, gb_quarter[n][0][:, 0:share], dst[0][:, 0:share])
+            scale_pass(nc.vector, factors, 1, 1, gb_quarter[n][1], dst[1])
+            scale_pass(nc.vector, factors, 1, 0, gb_quarter[n][0][:, share:], dst[0][:, share:])
+            return quarter_stages
 
-        stage = [staged(f"stage_d{n}", AT_LANE[0] + (5 * n + 14) * KIB // 2) for n in range(2)]
-        scale_b(True, 0, gb_late[2][:, 0:SHARE_D], entries(stage[0][:])[:, 0:SHARE_D])
-        scale_b(False, 1, gb_late[3], entries(stage[1][:]))
-        scale_b(False, 0, gb_late[2][:, SHARE_D:], entries(stage[0][:])[:, SHARE_D:])
-        finish_vector("00")
-        finish_vector("10")
-        for b in (1, 0):
-            quantize_b(b, HALF + QUARTER, QUARTER, stage[b][:])
-        score("0d", [0, 1], HALF + QUARTER, QUARTER, AT_TANH[1])
-        score("2d", [2, 3], HALF + QUARTER, QUARTER)
-        gelu_a(7, ga[7], passes=[1])
+        third, fourth = HALF, HALF + QUARTER
+        quantize_b(third, QUARTER, scale_quarter(0))
+        score(0, third, QUARTER, AT_RELEASE[5])
+        score(2, third, QUARTER)
+        gelu_a(6, 1)
+        gelu_a(LAST, 0)
 
-        def late_tile(i, at, on_gpsimd, plain, moved, at_tanh=None):
-            stage_i = staged(f"stage_late{i}", at + KIB)
-            share = 0
-            if on_gpsimd:
-                finish_gpsimd(on_gpsimd, at - KIB)
-            else:
-                share = SHARE_LATE
-                scale_a(True, ga[i][:, :, 0:share], as_passes(stage_i[:])[:, :, 0:share])
-            scale_a(False, ga[i][:, :, share:], as_passes(stage_i[:])[:, :, share:])
-            for name in plain:
-                finish_vector(name)
-            for name in moved:
-                finish_vector(name, moved=True)
-            quantize_a(i, 1, stage_i[:])
-            score(f"{i}0", [i], 0, HALF, at_tanh)
+        stages = scale_quarter(1)
+        finish_vector((0, 0))
+        finish_vector((1, 0))
+        quantize_b(fourth, QUARTER, stages)
+        score(0, fourth, QUARTER, AT_RELEASE[6])
+        score(2, fourth, QUARTER)
+        gelu_a(LAST, 1)
 
-        late_tile(4, AT_LANE[0] + 10 * KIB, "20", ["30"], ["0c"])
-        score("41", [4], HALF, HALF, AT_TANH[2])
-        late_tile(5, AT_TANH[0], "2c", [], ["0d"])
-        score("51", [5], HALF, HALF)
-        late_tile(6, AT_TANH[1], "2d", ["40"], ["41"])
-        score("61", [6], HALF, HALF)
+        def late_tile(i, for_gpsimd, for_vector):
+            stage = staged(f"stage_late{i}", AT_RELEASE[i] + KIB)
+            finish_gpsimd(for_gpsimd, AT_RELEASE[i] - KIB)
+            scale_a(nc.vector, factors, ga[i], as_passes(stage[:]))
+            for piece in for_vector:
+                finish_vector(piece, moved=piece == for_vector[-1])
+            quantize_a(i, 1, stage[:])
+            score(i, 0, HALF)
 
-        stage_7 = staged("stage_late7", AT_TANH[2] + 3 * KIB // 2)
-        finish_gpsimd("50", AT_TANH[2] - 3 * KIB // 2)
+        late_tile(4, (2, 0), [(3, 0), (0, third)])
+        score(4, HALF, HALF, AT_RELEASE[LAST])
+        finish_scalar((4, 0))
+        late_tile(5, (2, third), [(0, fourth)])
+        score(5, HALF, HALF)
+        late_tile(6, (2, fourth), [(4, HALF)])
+        score(6, HALF, HALF)
+
+        stage = staged("stage_last", AT_RELEASE[LAST] + KIB)
+        finish_gpsimd((5, 0), AT_RELEASE[LAST] - KIB)
         for b in range(PASSES):
-            cols = slice(HALF * b, HALF * (b + 1))
-            nc.vector.tensor_tensor(
-                entries(stage_7[:, cols]), ga[7][:, b], factors[:, 4 * b : 4 * b + 4].unsqueeze(1).to_broadcast([P, P, 4]), ALU.mult
-            )
-        banks = [psum.tile([P, HALF], F32, name=f"last{n}", offset=BANK_BYTES * (BANKS + 1 + n)) for n in range(3)]
+            scale_pass(nc.vector, factors, 0, b, ga[LAST][:, b], as_passes(stage[:])[:, b])
+        banks = [psum.tile([P, HALF], F32, name=f"last{n}", offset=at_factors + BANK_BYTES * (n + 1)) for n in range(3)]
         banks.append(next_bank()[:].rearrange("p t n -> p (t n)"))
-        for b in range(PASSES):
-            cols = slice(7 * UNIT_WORDS + P * b, 7 * UNIT_WORDS + P * (b + 1))
-            if b == 1:
-                finish_vector("51")
-            quantize(ha_codes[:, cols], ha_plane[:, cols], stage_7[:, HALF * b : HALF * (b + 1)])
+
+        def last_pass(b):
+            cols = slice(LAST * UNIT_WORDS + P * b, LAST * UNIT_WORDS + P * (b + 1))
+            quantize(ha_codes[:, cols], ha_plane[:, cols], stage[:, HALF * b : HALF * (b + 1)])
             for n in range(4):
-                cb = HALF * (PASSES * (n // 2) + b) + QUARTER * (n % 2)
-                nc.tensor.matmul_mx(
-                    banks[n][:, 0:QUARTER],
-                    lhsT=ha_codes[:, cols].bitcast(FP8X4),
-                    lhsT_scale=ha_plane[:, cols],
-                    rhs=hb_codes[:, cb : cb + QUARTER].bitcast(FP8X4),
-                    rhs_scale=hb_plane[:, cb : cb + QUARTER],
-                    start=(b == 0),
-                    stop=(b == PASSES - 1),
-                )
-        finish_vector("60")
-        finish_vector("61")
+                score_pass(banks[n][:, 0:QUARTER], ha_codes[:, cols], ha_plane[:, cols], b, QUARTER * n, QUARTER)
+
+        last_pass(0)
+        finish_vector((5, HALF))
+        last_pass(1)
+        finish_vector((6, 0))
+        finish_vector((6, HALF))
         for n in range(4):
-            tanh = keep.tile([P, QUARTER], F32, name=f"tanh_7{n}")
-            nc.scalar.activation(tanh[:], banks[n][:, 0:QUARTER], ACT.Tanh, scale=0.00390625)
-            piece[f"7{n}"] = (tanh, out[7 * P :, QUARTER * n : QUARTER * (n + 1)].rearrange("(s p) c -> p s c", p=P), 1)
-            finish_vector(f"7{n}")
+            tanh_piece(banks[n][:, 0:QUARTER], LAST, 1, QUARTER * n, QUARTER)
+            finish_vector((LAST, QUARTER * n))

@@ -25,29 +25,31 @@ UNIT = 1024
 UNIT_WORDS = UNIT // 4
 TILES = M // P
 ROW0 = P - 16
+FACTOR0 = P - 8
 BANKS = 4
 EARLY = 4
 AHEAD = 6
 LAST = TILES - 1
 SHARE_A = 156
 SHARE_HALF = 312
-SHARE_QUARTER = (144, 136)
+SHARE_THIRD = 144
+WB_FIRST = 768
+FIRST = 256
 BANK_BYTES = 2048
 KIB = 1024
 
 AT_WA_SCALES = 0
-AT_WORDS_A1 = 3 * KIB // 2
-AT_WA = 3 * KIB
-AT_WORDS_B = 4 * KIB
 AT_WB_ROUNDED = (12 * KIB, 26 * KIB)
 AT_STAGES_A = (9 * KIB, 15 * KIB)
 AT_STAGES_HALF = (13 * KIB, 17 * KIB)
-AT_STAGES_QUARTER = ((17 * KIB, 20 * KIB), (19 * KIB, 43 * KIB // 2))
+AT_STAGES_THIRD = (17 * KIB, 20 * KIB)
+AT_STAGES_FOURTH = (31 * KIB // 2, 19 * KIB)
+AT_PAIR_OUT = 43 * KIB // 2
 AT_GELU = 32 * KIB
 AT_PICKED_A = 96 * KIB
-AT_WB_RAW = AT_PICKED_A + KIB // 2
-AT_WB_PLANE = AT_PICKED_A - KIB // 2
-AT_RELEASE = {4: 22 * KIB, 5: 99 * KIB, 6: 105 * KIB, 7: 111 * KIB}
+AT_WB_RAW = (AT_PICKED_A + KIB // 2, AT_PICKED_A - 7 * KIB // 2)
+AT_RELEASE = {5: 99 * KIB, 6: 105 * KIB, 7: 111 * KIB}
+AT_LATE = {4: (35 * KIB // 2, 39 * KIB // 2), **{i: (at - KIB, at + KIB) for i, at in AT_RELEASE.items()}}
 
 
 def tile_list_biaff_gelu_cap_kernel(
@@ -66,7 +68,7 @@ def tile_list_biaff_gelu_cap_kernel(
         list_b = keep.tile([P, J // 16], U16, name="list_b")
         table = keep.tile([P, T], I32, name="table", align_bytes=64)
         table_sc = keep.tile([P, T // 4], I32, name="table_sc", align_bytes=64)
-        wa_raw = placed([P, R // 2], I32, "wa_raw", AT_WA)
+        wa_raw = keep.tile([P, R // 2], I32, name="wa_raw", align_bytes=64)
         wa_sc_raw = placed([P, R // 4], I32, "wa_sc_raw", AT_WA_SCALES)
         wa_codes = keep.tile([P, R // 2], I32, name="wa_codes", align_bytes=64)
         wb_rounded = [placed([P, 4 * HALF], BF16, f"wb_rounded{b}", AT_WB_ROUNDED[b]) for b in range(PASSES)]
@@ -83,9 +85,22 @@ def tile_list_biaff_gelu_cap_kernel(
         nc.sync.dma_start(list_a[:], offs)
         nc.sync.dma_start(wa_sc_raw[ROW0:P, :], wa_scales[0].bitcast(I32))
         nc.sync.dma_start(list_b[:], offs2)
+        factor_rows = keep.tile([P, PASSES, P], F32, name="factor_rows")
+        for side, vector in enumerate((sa, sb)):
+            row = FACTOR0 + 4 * side
+            nc.sync.dma_start(
+                factor_rows[row : row + 4].rearrange("t b (q i) -> t (b q) i", i=8),
+                vector.rearrange("(n t i) -> t n i", t=4, i=8),
+            )
         nc.sync.dma_start(table[:], tab_words[0].rearrange("p t i -> p (t i)").bitcast(I32))
         nc.sync.dma_start(wa_raw[:], wa_words[0].bitcast(I32))
         make_identity(nc, ident[:])
+        nc.scalar.activation(
+            factor_rows[0:FACTOR0],
+            ident[0:FACTOR0].unsqueeze(1).to_broadcast([FACTOR0, PASSES, P]),
+            ACT.Gelu_apprx_tanh,
+            scale=0.0,
+        )
 
         def carry_rows(plane, rows):
             for quad in range(4):
@@ -101,40 +116,34 @@ def tile_list_biaff_gelu_cap_kernel(
 
         picked_a = gather_scales(list_a[:], M, AT_PICKED_A, "picked_a")
         nc.vector.tensor_copy(
-            plane_a[:, M // 4 :].rearrange("p (c q i) -> p c q i", c=8, i=2),
-            wa_sc_raw[:].rearrange("p (q c i) -> p c q i", c=8, i=2),
+            plane_a[:, M // 4 :].rearrange("p (b t q i) -> p b t q i", b=PASSES, t=4, i=2),
+            wa_sc_raw[:].rearrange("p (b q t i) -> p b t q i", b=PASSES, t=4, i=2),
         )
         nc.vector.tensor_copy(plane_a[:, 0 : M // 4], picked_a)
         carry_rows(plane_a[:], plane_a[:])
-        wb_raw = placed([P, 4, R], F32, "wb_raw", AT_WB_RAW)
-        nc.sync.dma_start(wb_raw[:], wb.rearrange("(p j) c -> p j c", j=4))
-        factor_rows = placed([P, P], F32, "factor_rows", AT_PICKED_A)
-        nc.gpsimd.memset(factor_rows[:], 0.0)
-        for side, vector in enumerate((sa, sb)):
-            nc.sync.dma_start(
-                factor_rows[8 * side : 8 * side + 8, :].rearrange("c (q i) -> c q i", i=8),
-                vector.rearrange("(q c i) -> c q i", c=8, i=8),
-            )
+        wb_raw = [placed([P, 4, n], F32, f"wb_raw{n}", at) for n, at in zip((WB_FIRST, R - WB_FIRST), AT_WB_RAW)]
+        for raw, cols in zip(wb_raw, (slice(0, WB_FIRST), slice(WB_FIRST, R))):
+            nc.sync.dma_start(raw[:], wb[:, cols].rearrange("(p j) c -> p j c", j=4))
         carry_rows(plane_b[:], gather_scales(list_b[:], J, AT_WA_SCALES, "picked_b"))
 
         ha_codes = keep.tile([P, TILES * UNIT_WORDS], U32, name="ha_codes", align_bytes=64)
         hb_codes = keep.tile([P, TILES * UNIT_WORDS], U32, name="hb_codes", align_bytes=64)
-        factors_sb = keep.tile([P, 16], F32, name="factors_sb")
+        factors_sb = keep.tile([P, PASSES, 8], F32, name="factors_sb")
         ha_plane = keep.tile([P, TILES * UNIT_WORDS], U8, name="ha_plane", align_bytes=64)
         hb_plane = keep.tile([P, TILES * UNIT_WORDS], U8, name="hb_plane", align_bytes=64)
 
         words_a = [
-            keep.tile([P, HALF], U32, name="words_a0", align_bytes=64),
-            placed([P, HALF], U32, "words_a1", AT_WORDS_A1),
+            keep.tile([P, FIRST], U32, name="words_a0", align_bytes=64),
+            keep.tile([P, M - FIRST], U32, name="words_a1", align_bytes=64),
         ]
-        words_b = placed([P, J], U32, "words_b", AT_WORDS_B)
-        gather_words(words_a[0], list_a[:, 0:32])
+        words_b = keep.tile([P, J], U32, name="words_b", align_bytes=64)
+        gather_words(words_a[0], list_a[:, 0 : FIRST // 16])
         for b in range(PASSES):
-            nc.vector.tensor_copy(
-                wa_codes[:].rearrange("p (b t q i) -> p b t q i", b=PASSES, t=4, i=4)[:, b],
-                wa_raw[:].rearrange("p (q b t i) -> p b t q i", b=PASSES, t=4, i=4)[:, b],
+            nc.scalar.copy(
+                wa_codes[:].bitcast(U32).rearrange("p (b t q i) -> p b t q i", b=PASSES, t=4, i=4)[:, b],
+                wa_raw[:].bitcast(U32).rearrange("p (b q t i) -> p b t q i", b=PASSES, t=4, i=4)[:, b],
             )
-        gather_words(words_a[1], list_a[:, 32:64])
+        gather_words(words_a[1], list_a[:, FIRST // 16 :])
         gather_words(words_b, list_b[:])
 
         def quantize(codes, plane, src):
@@ -150,8 +159,8 @@ def tile_list_biaff_gelu_cap_kernel(
         def hidden_bank(side, tile, b, dst, bank):
             cols = slice(P * tile, P * (tile + 1))
             if side == 0:
-                half, entry0 = divmod(P * tile, HALF)
-                moving, moving_plane = words_a[half][:, entry0 : entry0 + P], plane_a[:].bitcast(U8)[:, cols]
+                part, entry0 = (0, P * tile) if P * tile < FIRST else (1, P * tile - FIRST)
+                moving, moving_plane = words_a[part][:, entry0 : entry0 + P], plane_a[:].bitcast(U8)[:, cols]
             else:
                 moving, moving_plane = words_b[:, cols], plane_b[:].bitcast(U8)[:, cols]
             for t in range(4):
@@ -189,12 +198,12 @@ def tile_list_biaff_gelu_cap_kernel(
             return dst
 
         def scale_a(engine, f, g, dst):
-            factor = f[:, 0:8].rearrange("p (b t) -> p b t", t=4).unsqueeze(2)
+            factor = f[:, :, 0:4].unsqueeze(2)
             engine.tensor_tensor(dst, g, factor.to_broadcast([P, PASSES, g.shape[2], 4]), ALU.mult)
 
         def scale_pass(engine, f, side, b, g, dst):
-            c0 = 8 * side + 4 * b
-            engine.tensor_tensor(dst, g, f[:, c0 : c0 + 4].unsqueeze(1).to_broadcast([P, g.shape[1], 4]), ALU.mult)
+            factor = f[:, b, 4 * side : 4 * side + 4].unsqueeze(1)
+            engine.tensor_tensor(dst, g, factor.to_broadcast([P, g.shape[1], 4]), ALU.mult)
 
         def staged(name, at, units=1):
             return placed([P, units * UNIT], BF16, name, at)
@@ -232,40 +241,49 @@ def tile_list_biaff_gelu_cap_kernel(
 
         pieces = {}
 
-        def tanh_piece(acc, i, tiles, col0, width, at=None):
+        def tanh_piece(acc, i, tiles, col0, width, at=None, values=None):
             shape, name = [P, tiles * width], f"tanh_{i}_{col0}"
-            values = keep.tile(shape, F32, name=name) if at is None else placed(shape, F32, name, at)
-            nc.scalar.activation(values[:], acc, ACT.Tanh, scale=0.00390625)
+            if values is None:
+                values = (keep.tile(shape, F32, name=name) if at is None else placed(shape, F32, name, at))[:]
+            nc.scalar.activation(values, acc, ACT.Tanh, scale=0.00390625)
             rows = out[P * i : P * (i + tiles), col0 : col0 + width].rearrange("(s p) c -> p s c", p=P)
             pieces[i, col0] = (values, rows, tiles)
 
-        def score(i, col0, width, at=None):
+        def score(i, col0, width, at=None, values=None):
             tiles = HALF // width
             acc = next_bank()[:].rearrange("p t n -> p (t n)")
             for s in range(tiles):
                 for b in range(PASSES):
                     codes, plane = ha[i + s]
                     score_pass(acc[:, width * s : width * (s + 1)], codes[:, b], plane[:, b], b, col0, width)
-            tanh_piece(acc, i, tiles, col0, width, at)
+            tanh_piece(acc, i, tiles, col0, width, at, values)
 
         def store(piece, src):
             nc.sync.dma_start(pieces[piece][1], src.rearrange("p (s c) -> p s c", s=pieces[piece][2]))
 
         def finish_vector(piece, moved=False):
             src = pieces[piece][0]
-            dst = keep.tile([P, HALF], F32, name=f"times8_{piece[0]}_{piece[1]}") if moved else src
-            nc.vector.tensor_scalar_mul(dst[:], src[:], 8.0)
-            store(piece, dst[:])
+            dst = keep.tile([P, HALF], F32, name=f"times8_{piece[0]}_{piece[1]}")[:] if moved else src
+            nc.vector.tensor_scalar_mul(dst, src, 8.0)
+            store(piece, dst)
 
         def finish_scalar(piece):
             src = pieces[piece][0]
-            nc.scalar.activation(src[:], src[:], ACT.Copy, scale=8.0)
-            store(piece, src[:])
+            nc.scalar.activation(src, src, ACT.Copy, scale=8.0)
+            store(piece, src)
 
         def finish_gpsimd(piece, at):
-            dst = placed([P, HALF], F32, f"times8_{piece[0]}_{piece[1]}", at)
-            nc.gpsimd.tensor_scalar(dst[:], pieces[piece][0][:], 8.0, 0.0, ALU.mult, ALU.add)
+            src = pieces[piece][0]
+            dst = placed(list(src.shape), F32, f"times8_{piece[0]}_{piece[1]}", at)
+            nc.gpsimd.tensor_scalar(dst[:], src, 8.0, 0.0, ALU.mult, ALU.add)
             store(piece, dst[:])
+
+        at_factors = BANKS * BANK_BYTES
+        turned = psum.tile([P, PASSES, P], F32, name="factors", offset=at_factors)
+        for b in range(PASSES):
+            nc.tensor.transpose(turned[:, b, :], factor_rows[:, b, :], ident[:])
+        factors = turned[:, :, FACTOR0:]
+        nc.scalar.copy(factors_sb[:], factors)
 
         pair = as_passes(keep.tile([P, 2 * UNIT], F32, name="gelu_a01")[:])
         ga = {0: pair[:, :, 0:P], 1: pair[:, :, P : 2 * P]}
@@ -274,24 +292,19 @@ def tile_list_biaff_gelu_cap_kernel(
         for i in range(2):
             for b in range(PASSES):
                 gelu_a(i, b)
-        at_factors = BANKS * BANK_BYTES
-        hidden_bank(0, 2, 0, ga[2][:, 0], psum.tile([P, 4, P], F32, name="ahead_of_factors", offset=at_factors))
-        gelu_a(2, 1)
-        factors = psum.tile([P, P], F32, name="factors", offset=at_factors)
-        for b in range(PASSES):
-            gelu_a(3, b)
-        nc.tensor.transpose(factors[:], factor_rows[:], ident[:])
-        passing = next_bank()
-        nc.tensor.transpose(passing[:, 0, :], factor_rows[:], ident[:])
-        nc.scalar.copy(factors_sb[:], passing[:, 0, 0:16])
-        for i in range(EARLY, AHEAD):
+        for i in range(2, AHEAD):
             for b in range(PASSES):
                 gelu_a(i, b)
 
-        wb_plane = placed([P, R], U8, "wb_plane", AT_WB_PLANE)
-        for b in range(PASSES):
-            dst = wb_rounded[b][:].rearrange("p (t q u e j) -> p t q u j e", t=4, u=4, e=2, j=4)
-            src = wb_raw[:].rearrange("p j (q b t u e) -> p b t q u j e", b=PASSES, t=4, u=4, e=2)[:, b]
+        wb_plane = keep.tile([P, R], U8, name="wb_plane", align_bytes=64)
+        parts = (
+            (0, slice(0, 16), wb_raw[0][:, :, 0:HALF]),
+            (1, slice(0, 8), wb_raw[0][:, :, HALF:]),
+            (1, slice(8, 16), wb_raw[1][:]),
+        )
+        for b, blocks, raw in parts:
+            dst = wb_rounded[b][:].rearrange("p (t q u e j) -> p t q u j e", t=4, u=4, e=2, j=4)[:, :, blocks]
+            src = raw.rearrange("p j (q t u e) -> p t q u j e", t=4, u=4, e=2)
             for t in range(4):
                 nc.vector.tensor_copy(dst[:, t], src[:, t])
         for b in range(PASSES):
@@ -304,7 +317,7 @@ def tile_list_biaff_gelu_cap_kernel(
 
         stages = [staged(f"stage_a{n}", AT_STAGES_A[n], 2) for n in range(2)]
         shared, own = as_passes(stages[0][:]), as_passes(stages[1][:])
-        scale_a(nc.gpsimd, factors_sb, pair[:, :, 0:SHARE_A], shared[:, :, 0:SHARE_A])
+        scale_a(nc.gpsimd, factors_sb[:], pair[:, :, 0:SHARE_A], shared[:, :, 0:SHARE_A])
         scale_a(nc.vector, factors, ga[2], own[:, :, 0:P])
         scale_a(nc.vector, factors, ga[3], own[:, :, P:])
         scale_a(nc.vector, factors, pair[:, :, SHARE_A:], shared[:, :, SHARE_A:])
@@ -313,57 +326,56 @@ def tile_list_biaff_gelu_cap_kernel(
 
         stages = [staged(f"stage_half{b}", AT_STAGES_HALF[b], 2) for b in range(PASSES)]
         shared, own = as_entries(stages[0][:]), as_entries(stages[1][:])
-        scale_pass(nc.gpsimd, factors_sb, 1, 0, gb_half[0][:, 0:SHARE_HALF], shared[:, 0:SHARE_HALF])
+        scale_pass(nc.gpsimd, factors_sb[:], 1, 0, gb_half[0][:, 0:SHARE_HALF], shared[:, 0:SHARE_HALF])
         scale_pass(nc.vector, factors, 1, 1, gb_half[1], own[:, 0:QUARTER])
         scale_pass(nc.vector, factors, 1, 1, gb_half[2], own[:, QUARTER:])
         scale_pass(nc.vector, factors, 1, 0, gb_half[0][:, SHARE_HALF:], shared[:, SHARE_HALF:])
         quantize_b(0, HALF, stages)
+        first_two = keep.tile([P, 2 * HALF], F32, name="tanh_first_two")
         for i in range(EARLY):
-            score(i, 0, HALF)
-
-        def scale_quarter(n):
-            share = SHARE_QUARTER[n]
-            quarter_stages = [staged(f"stage_quarter{n}{b}", AT_STAGES_QUARTER[n][b]) for b in range(PASSES)]
-            dst = [as_entries(stage[:]) for stage in quarter_stages]
-            scale_pass(nc.gpsimd, factors_sb, 1, 0, gb_quarter[n][0][:, 0:share], dst[0][:, 0:share])
-            scale_pass(nc.vector, factors, 1, 1, gb_quarter[n][1], dst[1])
-            scale_pass(nc.vector, factors, 1, 0, gb_quarter[n][0][:, share:], dst[0][:, share:])
-            return quarter_stages
+            score(i, 0, HALF, values=first_two[:, HALF * i : HALF * (i + 1)] if i < 2 else None)
+        pieces[0, 0] = (first_two[:], out[0 : 2 * P, 0:HALF].rearrange("(s p) c -> p s c", p=P), 2)
 
         third, fourth = HALF, HALF + QUARTER
-        quantize_b(third, QUARTER, scale_quarter(0))
+        stages = [staged(f"stage_third{b}", AT_STAGES_THIRD[b]) for b in range(PASSES)]
+        dst = [as_entries(stage[:]) for stage in stages]
+        scale_pass(nc.gpsimd, factors_sb[:], 1, 0, gb_quarter[0][0][:, 0:SHARE_THIRD], dst[0][:, 0:SHARE_THIRD])
+        scale_pass(nc.vector, factors, 1, 1, gb_quarter[0][1], dst[1])
+        scale_pass(nc.vector, factors, 1, 0, gb_quarter[0][0][:, SHARE_THIRD:], dst[0][:, SHARE_THIRD:])
+        quantize_b(third, QUARTER, stages)
         score(0, third, QUARTER, AT_RELEASE[5])
         score(2, third, QUARTER)
+        finish_scalar((3, 0))
         gelu_a(6, 1)
         gelu_a(LAST, 0)
 
-        stages = scale_quarter(1)
-        finish_vector((0, 0))
-        finish_vector((1, 0))
+        stages = [staged(f"stage_fourth{b}", AT_STAGES_FOURTH[b]) for b in range(PASSES)]
+        finish_gpsimd((0, 0), AT_PAIR_OUT)
+        for b in (1, 0):
+            scale_pass(nc.vector, factors, 1, b, gb_quarter[1][b], as_entries(stages[b][:]))
         quantize_b(fourth, QUARTER, stages)
         score(0, fourth, QUARTER, AT_RELEASE[6])
         score(2, fourth, QUARTER)
         gelu_a(LAST, 1)
 
-        def late_tile(i, for_gpsimd, for_vector):
-            stage = staged(f"stage_late{i}", AT_RELEASE[i] + KIB)
-            finish_gpsimd(for_gpsimd, AT_RELEASE[i] - KIB)
+        def late_tile(i, for_gpsimd, for_vector, at=None):
+            stage = staged(f"stage_late{i}", AT_LATE[i][1])
+            finish_gpsimd(for_gpsimd, AT_LATE[i][0])
             scale_a(nc.vector, factors, ga[i], as_passes(stage[:]))
-            for piece in for_vector:
-                finish_vector(piece, moved=piece == for_vector[-1])
+            finish_vector(for_vector, moved=True)
             quantize_a(i, 1, stage[:])
-            score(i, 0, HALF)
+            score(i, 0, HALF, at)
 
-        late_tile(4, (2, 0), [(3, 0), (0, third)])
-        score(4, HALF, HALF, AT_RELEASE[LAST])
-        finish_scalar((4, 0))
-        late_tile(5, (2, third), [(0, fourth)])
+        late_tile(4, (2, 0), (0, third), AT_RELEASE[LAST])
+        score(4, HALF, HALF)
+        late_tile(5, (2, third), (0, fourth))
+        finish_scalar((4, HALF))
         score(5, HALF, HALF)
-        late_tile(6, (2, fourth), [(4, HALF)])
+        late_tile(6, (2, fourth), (4, 0))
         score(6, HALF, HALF)
 
-        stage = staged("stage_last", AT_RELEASE[LAST] + KIB)
-        finish_gpsimd((5, 0), AT_RELEASE[LAST] - KIB)
+        stage = staged("stage_last", AT_LATE[LAST][1])
+        finish_gpsimd((5, 0), AT_LATE[LAST][0])
         for b in range(PASSES):
             scale_pass(nc.vector, factors, 0, b, ga[LAST][:, b], as_passes(stage[:])[:, b])
         banks = [psum.tile([P, HALF], F32, name=f"last{n}", offset=at_factors + BANK_BYTES * (n + 1)) for n in range(3)]

@@ -85,6 +85,8 @@ def tile_list_biaff_gelu_cap_kernel(
         nc.sync.dma_start(list_a[:], offs)
         nc.sync.dma_start(wa_sc_raw[ROW0:P, :], wa_scales[0].bitcast(I32))
         nc.sync.dma_start(list_b[:], offs2)
+        nc.sync.dma_start(table[:], tab_words[0].rearrange("p t i -> p (t i)").bitcast(I32))
+        nc.sync.dma_start(wa_raw[:], wa_words[0].bitcast(I32))
         factor_rows = keep.tile([P, PASSES, P], F32, name="factor_rows")
         for side, vector in enumerate((sa, sb)):
             row = FACTOR0 + 4 * side
@@ -92,8 +94,6 @@ def tile_list_biaff_gelu_cap_kernel(
                 factor_rows[row : row + 4].rearrange("t b (q i) -> t (b q) i", i=8),
                 vector.rearrange("(n t i) -> t n i", t=4, i=8),
             )
-        nc.sync.dma_start(table[:], tab_words[0].rearrange("p t i -> p (t i)").bitcast(I32))
-        nc.sync.dma_start(wa_raw[:], wa_words[0].bitcast(I32))
         make_identity(nc, ident[:])
         nc.scalar.activation(
             factor_rows[0:FACTOR0],
@@ -278,20 +278,20 @@ def tile_list_biaff_gelu_cap_kernel(
             nc.gpsimd.tensor_scalar(dst[:], src, 8.0, 0.0, ALU.mult, ALU.add)
             store(piece, dst[:])
 
+        pair = as_passes(keep.tile([P, 2 * UNIT], F32, name="gelu_a01")[:])
+        ga = {0: pair[:, :, 0:P], 1: pair[:, :, P : 2 * P]}
+        for i in range(2, TILES):
+            ga[i] = as_passes(placed([P, UNIT], F32, f"gelu_a{i}", AT_GELU + 4 * KIB * (i - 2))[:])
+        for b in range(PASSES):
+            gelu_a(0, b)
         at_factors = BANKS * BANK_BYTES
+        hidden_bank(0, 1, 0, ga[1][:, 0], psum.tile([P, 4, P], F32, name="ahead_of_factors", offset=at_factors))
+        gelu_a(1, 1)
         turned = psum.tile([P, PASSES, P], F32, name="factors", offset=at_factors)
         for b in range(PASSES):
             nc.tensor.transpose(turned[:, b, :], factor_rows[:, b, :], ident[:])
         factors = turned[:, :, FACTOR0:]
         nc.scalar.copy(factors_sb[:], factors)
-
-        pair = as_passes(keep.tile([P, 2 * UNIT], F32, name="gelu_a01")[:])
-        ga = {0: pair[:, :, 0:P], 1: pair[:, :, P : 2 * P]}
-        for i in range(2, TILES):
-            ga[i] = as_passes(placed([P, UNIT], F32, f"gelu_a{i}", AT_GELU + 4 * KIB * (i - 2))[:])
-        for i in range(2):
-            for b in range(PASSES):
-                gelu_a(i, b)
         for i in range(2, AHEAD):
             for b in range(PASSES):
                 gelu_a(i, b)

@@ -28,11 +28,14 @@ ROW0 = P - 16
 FACTOR0 = P - 8
 BANKS = 4
 EARLY = 4
-AHEAD = 6
+AHEAD = 5
 LAST = TILES - 1
 SHARE_A = 156
 SHARE_HALF = 312
 SHARE_THIRD = 144
+WIDE = 768
+SCALAR_BLOCKS = 4
+LAST_PIECES = ((0, 256), (256, 256), (512, 256), (768, 128), (896, 128))
 WB_FIRST = 768
 FIRST = 256
 BANK_BYTES = 2048
@@ -42,14 +45,14 @@ AT_WA_SCALES = 0
 AT_WB_ROUNDED = (12 * KIB, 26 * KIB)
 AT_STAGES_A = (9 * KIB, 15 * KIB)
 AT_STAGES_HALF = (13 * KIB, 17 * KIB)
-AT_STAGES_THIRD = (17 * KIB, 20 * KIB)
-AT_STAGES_FOURTH = (31 * KIB // 2, 19 * KIB)
-AT_PAIR_OUT = 43 * KIB // 2
+AT_STAGES_THIRD = (17 * KIB, 83 * KIB // 4)
+AT_STAGES_FOURTH = (61 * KIB // 4, 20 * KIB)
+AT_PAIR_OUT = 45 * KIB // 2
 AT_GELU = 32 * KIB
 AT_PICKED_A = 96 * KIB
 AT_WB_RAW = (AT_PICKED_A + KIB // 2, AT_PICKED_A - 7 * KIB // 2)
 AT_RELEASE = {5: 99 * KIB, 6: 105 * KIB, 7: 111 * KIB}
-AT_LATE = {4: (35 * KIB // 2, 39 * KIB // 2), **{i: (at - KIB, at + KIB) for i, at in AT_RELEASE.items()}}
+AT_LATE = {4: (69 * KIB // 4, 81 * KIB // 4), **{i: (at - 2 * KIB, at + KIB) for i, at in AT_RELEASE.items()}}
 
 
 def tile_list_biaff_gelu_cap_kernel(
@@ -274,9 +277,15 @@ def tile_list_biaff_gelu_cap_kernel(
 
         def finish_gpsimd(piece, at):
             src = pieces[piece][0]
-            dst = placed(list(src.shape), F32, f"times8_{piece[0]}_{piece[1]}", at)
+            dst = placed([P, max(src.shape[1], WIDE)], F32, f"times8_{piece[0]}_{piece[1]}", at)[:, 0 : src.shape[1]]
+            nc.gpsimd.tensor_scalar(dst, src, 8.0, 0.0, ALU.mult, ALU.add)
+            store(piece, dst)
+
+        def finish_wide(src, parts, at):
+            dst = placed([P, WIDE], F32, f"times8_wide{at}", at)
             nc.gpsimd.tensor_scalar(dst[:], src, 8.0, 0.0, ALU.mult, ALU.add)
-            store(piece, dst[:])
+            for rows, tiles, cols in parts:
+                nc.sync.dma_start(rows, dst[:, cols].rearrange("p (s c) -> p s c", s=tiles))
 
         pair = as_passes(keep.tile([P, 2 * UNIT], F32, name="gelu_a01")[:])
         ga = {0: pair[:, :, 0:P], 1: pair[:, :, P : 2 * P]}
@@ -292,14 +301,19 @@ def tile_list_biaff_gelu_cap_kernel(
             nc.tensor.transpose(turned[:, b, :], factor_rows[:, b, :], ident[:])
         factors = turned[:, :, FACTOR0:]
         nc.scalar.copy(factors_sb[:], factors)
+        nc.scalar.copy(
+            wb_rounded[1][:].rearrange("p (t q i j) -> p t q i j", t=4, i=8, j=4)[:, :, 0:SCALAR_BLOCKS],
+            wb_raw[0][:, :, HALF : HALF + 32 * SCALAR_BLOCKS].rearrange("p j (q t i) -> p t q i j", t=4, i=8),
+        )
         for i in range(2, AHEAD):
             for b in range(PASSES):
                 gelu_a(i, b)
 
+        gelu_a(5, 0)
         wb_plane = keep.tile([P, R], U8, name="wb_plane", align_bytes=64)
         parts = (
             (0, slice(0, 16), wb_raw[0][:, :, 0:HALF]),
-            (1, slice(0, 8), wb_raw[0][:, :, HALF:]),
+            (1, slice(SCALAR_BLOCKS, 8), wb_raw[0][:, :, HALF + 32 * SCALAR_BLOCKS :]),
             (1, slice(8, 16), wb_raw[1][:]),
         )
         for b, blocks, raw in parts:
@@ -313,7 +327,7 @@ def tile_list_biaff_gelu_cap_kernel(
 
         gb_half = [gelu_b(0, 0, 4, 0), gelu_b(2, 0, 2, 1), gelu_b(3, 2, 2, 1)]
         gb_quarter = [[gelu_b(4 + 2 * n + b, 4 + 2 * n, 2, b) for b in range(PASSES)] for n in range(2)]
-        gelu_a(6, 0)
+        gelu_a(5, 1)
 
         stages = [staged(f"stage_a{n}", AT_STAGES_A[n], 2) for n in range(2)]
         shared, own = as_passes(stages[0][:]), as_passes(stages[1][:])
@@ -332,8 +346,9 @@ def tile_list_biaff_gelu_cap_kernel(
         scale_pass(nc.vector, factors, 1, 0, gb_half[0][:, SHARE_HALF:], shared[:, SHARE_HALF:])
         quantize_b(0, HALF, stages)
         first_two = keep.tile([P, 2 * HALF], F32, name="tanh_first_two")
+        next_three = keep.tile([P, 2 * WIDE], F32, name="tanh_next_three")
         for i in range(EARLY):
-            score(i, 0, HALF, values=first_two[:, HALF * i : HALF * (i + 1)] if i < 2 else None)
+            score(i, 0, HALF, values=(first_two, next_three)[i // 2][:, HALF * (i % 2) : HALF * (i % 2 + 1)])
         pieces[0, 0] = (first_two[:], out[0 : 2 * P, 0:HALF].rearrange("(s p) c -> p s c", p=P), 2)
 
         third, fourth = HALF, HALF + QUARTER
@@ -344,8 +359,8 @@ def tile_list_biaff_gelu_cap_kernel(
         scale_pass(nc.vector, factors, 1, 0, gb_quarter[0][0][:, SHARE_THIRD:], dst[0][:, SHARE_THIRD:])
         quantize_b(third, QUARTER, stages)
         score(0, third, QUARTER, AT_RELEASE[5])
-        score(2, third, QUARTER)
-        finish_scalar((3, 0))
+        score(2, third, QUARTER, values=next_three[:, 2 * HALF :])
+        gelu_a(6, 0)
         gelu_a(6, 1)
         gelu_a(LAST, 0)
 
@@ -360,18 +375,23 @@ def tile_list_biaff_gelu_cap_kernel(
 
         def late_tile(i, for_gpsimd, for_vector, at=None):
             stage = staged(f"stage_late{i}", AT_LATE[i][1])
-            finish_gpsimd(for_gpsimd, AT_LATE[i][0])
+            for_gpsimd(AT_LATE[i][0])
             scale_a(nc.vector, factors, ga[i], as_passes(stage[:]))
             finish_vector(for_vector, moved=True)
             quantize_a(i, 1, stage[:])
             score(i, 0, HALF, at)
 
-        late_tile(4, (2, 0), (0, third), AT_RELEASE[LAST])
+        rows3 = pieces[3, 0][1]
+        wide = [
+            [(pieces[2, 0][1], 1, slice(0, HALF)), (rows3[:, :, 0:QUARTER], 1, slice(HALF, WIDE))],
+            [(rows3[:, :, QUARTER:], 1, slice(0, QUARTER)), (pieces[2, third][1], 2, slice(QUARTER, WIDE))],
+        ]
+        late_tile(4, lambda at: finish_wide(next_three[:, 0:WIDE], wide[0], at), (0, third), AT_RELEASE[LAST])
         score(4, HALF, HALF)
-        late_tile(5, (2, third), (0, fourth))
+        late_tile(5, lambda at: finish_wide(next_three[:, WIDE:], wide[1], at), (0, fourth))
         finish_scalar((4, HALF))
         score(5, HALF, HALF)
-        late_tile(6, (2, fourth), (4, 0))
+        late_tile(6, lambda at: finish_gpsimd((2, fourth), at), (4, 0))
         score(6, HALF, HALF)
 
         stage = staged("stage_last", AT_LATE[LAST][1])
@@ -392,6 +412,7 @@ def tile_list_biaff_gelu_cap_kernel(
         last_pass(1)
         finish_vector((6, 0))
         finish_vector((6, HALF))
-        for n in range(4):
-            tanh_piece(banks[n][:, 0:QUARTER], LAST, 1, QUARTER * n, QUARTER)
-            finish_vector((LAST, QUARTER * n))
+        for col0, width in LAST_PIECES:
+            n, at = divmod(col0, QUARTER)
+            tanh_piece(banks[n][:, at : at + width], LAST, 1, col0, width)
+            finish_vector((LAST, col0))

from contextlib import ExitStack

import concourse.mybir as mybir
from concourse.masks import make_identity

K, R, T, M, J = 512, 1024, 4096, 1024, 1024
FLOPS = 2 * K * R * M + 2 * K * R * J + 2 * R * M * J

F32 = mybir.dt.float32
BF16 = mybir.dt.bfloat16
I32 = mybir.dt.int32
U32 = mybir.dt.uint32
U16 = mybir.dt.uint16
U8 = mybir.dt.uint8
FP8X4 = mybir.dt.float8_e4m3fn_x4
FP4X4 = mybir.dt.float4_e2m1fn_x4
ACT = mybir.ActivationFunctionType
ALU = mybir.AluOpType

P = 128
PASSES = 2
HALF = 512
QUARTER = 256
UNIT = 1024
UNIT_WORDS = UNIT // 4
TILES = M // P
ROW0 = P - 16
FACTOR0 = P - 8
BANKS = 4
EARLY = 4
AHEAD = 5
LAST = TILES - 1
SHARE_A = 156
SHARE_HALF = 312
SHARE_THIRD = 144
WIDE = 768
SCALAR_BLOCKS = 4
LAST_PIECES = ((0, 256), (256, 256), (512, 256), (768, 128), (896, 128))
WB_FIRST = 768
FIRST = 256
BANK_BYTES = 2048
KIB = 1024

AT_WA_SCALES = 0
AT_WB_ROUNDED = (12 * KIB, 26 * KIB)
AT_STAGES_A = (9 * KIB, 15 * KIB)
AT_STAGES_HALF = (13 * KIB, 17 * KIB)
AT_STAGES_THIRD = (17 * KIB, 83 * KIB // 4)
AT_STAGES_FOURTH = (61 * KIB // 4, 20 * KIB)
AT_PAIR_OUT = 45 * KIB // 2
AT_GELU = 32 * KIB
AT_PICKED_A = 96 * KIB
AT_WB_RAW = (AT_PICKED_A + KIB // 2, AT_PICKED_A - 7 * KIB // 2)
AT_RELEASE = {5: 99 * KIB, 6: 105 * KIB, 7: 111 * KIB}
AT_LATE = {4: (69 * KIB // 4, 81 * KIB // 4), **{i: (at - 2 * KIB, at + KIB) for i, at in AT_RELEASE.items()}}


def tile_list_biaff_gelu_cap_kernel(
    tc, tab_words, tab_scales, wa_words, wa_scales, wb, sa, sb, offs, offs2, out
):
    nc = tc.nc
    with ExitStack() as ctx:
        keep = ctx.enter_context(tc.tile_pool(name="keep", bufs=1))
        reuse = ctx.enter_context(tc.tile_pool(name="reuse", bufs=1))
        psum = ctx.enter_context(tc.psum_pool(name="psum", bufs=1))

        def placed(shape, dtype, name, at):
            return reuse.tile(shape, dtype, name=name, align_bytes=64, offset=at)

        list_a = keep.tile([P, M // 16], U16, name="list_a")
        list_b = keep.tile([P, J // 16], U16, name="list_b")
        table = keep.tile([P, T], I32, name="table", align_bytes=64)
        table_sc = keep.tile([P, T // 4], I32, name="table_sc", align_bytes=64)
        wa_raw = keep.tile([P, R // 2], I32, name="wa_raw", align_bytes=64)
        wa_sc_raw = placed([P, R // 4], I32, "wa_sc_raw", AT_WA_SCALES)
        wa_codes = keep.tile([P, R // 2], I32, name="wa_codes", align_bytes=64)
        wb_rounded = [placed([P, 4 * HALF], BF16, f"wb_rounded{b}", AT_WB_ROUNDED[b]) for b in range(PASSES)]
        wb_codes = keep.tile([P, R], U32, name="wb_codes", align_bytes=64)
        ident = keep.tile([P, P], F32, name="ident")
        plane_a = keep.tile([P, (M + R) // 4], I32, name="plane_a", align_bytes=64)
        plane_b = keep.tile([P, J // 4], I32, name="plane_b", align_bytes=64)

        nc.vector.memset(table_sc[0:ROW0, :], 0)
        nc.vector.memset(wa_sc_raw[0:ROW0, :], 0)
        nc.gpsimd.memset(plane_b[:], 0)

        nc.sync.dma_start(table_sc[ROW0:P, :], tab_scales[0].bitcast(I32))
        nc.sync.dma_start(list_a[:], offs)
        nc.sync.dma_start(wa_sc_raw[ROW0:P, :], wa_scales[0].bitcast(I32))
        nc.sync.dma_start(list_b[:], offs2)
        nc.sync.dma_start(table[:], tab_words[0].rearrange("p t i -> p (t i)").bitcast(I32))
        nc.sync.dma_start(wa_raw[:], wa_words[0].bitcast(I32))
        factor_rows = keep.tile([P, PASSES, P], F32, name="factor_rows")
        for side, vector in enumerate((sa, sb)):
            row = FACTOR0 + 4 * side
            nc.sync.dma_start(
                factor_rows[row : row + 4].rearrange("t b (q i) -> t (b q) i", i=8),
                vector.rearrange("(n t i) -> t n i", t=4, i=8),
            )
        make_identity(nc, ident[:])
        nc.scalar.activation(
            factor_rows[0:FACTOR0],
            ident[0:FACTOR0].unsqueeze(1).to_broadcast([FACTOR0, PASSES, P]),
            ACT.Gelu_apprx_tanh,
            scale=0.0,
        )

        def carry_rows(plane, rows):
            for quad in range(4):
                nc.sync.dma_start(plane[32 * quad : 32 * quad + 4, :], rows[ROW0 + 4 * quad : ROW0 + 4 * quad + 4, :])

        def gather_scales(offsets, count, at, name):
            picked = placed([P, count], U8, name, at)
            nc.vector.tensor_copy(picked[:], table_sc[:].bitcast(U8).indirect(offsets))
            return picked[:].bitcast(I32)

        def gather_words(words, offsets):
            nc.vector.tensor_copy(words[:], table[:].bitcast(U32).indirect(offsets))

        picked_a = gather_scales(list_a[:], M, AT_PICKED_A, "picked_a")
        nc.vector.tensor_copy(
            plane_a[:, M // 4 :].rearrange("p (b t q i) -> p b t q i", b=PASSES, t=4, i=2),
            wa_sc_raw[:].rearrange("p (b q t i) -> p b t q i", b=PASSES, t=4, i=2),
        )
        nc.vector.tensor_copy(plane_a[:, 0 : M // 4], picked_a)
        carry_rows(plane_a[:], plane_a[:])
        wb_raw = [placed([P, 4, n], F32, f"wb_raw{n}", at) for n, at in zip((WB_FIRST, R - WB_FIRST), AT_WB_RAW)]
        for raw, cols in zip(wb_raw, (slice(0, WB_FIRST), slice(WB_FIRST, R))):
            nc.sync.dma_start(raw[:], wb[:, cols].rearrange("(p j) c -> p j c", j=4))
        carry_rows(plane_b[:], gather_scales(list_b[:], J, AT_WA_SCALES, "picked_b"))

        ha_codes = keep.tile([P, TILES * UNIT_WORDS], U32, name="ha_codes", align_bytes=64)
        hb_codes = keep.tile([P, TILES * UNIT_WORDS], U32, name="hb_codes", align_bytes=64)
        factors_sb = keep.tile([P, PASSES, 8], F32, name="factors_sb")
        ha_plane = keep.tile([P, TILES * UNIT_WORDS], U8, name="ha_plane", align_bytes=64)
        hb_plane = keep.tile([P, TILES * UNIT_WORDS], U8, name="hb_plane", align_bytes=64)

        words_a = [
            keep.tile([P, FIRST], U32, name="words_a0", align_bytes=64),
            keep.tile([P, M - FIRST], U32, name="words_a1", align_bytes=64),
        ]
        words_b = keep.tile([P, J], U32, name="words_b", align_bytes=64)
        gather_words(words_a[0], list_a[:, 0 : FIRST // 16])
        for b in range(PASSES):
            nc.scalar.copy(
                wa_codes[:].bitcast(U32).rearrange("p (b t q i) -> p b t q i", b=PASSES, t=4, i=4)[:, b],
                wa_raw[:].bitcast(U32).rearrange("p (b q t i) -> p b t q i", b=PASSES, t=4, i=4)[:, b],
            )
        gather_words(words_a[1], list_a[:, FIRST // 16 :])
        gather_words(words_b, list_b[:])

        def quantize(codes, plane, src):
            nc.vector.quantize_mx(codes.bitcast(FP8X4), plane, src)

        turns = []

        def next_bank():
            turn = len(turns)
            turns.append(psum.tile([P, 4, P], F32, name=f"bank{turn}", offset=BANK_BYTES * (turn % BANKS)))
            return turns[turn]

        def hidden_bank(side, tile, b, dst, bank):
            cols = slice(P * tile, P * (tile + 1))
            if side == 0:
                part, entry0 = (0, P * tile) if P * tile < FIRST else (1, P * tile - FIRST)
                moving, moving_plane = words_a[part][:, entry0 : entry0 + P], plane_a[:].bitcast(U8)[:, cols]
            else:
                moving, moving_plane = words_b[:, cols], plane_b[:].bitcast(U8)[:, cols]
            for t in range(4):
                c0 = P * (4 * b + t)
                if side == 0:
                    weight = wa_codes[:].bitcast(U8)[:, 2 * c0 : 2 * (c0 + P)].bitcast(FP4X4)
                    weight_plane = plane_a[:].bitcast(U8)[:, M + c0 : M + c0 + P]
                else:
                    weight, weight_plane = wb_codes[:, c0 : c0 + P].bitcast(FP8X4), wb_plane[:, c0 : c0 + P]
                nc.tensor.matmul_mx(
                    bank[:, t, :],
                    lhsT=weight,
                    lhsT_scale=weight_plane,
                    rhs=moving.bitcast(FP8X4),
                    rhs_scale=moving_plane,
                    start=True,
                    stop=True,
                )
            nc.scalar.activation(dst, bank[:].rearrange("p t n -> p n t"), ACT.Gelu_apprx_tanh)

        def as_passes(ap):
            return ap.rearrange("p (b n t) -> p b n t", b=PASSES, t=4)

        def as_entries(ap):
            return ap.rearrange("p (n t) -> p n t", t=4)

        def gelu_a(i, b):
            hidden_bank(0, i, b, ga[i][:, b], next_bank())

        def gelu_b(unit0, tile0, tiles, b):
            at = AT_GELU + 4 * KIB * (TILES - 2 + unit0)
            dst = as_entries(placed([P, 4 * P * tiles], F32, f"gelu_b{unit0}", at)[:])
            for s in range(tiles):
                hidden_bank(1, tile0 + s, b, dst[:, P * s : P * (s + 1)], next_bank())
            return dst

        def scale_a(engine, f, g, dst):
            factor = f[:, :, 0:4].unsqueeze(2)
            engine.tensor_tensor(dst, g, factor.to_broadcast([P, PASSES, g.shape[2], 4]), ALU.mult)

        def scale_pass(engine, f, side, b, g, dst):
            factor = f[:, b, 4 * side : 4 * side + 4].unsqueeze(1)
            engine.tensor_tensor(dst, g, factor.to_broadcast([P, g.shape[1], 4]), ALU.mult)

        def staged(name, at, units=1):
            return placed([P, units * UNIT], BF16, name, at)

        ha = {}

        def quantize_a(i, tiles, src):
            cols = slice(UNIT_WORDS * i, UNIT_WORDS * (i + tiles))
            codes, plane = ha_codes[:, cols], ha_plane[:, cols]
            quantize(codes, plane, src)
            for n in range(tiles):
                ha[i + n] = [x.rearrange("p (b s c) -> p b s c", b=PASSES, s=tiles)[:, :, n, :] for x in (codes, plane)]

        def hb_cols(b, col0, width):
            half, entry0 = divmod(col0, HALF)
            start = HALF * (PASSES * half + b) + entry0
            return slice(start, start + width)

        def quantize_b(col0, width, stages):
            for b in (1, 0):
                cols = hb_cols(b, col0, width)
                quantize(hb_codes[:, cols], hb_plane[:, cols], stages[b][:])

        def score_pass(acc, codes, plane, b, col0, width):
            cols = hb_cols(b, col0, width)
            nc.tensor.matmul_mx(
                acc,
                lhsT=codes.bitcast(FP8X4),
                lhsT_scale=plane,
                rhs=hb_codes[:, cols].bitcast(FP8X4),
                rhs_scale=hb_plane[:, cols],
                start=(b == 0),
                stop=(b == PASSES - 1),
            )

        pieces = {}

        def tanh_piece(acc, i, tiles, col0, width, at=None, values=None):
            shape, name = [P, tiles * width], f"tanh_{i}_{col0}"
            if values is None:
                values = (keep.tile(shape, F32, name=name) if at is None else placed(shape, F32, name, at))[:]
            nc.scalar.activation(values, acc, ACT.Tanh, scale=0.00390625)
            rows = out[P * i : P * (i + tiles), col0 : col0 + width].rearrange("(s p) c -> p s c", p=P)
            pieces[i, col0] = (values, rows, tiles)

        def score(i, col0, width, at=None, values=None):
            tiles = HALF // width
            acc = next_bank()[:].rearrange("p t n -> p (t n)")
            for s in range(tiles):
                for b in range(PASSES):
                    codes, plane = ha[i + s]
                    score_pass(acc[:, width * s : width * (s + 1)], codes[:, b], plane[:, b], b, col0, width)
            tanh_piece(acc, i, tiles, col0, width, at, values)

        def store(piece, src):
            nc.sync.dma_start(pieces[piece][1], src.rearrange("p (s c) -> p s c", s=pieces[piece][2]))

        def finish_vector(piece, moved=False):
            src = pieces[piece][0]
            dst = keep.tile([P, HALF], F32, name=f"times8_{piece[0]}_{piece[1]}")[:] if moved else src
            nc.vector.tensor_scalar_mul(dst, src, 8.0)
            store(piece, dst)

        def finish_scalar(piece):
            src = pieces[piece][0]
            nc.scalar.activation(src, src, ACT.Copy, scale=8.0)
            store(piece, src)

        def finish_gpsimd(piece, at):
            src = pieces[piece][0]
            dst = placed([P, max(src.shape[1], WIDE)], F32, f"times8_{piece[0]}_{piece[1]}", at)[:, 0 : src.shape[1]]
            nc.gpsimd.tensor_scalar(dst, src, 8.0, 0.0, ALU.mult, ALU.add)
            store(piece, dst)

        def finish_wide(src, parts, at):
            dst = placed([P, WIDE], F32, f"times8_wide{at}", at)
            nc.gpsimd.tensor_scalar(dst[:], src, 8.0, 0.0, ALU.mult, ALU.add)
            for rows, tiles, cols in parts:
                nc.sync.dma_start(rows, dst[:, cols].rearrange("p (s c) -> p s c", s=tiles))

        pair = as_passes(keep.tile([P, 2 * UNIT], F32, name="gelu_a01")[:])
        ga = {0: pair[:, :, 0:P], 1: pair[:, :, P : 2 * P]}
        for i in range(2, TILES):
            ga[i] = as_passes(placed([P, UNIT], F32, f"gelu_a{i}", AT_GELU + 4 * KIB * (i - 2))[:])
        for b in range(PASSES):
            gelu_a(0, b)
        at_factors = BANKS * BANK_BYTES
        hidden_bank(0, 1, 0, ga[1][:, 0], psum.tile([P, 4, P], F32, name="ahead_of_factors", offset=at_factors))
        gelu_a(1, 1)
        turned = psum.tile([P, PASSES, P], F32, name="factors", offset=at_factors)
        for b in range(PASSES):
            nc.tensor.transpose(turned[:, b, :], factor_rows[:, b, :], ident[:])
        factors = turned[:, :, FACTOR0:]
        nc.scalar.copy(factors_sb[:], factors)
        nc.scalar.copy(
            wb_rounded[1][:].rearrange("p (t q i j) -> p t q i j", t=4, i=8, j=4)[:, :, 0:SCALAR_BLOCKS],
            wb_raw[0][:, :, HALF : HALF + 32 * SCALAR_BLOCKS].rearrange("p j (q t i) -> p t q i j", t=4, i=8),
        )
        for i in range(2, AHEAD):
            for b in range(PASSES):
                gelu_a(i, b)

        gelu_a(5, 0)
        wb_plane = keep.tile([P, R], U8, name="wb_plane", align_bytes=64)
        parts = (
            (0, slice(0, 16), wb_raw[0][:, :, 0:HALF]),
            (1, slice(SCALAR_BLOCKS, 8), wb_raw[0][:, :, HALF + 32 * SCALAR_BLOCKS :]),
            (1, slice(8, 16), wb_raw[1][:]),
        )
        for b, blocks, raw in parts:
            dst = wb_rounded[b][:].rearrange("p (t q u e j) -> p t q u j e", t=4, u=4, e=2, j=4)[:, :, blocks]
            src = raw.rearrange("p j (q t u e) -> p t q u j e", t=4, u=4, e=2)
            for t in range(4):
                nc.vector.tensor_copy(dst[:, t], src[:, t])
        for b in range(PASSES):
            cols = slice(HALF * b, HALF * (b + 1))
            quantize(wb_codes[:, cols], wb_plane[:, cols], wb_rounded[b][:])

        gb_half = [gelu_b(0, 0, 4, 0), gelu_b(2, 0, 2, 1), gelu_b(3, 2, 2, 1)]
        gb_quarter = [[gelu_b(4 + 2 * n + b, 4 + 2 * n, 2, b) for b in range(PASSES)] for n in range(2)]
        gelu_a(5, 1)

        stages = [staged(f"stage_a{n}", AT_STAGES_A[n], 2) for n in range(2)]
        shared, own = as_passes(stages[0][:]), as_passes(stages[1][:])
        scale_a(nc.gpsimd, factors_sb[:], pair[:, :, 0:SHARE_A], shared[:, :, 0:SHARE_A])
        scale_a(nc.vector, factors, ga[2], own[:, :, 0:P])
        scale_a(nc.vector, factors, ga[3], own[:, :, P:])
        scale_a(nc.vector, factors, pair[:, :, SHARE_A:], shared[:, :, SHARE_A:])
        for n in (1, 0):
            quantize_a(2 * n, 2, stages[n][:])

        stages = [staged(f"stage_half{b}", AT_STAGES_HALF[b], 2) for b in range(PASSES)]
        shared, own = as_entries(stages[0][:]), as_entries(stages[1][:])
        scale_pass(nc.gpsimd, factors_sb[:], 1, 0, gb_half[0][:, 0:SHARE_HALF], shared[:, 0:SHARE_HALF])
        scale_pass(nc.vector, factors, 1, 1, gb_half[1], own[:, 0:QUARTER])
        scale_pass(nc.vector, factors, 1, 1, gb_half[2], own[:, QUARTER:])
        scale_pass(nc.vector, factors, 1, 0, gb_half[0][:, SHARE_HALF:], shared[:, SHARE_HALF:])
        quantize_b(0, HALF, stages)
        first_two = keep.tile([P, 2 * HALF], F32, name="tanh_first_two")
        next_three = keep.tile([P, 2 * WIDE], F32, name="tanh_next_three")
        for i in range(EARLY):
            score(i, 0, HALF, values=(first_two, next_three)[i // 2][:, HALF * (i % 2) : HALF * (i % 2 + 1)])
        pieces[0, 0] = (first_two[:], out[0 : 2 * P, 0:HALF].rearrange("(s p) c -> p s c", p=P), 2)

        third, fourth = HALF, HALF + QUARTER
        stages = [staged(f"stage_third{b}", AT_STAGES_THIRD[b]) for b in range(PASSES)]
        dst = [as_entries(stage[:]) for stage in stages]
        scale_pass(nc.gpsimd, factors_sb[:], 1, 0, gb_quarter[0][0][:, 0:SHARE_THIRD], dst[0][:, 0:SHARE_THIRD])
        scale_pass(nc.vector, factors, 1, 1, gb_quarter[0][1], dst[1])
        scale_pass(nc.vector, factors, 1, 0, gb_quarter[0][0][:, SHARE_THIRD:], dst[0][:, SHARE_THIRD:])
        quantize_b(third, QUARTER, stages)
        score(0, third, QUARTER, AT_RELEASE[5])
        score(2, third, QUARTER, values=next_three[:, 2 * HALF :])
        gelu_a(6, 0)
        gelu_a(6, 1)
        gelu_a(LAST, 0)

        stages = [staged(f"stage_fourth{b}", AT_STAGES_FOURTH[b]) for b in range(PASSES)]
        finish_gpsimd((0, 0), AT_PAIR_OUT)
        for b in (1, 0):
            scale_pass(nc.vector, factors, 1, b, gb_quarter[1][b], as_entries(stages[b][:]))
        quantize_b(fourth, QUARTER, stages)
        score(0, fourth, QUARTER, AT_RELEASE[6])
        score(2, fourth, QUARTER)
        gelu_a(LAST, 1)

        def late_tile(i, for_gpsimd, for_vector, at=None):
            stage = staged(f"stage_late{i}", AT_LATE[i][1])
            for_gpsimd(AT_LATE[i][0])
            scale_a(nc.vector, factors, ga[i], as_passes(stage[:]))
            finish_vector(for_vector, moved=True)
            quantize_a(i, 1, stage[:])
            score(i, 0, HALF, at)

        rows3 = pieces[3, 0][1]
        wide = [
            [(pieces[2, 0][1], 1, slice(0, HALF)), (rows3[:, :, 0:QUARTER], 1, slice(HALF, WIDE))],
            [(rows3[:, :, QUARTER:], 1, slice(0, QUARTER)), (pieces[2, third][1], 2, slice(QUARTER, WIDE))],
        ]
        late_tile(4, lambda at: finish_wide(next_three[:, 0:WIDE], wide[0], at), (0, third), AT_RELEASE[LAST])
        score(4, HALF, HALF)
        late_tile(5, lambda at: finish_wide(next_three[:, WIDE:], wide[1], at), (0, fourth))
        finish_scalar((4, HALF))
        score(5, HALF, HALF)
        late_tile(6, lambda at: finish_gpsimd((2, fourth), at), (4, 0))
        score(6, HALF, HALF)

        stage = staged("stage_last", AT_LATE[LAST][1])
        finish_gpsimd((5, 0), AT_LATE[LAST][0])
        for b in range(PASSES):
            scale_pass(nc.vector, factors, 0, b, ga[LAST][:, b], as_passes(stage[:])[:, b])
        banks = [psum.tile([P, HALF], F32, name=f"last{n}", offset=at_factors + BANK_BYTES * (n + 1)) for n in range(3)]
        banks.append(next_bank()[:].rearrange("p t n -> p (t n)"))

        def last_pass(b):
            cols = slice(LAST * UNIT_WORDS + P * b, LAST * UNIT_WORDS + P * (b + 1))
            quantize(ha_codes[:, cols], ha_plane[:, cols], stage[:, HALF * b : HALF * (b + 1)])
            for n in range(4):
                score_pass(banks[n][:, 0:QUARTER], ha_codes[:, cols], ha_plane[:, cols], b, QUARTER * n, QUARTER)

        last_pass(0)
        finish_vector((5, HALF))
        last_pass(1)
        finish_vector((6, 0))
        finish_vector((6, HALF))
        for col0, width in LAST_PIECES:
            n, at = divmod(col0, QUARTER)
            tanh_piece(banks[n][:, at : at + width], LAST, 1, col0, width)
            finish_vector((LAST, col0))
